import numpy as np, ml_dtypes
CORES = [113,118,241,246]
N = 4
BF = ml_dtypes.bfloat16
def gentries(a):
    return np.ascontiguousarray(a.reshape(8, 16, -1).transpose(0, 2, 1)).reshape(8, -1)
def gtable(e):
    e = np.asarray(e); return np.ascontiguousarray(e.reshape(8, -1, 16).transpose(0, 2, 1)).reshape(128, -1).astype(np.int32)
S, B, T, RO = 1952, 16, 256, 3
H, TH, NC = S + 2 * RO * B, T // 2, (S + 2 * RO * B) // 16
G8 = np.arange(8)
def parts(rng, noise, skew):
    lab = np.argsort(rng.random((8, H)), axis=1).reshape(8, NC, 16); cl = np.zeros((8, H), np.int64)
    for g in range(8): cl[g, lab[g].reshape(-1)] = np.arange(H) // 16
    o = rng.integers(0, 16, (N, 8, 15, H))
    if skew: o = (o * rng.integers(0, 17, o.shape)) >> 4
    nm = lab[G8[None, :, None, None], ((cl + 1) % NC)[None, :, None, :], o]
    if noise > 0: nm = np.where(rng.random(nm.shape) < noise, rng.integers(0, H, nm.shape), nm)
    c = (rng.integers(0, NC, (1, 8, 1)) + np.arange(N)[:, None, None] * T + np.arange(T)[None, None, :]) % NC
    loose = lab[G8[None, :, None], c, rng.integers(0, 16, (N, 8, T))]; st = loose.copy()
    fol = rng.random((N, 8, T)) < 0.6; k = rng.integers(0, 15, (N, 8, T)); qn = np.arange(N)[:, None]
    for t in range(1, T): st[:, :, t] = np.where(fol[:, :, t], nm[qn, G8[None, :], k[:, :, t], st[:, :, t - 1]], loose[:, :, t])
    if noise > 0: st = np.where(rng.random(st.shape) < noise, rng.integers(0, H, st.shape), st)
    d = {"nm": nm, "wt": rng.integers(1, 256, (N, 8, 15, H)), "st": st}
    top = np.array([12, 60, 140, 255])[rng.integers(0, 4, (N, 8, 1))]
    d["w15"] = 1 + (top * rng.random((N, 8, H))).astype(np.int64)
    d["em"] = rng.integers(0, 16, (N, 8, 16, H)); d["ob"] = rng.integers(0, 16, (N, 8, 16, T)); d["xb"] = rng.integers(0, 16, (N, 8, 16))
    for n in ("a", "b", "v"): d[n] = rng.integers(0, 256, (N, 8, RO * T))
    return d, lab
def pack(d):
    lk = np.concatenate([256 * d["nm"] + d["wt"], d["w15"][:, :, None, :]], axis=2)
    return {"lk": np.ascontiguousarray(lk.reshape(N, 128, H)).astype(np.int32), "em": d["em"].reshape(N, 128, H).astype(np.float32).astype(BF),
            "ob": d["ob"].reshape(N, 128, T).astype(np.float32).astype(BF), "xb": d["xb"].reshape(N, 128, 1).astype(np.float32).astype(BF),
            "pe": np.stack([gtable(p[:, 0::2]) for p in d["st"]]), "po": np.stack([gtable(p[:, 1::2]) for p in d["st"]]),
            "nua": d["a"].astype(np.int32), "nub": d["b"].astype(np.int32), "vd": d["v"].astype(np.int32)}
def shares(t, n):
    return t // n + (np.arange(n) < t % n)
def tight(rng, d, g, i0):
    o = 2 + rng.permutation(S - 2)[:128]; X, Y, z = o[:8], o[8:].reshape(8, 15), o[8:]
    i = np.arange(i0, TH); p = np.arange(max(i0 - 1, 0), TH); vs = np.array([255, 255, 255, 255, 255, 255, 128, 128])
    x = d["st"][:, g]; x[:, 2 * p + 1] = X[p % 8]
    y = np.full(16, 15); y[15] = 1
    x = d["ob"][:, g]; x[:, :, 2 * i] = y[:, None]
    x = d["nm"][:, g]; x[:, :, X] = Y.T
    x[:, :8, z] = X[(np.arange(8)[:, None] + np.arange(120)[None, :]) % 8]; x[:, 8:, z] = rng.integers(0, H, (N, 7, 120))
    d["xb"][:, g] = 0
    for h in range(0, 2 * RO, 2):
        for n in ("a", "b"):
            x = d[n][:, g]; x[:, h * TH + i] = 0
        x = d["v"][:, g]; x[:, h * TH + i] = vs[(i - 1) % 8]
    for r in range(N):
        m = [int(rng.integers(17, 27)), int(rng.integers(33, 40)), int(rng.integers(65, 67)), int(rng.integers(180, 186)), int(rng.choice(np.array([7, 13, 14, 26, 28]))), int(rng.choice(np.array([52, 56, 104, 112])))]
        c6 = 128 * int(rng.integers(130, 181)) + int(rng.integers(1, 64)); c7 = 128 * int(rng.integers(130, 180)) + 65 + int(rng.integers(0, 64))
        case = ((1, 255 * m[0] + 1, m[0]), (2, 255 * m[1] + 1, m[1]), (4, 255 * m[2] + 1, m[2]), (13, 255 * m[3] + 1, m[3]),
                (3, 255 * m[4], m[4]), (9, 255 * m[5], m[5]),
                (7, c6, c6), (7, c7, c7 - 1))
        for j in range(8):
            k, c, rest = case[j]
            e = np.concatenate([shares(c, k + 1), shares(rest, 14 - k)]); a = e // 15
            F = np.zeros((16, 15), np.int64)
            F[:15] = (a // 15 + (np.arange(15)[:, None] < a % 15))[rng.permutation(15)]; F[15] = e - 15 * a
            x = d["em"][r, g]; x[:, Y[j]] = F
def setup_inputs(rng):
    return pack(parts(rng, 0.05, False)[0])
def setup_inputs_spread(rng):
    d, lab = parts(rng, 0.05, True)
    d["wt"] = np.minimum(np.exp2(8 * rng.random((N, 8, 15, H))).astype(np.int64), 255); d["w15"] = np.minimum(np.exp2(8 * rng.random((N, 8, H))).astype(np.int64), 255)
    top = np.array([2, 4, 8, 16])
    d["em"] = (top[rng.integers(0, 4, (N, 8, 1, H))] * rng.random((N, 8, 16, H))).astype(np.int64)
    d["ob"] = (top[rng.integers(0, 4, (N, 8, 1, T))] * rng.random((N, 8, 16, T))).astype(np.int64)
    d["a"] = (256 * rng.random(d["a"].shape) ** 2).astype(np.int64); d["b"] = (256 * rng.random(d["b"].shape) ** 3).astype(np.int64)
    d["v"] = np.where(rng.random(d["v"].shape) < 0.5, (256 * rng.random(d["v"].shape) ** 3).astype(np.int64), 255 - (256 * rng.random(d["v"].shape) ** 3).astype(np.int64))
    return pack(d)
def setup_inputs_ends(rng):
    d, lab = parts(rng, 0.0, False)
    m = rng.random(d["nm"].shape) < 0.76; hi = rng.random(d["nm"].shape) < 0.5
    d["nm"] = np.where(m, np.where(hi, H - 1, 0), d["nm"]); d["wt"] = np.where(hi, 255, 1)
    d["w15"] = 1 + 254 * rng.integers(0, 2, (N, 8, H))
    for n in ("em", "ob", "xb"): d[n] = 15 * rng.integers(0, 2, d[n].shape)
    d["st"] = np.where(rng.random(d["st"].shape) < 0.72, (H - 1) * rng.integers(0, 2, d["st"].shape), d["st"])
    for n in ("a", "b"): d[n] = 255 * rng.integers(0, 2, d[n].shape)
    v = 255 * rng.integers(0, 2, d["v"].shape)
    d["v"] = np.where(rng.random(v.shape) < 0.78, v, rng.choice(np.array([1, 127, 128, 129, 254]), v.shape))
    d["v"][:, 7] = np.where(rng.random((N, RO * T)) < 0.4, 128, d["v"][:, 7])
    ring = np.array([H - 1, 1, H - 1, H - 2, H - 1, 1, H - 1, H - 1, H - 2, H - 1, 1, H - 1, H - 2, H - 1, H - 2])
    for c, full in ((H - 1, 15), (H - 2, 9), (1, 11)):
        d["nm"][:, 7, :, c] = ring; d["wt"][:, 7, :, c] = np.where(np.arange(15) < full, 255, 1); d["w15"][:, 7, c] = 255; d["em"][:, 7, :, c] = 15
    d["nm"][:, 7, :, 0] = 0; d["wt"][:, 7, :, 0] = 1; d["w15"][:, 7, 0] = 1; d["em"][:, 7, :, 0] = 0; d["xb"][:, 7] = 15
    d["st"][:, 7] = rng.choice(np.array([0, 0, 0, 0, H - 1, H - 1, H - 1, H - 1, H - 2, 1]), (N, T))
    d["st"][:, 7, T - 3] = H - 1; d["st"][:, 7, T - 2] = 0; d["st"][:, 7, T - 1] = H - 1; d["st"][:, 7, 0] = H - 1
    o = rng.random((N, 8, 1, T)); d["ob"] = np.where(o < 0.08, 0, d["ob"])
    d["ob"][:, 7] = np.where(o[:, 7] > 0.5, 15, d["ob"][:, 7]); d["ob"][:, 7, :, T - 2:] = 15
    for h in range(2 * RO):
        j = h * TH + TH - 1; d["a"][:, 7, j] = 0; d["b"][:, 7, j] = 0; d["v"][:, 7, j] = 128
    X, L, V = (int(c) for c in 2 + rng.permutation(S - 2)[:3]); few = np.array([0, 16, 17, 18, 255]); rk = np.arange(N)
    x = d["nm"][:, 6]; x[(x == L) | (x == V)] = 0
    d["nm"][:, 6, :, L] = V; d["nm"][:, 6, :, V] = 0; d["nm"][:, 6, 0, V] = X; d["wt"][:, 6, 0, V] = 254; d["em"][:, 6, 0::2, V] = 15
    d["nm"][:, 6, :, X] = X; d["wt"][:, 6, :, X] = 255; d["w15"][:, 6, X] = 254; d["em"][:, 6, 0::2, X] = 15; d["xb"][:, 6, 0] = 15
    x = d["st"][:, 6]; x[(x == L) | (x == V)] = 0
    d["st"][:, 6] = np.where(rng.random((N, T)) < 0.7, X, d["st"][:, 6])
    d["st"][:, 6, :3] = X; d["st"][:, 6, T - 2 * RO - 4:] = X; d["ob"][:, 6, 0, :2] = 15
    x = d["st"][:, 6]; x[:, [TH - 1, TH + 8]] = L; x[:, [TH, TH + 1, TH + 9, TH + 10]] = X
    x = d["ob"][:, 6]; x[:, :, [TH - 1, TH, TH + 1, TH + 8, TH + 9, TH + 10]] = 0
    for n in ("a", "b"): d[n][:, 6] = few[rng.integers(0, 5, (N, RO * T))]
    for h in range(2 * RO):
        i = h * TH; j = i + TH - 1
        d["b"][:, 6, i] = few[rng.integers(0, 3, N)]; d["v"][:, 6, i] = 0
        d["a"][:, 6, j] = 17 + (rk + h) % 2; d["b"][:, 6, j] = 17 + ((rk + h) >> 1) % 2
        j = i + TH // 2 + 4 * (h & 1); d["a"][:, 6, j] = 0; d["b"][:, 6, j] = 17
    tight(rng, d, 5, TH - 16)
    return pack(d)
def setup_inputs_corners(rng):
    d, lab = parts(rng, 0.0, False)
    few = np.array([1, 2, 127, 128, 129, 238, 239, 240, 254, 255])
    d["wt"] = few[rng.integers(0, 10, (N, 8, 15, H))]; d["w15"] = few[rng.integers(0, 9, (N, 8, H))]
    for n in ("a", "b"): d[n] = rng.choice(np.array([0, 1, 128, 254, 255]), d[n].shape)
    d["v"] = rng.choice(np.array([0, 1, 127, 128, 129, 254, 255]), d["v"].shape)
    d["xb"][:, :, 0] = np.maximum(d["xb"][:, :, 0], 1); d["ob"][:, :, 0] = np.maximum(d["ob"][:, :, 0], 1)
    for g in range(8):
        o = rng.permutation(H); low, odd, z0 = o[:24], o[24:24 + TH + 32], o[24 + TH + 32]
        d["nm"][:, g] = low[rng.integers(0, 24, (N, 15, H))]
        for r in range(N):
            p = d["st"][r, g]; p[0::2] = low[rng.integers(0, 24, TH)]; p[1::2] = rng.permutation(odd)[:TH]; p[T - 1] = z0
            c = (g + r) % 8; n = (0, 1, B - 1, B + 1, B, TH, B, 2)[c]; z = rng.permutation(TH)
            if c in (1, 4, 6): z = np.concatenate([np.array([TH - 1]), z[z != TH - 1]])
            shut = z[n:]
            l = np.concatenate([np.array([z0]), p[1:T - 1:2]])
            d["a"][r, g, :TH] = 0; d["a"][r, g, shut] = 255
            d["nm"][r, g, 0, l[shut]] = p[2 * shut]; d["wt"][r, g, 0, l[shut]] = 255
    return pack(d)
def setup_inputs_crowd(rng):
    d, lab = parts(rng, 0.03, False)
    for g in range(4):
        c = rng.permutation(lab[g, int(rng.integers(0, NC))])[:4]
        x = d["nm"][:, g]; x[:, :, c] = c[rng.integers(0, 4, (N, 15, 4))]
        x = d["w15"][:, g]; x[:, c] = 255
        if g < 2: d["st"][:, g] = c[0]
        if g == 1: d["st"][np.arange(N), 1, rng.integers(0, T, N)] = c[1]
        if g == 2: d["st"][:, g] = c[rng.integers(0, 4, (N, T))]
        if g == 3: d["st"][:, g] = np.where(np.arange(T) % 2 == 0, c[0], c[1])
        for n in ("a", "b"): d[n][:, g] = rng.integers(0, 30, (N, RO * T)) * rng.integers(0, 2, (N, RO * T))
    d["v"][:, 0] = 255; d["v"][:, 1] = 0
    d["ob"][:, 7, :, 1::2] = 0
    tight(rng, d, 7, 0)
    return pack(d)
def setup_inputs_calm(rng):
    d, lab = parts(rng, 0.0, False)
    d["w15"][:] = 255; d["xb"][:] = 0; d["xb"][:, :, 0] = 15; d["ob"][:, :, 0] = 0
    for g in range(8):
        for par in range(2):
            pos = 1 + rng.permutation(15)[:g % 4]
            x = d["ob"][:, g, 0]; x[:, 2 * pos + par] = 15
            for w in range(RO):
                j = (2 * w + par) * TH + pos
                x = d["v"][:, g]; x[:, j] = 255
                x = d["a"][:, g]; x[:, j] = 0
    return pack(d)
def check_ranges(d):
    bad = []
    for k, lo, hi in (("lk", 1, 256 * H - 1), ("em", 0, 15), ("ob", 0, 15), ("xb", 0, 15), ("pe", 0, H - 1), ("po", 0, H - 1), ("nua", 0, 255), ("nub", 0, 255), ("vd", 0, 255)):
        x = np.asarray(d[k]).astype(np.float64)
        if not (np.min(x) >= lo and np.max(x) <= hi): bad.append("range of " + k)
        elif np.any(x != np.floor(x)): bad.append(k + " is not whole")
    x = np.asarray(d["lk"]).astype(np.int64)
    if np.any((x & 255) == 0): bad.append("a weight of lk is 0")
    if np.any(x.reshape(N, 8, 16, H)[:, :, 15] > 255): bad.append("a leftover of lk has a name")
    return bad
def pick(tab, ix):
    return np.take_along_axis(tab, ix.reshape(8, 1, -1), 2).reshape((8, 16) + ix.shape[1:])
def reference(lk, em, ob, xb, pe, po, nua, nub, vd):
    P = lk.astype(np.int64).reshape(N, 8, 16, H); E = em.astype(np.float32).astype(np.int64).reshape(N, 8, 16, H)
    O = ob.astype(np.float32).astype(np.int64).reshape(N, 8, 16, T); base = xb.astype(np.float32).astype(np.int64).reshape(N, 8, 16)
    st = np.zeros((N, 8, T), np.int64)
    for b in range(N): st[b, :, 0::2] = gentries(pe[b]); st[b, :, 1::2] = gentries(po[b])
    na = nua.astype(np.int64); nb = nub.astype(np.int64); vv = vd.astype(np.int64)
    named = (np.arange(16) < 15)[None, :, None]; acc = np.zeros((N, 8, 16, T), np.float64)
    for h in range(2 * RO):
        w, par = h >> 1, h & 1; cut = slice(h * TH, (h + 1) * TH)
        for r in range(N):
            b = (r + w) % N; path = st[b]
            if par == 0: s, q, l = path[:, 0::2], path[:, 1::2], np.concatenate([st[(b - 1) % N][:, T - 1:], path[:, 1:T - 1:2]], axis=1)
            else: s, l, q = path[:, 1::2], path[:, 0::2], np.concatenate([path[:, 2::2], st[(b + 1) % N][:, :1]], axis=1)
            y = O[b][:, :, par::2]; v = vv[r][:, cut]
            A = pick(P[r], l); nm, wt = A >> 8, A & 255
            u = (na[r][:, cut] * np.sum(np.where(named & (nm == s[:, None, :]), wt, 0), axis=1)) >> 8
            D = pick(P[r], s)
            u2 = (nb[r][:, cut] * np.sum(np.where(named & ((D >> 8) == q[:, None, :]), D & 255, 0), axis=1)) >> 8
            C = pick(P[r], nm)
            hold = np.any(named[..., None] & ((C >> 8) == q[:, None, None, :]) & ((C & 255) > u2[:, None, None, :]), axis=1)
            hold[:, 15] = True
            F = pick(E[r], nm); F[:, :, 15] = base[r][:, :, None]
            e = np.sum(F * y[:, :, None, :], axis=1)
            sv = (wt > u[:, None, :]) & hold
            c = np.add.accumulate(np.where(sv, e, 0), axis=1)
            hit = 256 * c > v[:, None, :] * c[:, 15:16]; got = hit[:, 15]; k = np.argmax(hit, axis=1)
            gw = np.where(sv, 1.0, 0.5) * np.exp(e * 2.0 ** -12)
            acc[r][:, :, par::2] = 0.5 * acc[r][:, :, par::2] + np.sum(gw[:, None] * F, axis=2)
            first = np.zeros((8, TH), bool)
            for g in range(8): first[g, np.unique(l[g], return_index=True)[1]] = True
            ask = (got & (k == 15) & first).astype(np.int64); before = np.add.accumulate(ask, axis=1) - ask; born = (ask == 1) & (before < B)
            ns = np.where(got & (k < 15), np.take_along_axis(nm, k[:, None, :], 1)[:, 0], s); ns = np.where(born, S + h * B + before, ns)
            for g in range(8):
                i = np.flatnonzero(first[g] & got[g] & (k[g] < 15)); ki = k[g, i]
                P[r, g, ki, l[g, i]] = 256 * nm[g, ki, i] + np.minimum(wt[g, ki, i] + 16, 255)
                i = np.flatnonzero(born[g]); j = before[g, i]; new = S + h * B + j
                P[r, g, j & 7, l[g, i]] = 256 * new + 128
                tile = A[g][:, i]; tile[0] = 256 * q[g, i] + 128
                P[r, g][:, new] = tile; E[r, g][:, new] = y[g][:, i]
            st[b, :, par::2] = ns
    z = np.zeros((N, 8, 16, T), np.float64)
    for r in range(N):
        A = pick(P[r], st[(r + RO - 1) % N]); F = pick(E[r], A >> 8); F[:, :, 15] = base[r][:, :, None]
        z[r] = np.sum((A & 255)[:, None] * F, axis=2)
    return {"ya": acc.reshape(N, 128, T).astype(np.float32), "yz": z.reshape(N, 128, T).astype(np.float32)}

def check_inputs(d):
    bad = list(check_ranges(d))
    if not bad:
        for name, y in reference(**d).items():
            for q in range(N):
                v = np.abs(np.asarray(y[q], np.float64)); s = np.sqrt(np.mean(v * v))
                if v.max() > 8 * s or s < 2.0 ** 4: bad.append('%s of rank %d is uneven or too small' % (name, q))
    return bad

@@ -1,0 +1,679 @@
+import math
+from concourse.bass import DstId, RemoteDMATransfer
+from concourse.mybir import AluOpType as ALU, ActivationFunctionType as AF
+
+F32, BF, F16, I32, U16 = "float32", "bfloat16", "float16", "int32", "uint16"
+H, S0, NH = 2048, 1952, 6
+SL = 144
+SB = {
+    "LK": (2048, I32), "TB": (2304, F32), "EM": (2048, BF), "OB": (768, BF), "XB": (1, F32),
+    "PEPO": (16, I32), "POX": (8, I32), "RN": (144, I32), "RB": (144, BF), "L16": (18, F16),
+    "RX": (7 * SL, F32), "PK": (6 * SL, F32), "LU": (7 * 16, U16), "PU": (48, U16), "CR": (432, BF), "CS": (256, BF), "EQ0": (128, BF),
+    "AB": (352, F32), "TT": (576, F32), "NL": (256, U16), "PERM": (8, U16),
+    "FA": (2048, BF), "FB": (2048, BF), "CW": (2048, F32), "XW": (2048, BF), "IW": (2048, BF), "PW": (2048, BF),
+    "PR0": (2048, F32), "PR1": (2048, F32), "PZ": (2048, F16), "HB": (768, F32), "AC": (768, F32),
+    "DD": (256, BF), "CL": (256, BF), "GT": (256, BF), "U2": (128, F16), "NM": (256, F32),
+    "WT": (128, F32), "WB": (256, BF), "SVW": (128, F32), "ND": (128, F32), "ND0": (128, F32),
+    "VM": (128, F32), "AQ": (144, F32), "YS": (288, BF), "ABV": (768, F32), "EA": (704, BF), "EQ": (704, BF),
+    "OF": (128, F16), "OFU": (16, U16), "SV": (128, BF), "SE": (128, F32), "GH": (256, BF),
+    "GL": (256, BF), "VC": (128, F32), "HIT": (128, BF), "ASK": (144, BF), "CUM": (145, BF),
+    "ZZ": (128, F32), "XX": (128, F16), "YY": (128, F16), "NN": (144, F32), "JK": (144, BF), "IAC": (1, F32),
+    "IDX": (2, U16), "G1": (16, F32), "YA": (256, F32), "YZ": (256, F32),
+    "PI": (8, I32), "PC": (16, F32), "RM": (16, F32), "BM": (16, F32), "COLG": (128, F32), "COLK": (128, F32),
+    "DUM": (128, F32), "CV": (96, F32), "C2": (8, F32), "POSK": (8, F32), "T0": (128, F32), "T1": (128, F32),
+    "T2": (128, F32), "BO": (128, BF), "BO32": (128, F32), "BO15": (128, BF), "IDS": (128, F32), "BO4": (128, BF),
+    "ES": (128, F32), "ZS": (143, BF), "ZH": (143, BF), "Z1": (143, BF), "ZX": (128, BF), "TRI": (128, F32),
+    "DIF": (128, BF), "DIFX": (128, BF), "ASKM": (128, BF), "ID": (128, BF), "IDN": (128, BF), "ID32": (128, F32),
+    "ID128": (128, BF), "IC1": (128, BF), "IC2": (128, BF), "DN": (128, F32), "D0": (128, F32), "ST": (2048, BF),
+    "ZERO": (512, BF), "ZP": (528, BF), "POSB": (128, BF), "K256": (128, BF), "KM": (128, BF),
+    "K16": (144, BF), "KM8": (512, BF), "R0M": (128, BF),
+}
+SCRATCH = {n: ("sbuf", [128, w], d) for n, (w, d) in SB.items()}
+for _b in range(8):
+    SCRATCH["P%d" % _b] = ("psum", [128, 512], F32)
+DMAS = ["dpo", "dpe", "dl0", "dl1", "dl2", "dl3", "dem", "dob", "dn0", "dn1", "dn2", "dxb", "dya", "dyz"]
+SEMAPHORES = (["qv", "qa", "qp", "qg", "loc", "pox", "ob1", "ob2", "fl0", "fl1", "cx0", "cx1"] + DMAS + ["rx%d" % h for h in range(5)]
+              + ["fa%d" % h for h in range(NH)] + ["fb%d" % h for h in range(NH)])
+CYC, PEC, FIX, GAT, SCA, HOP, REM = 1.0, 0.5, 60.0, 1.56, 3.8, 70.0, 2500.0
+
+
+def bits(engines):
+    m = 0
+    for e in engines:
+        m |= 1 << e
+    return m
+
+
+def helper_of(c, T, topo):
+    return [x for x in topo.cores_of(c) if x not in T.cores and topo.die(x) == topo.die(c)][0]
+
+
+def helper_program(g, core, owner, T, topo):
+    rid, pid = topo.addr(owner, core)
+    eng = topo.engines(core, owner)
+    eng = eng[len(eng) // 2:]
+    for h in range(NH):
+        g.wait_ge(T.sem["fa%d" % h], len(eng))
+        g.remote_dma(T.AC[:, h * 128:(h + 1) * 128], T.HB[:, h * 128:(h + 1) * 128], T.sem["fb%d" % h], T.sem.loc,
+                     pid, rid, bits(eng))
+    g.wait_ge(T.sem.loc, NH * len(eng))
+
+
+def hit(x, y):
+    return x[1] < y[2] and y[1] < x[2]
+
+
+def depends(ops, banks):
+    deps, last, lastmm, others = [], {}, {}, {}
+    for i, (q, fn, rd, wr, tok, c, lat, aft) in enumerate(ops):
+        d = set()
+        for lst, isw in ((rd, False), (wr, True)):
+            for r in lst:
+                ps = SCRATCH[r[0]][0] == "psum"
+                for (j, r2, w2) in last.get(r[0], []):
+                    same = ops[j][0] == q
+                    if q == "p" and same:
+                        continue
+                    if (banks and ps and not same) or ((w2 or isw) and hit(r, r2)):
+                        d.add(j)
+        if q == "p" and not banks:
+            if wr[0][0] in lastmm:
+                d.add(lastmm[wr[0][0]])
+            lastmm[wr[0][0]] = i
+            d |= others.pop(wr[0][0], set())
+        elif not banks:
+            for r in rd + wr:
+                if SCRATCH[r[0]][0] == "psum":
+                    others.setdefault(r[0], set()).add(i)
+                    if r[0] in lastmm:
+                        d.add(lastmm[r[0]])
+        if q == "x":
+            d = set()
+        deps.append(d)
+        for lst, isw in ((rd, False), (wr, True)):
+            for r in lst:
+                old = last.get(r[0], [])
+                if isw:
+                    old = [e for e in old if not (r[1] <= e[1][1] and e[1][2] <= r[2] and
+                                                  (e[0] in d or (q == "p" and ops[e[0]][0] == q)))]
+                last[r[0]] = old + [(i, r, isw)]
+    return deps
+
+
+def schedule(ops):
+    n = len(ops)
+    deps = depends(ops, False)
+    for i in range(n):
+        if ops[i][7] is not None:
+            deps[i].add(ops[i][7])
+    suc = [[] for _ in range(n)]
+    for i in range(n):
+        for j in deps[i]:
+            suc[j].append(i)
+    pb = [set(r[0] for r in o[2] + o[3] if SCRATCH[r[0]][0] == "psum") for o in ops]
+
+    def chains(order, mix):
+        pri, nxt = [0.0] * n, {}
+        for i in reversed(order):
+            q = ops[i][0]
+            p = ops[i][6] + max([pri[k] + (0 if ops[k][0] == "p" == q else HOP) for k in suc[i]] + [0.0])
+            if q in nxt and q != "x":
+                p = max(p, (1 - mix) * p + mix * pri[nxt[q]])
+            pri[i] = ops[i][5] + p
+            nxt[q] = i
+        return pri
+
+    def run(pri, slack):
+        left = [len(d) for d in deps]
+        ready = [i for i in range(n) if not left[i]]
+        fin, free, bank, order, base = [0.0] * n, {}, {}, [], [0.0] * n
+        while ready:
+            est = {}
+            for i in ready:
+                q = ops[i][0]
+                t = max(base[i], free.get(q, 0.0) if q != "x" else 0.0)
+                for b in pb[i]:
+                    for q2, f in bank.get(b, {}).items():
+                        if q2 != q:
+                            t = max(t, f + HOP)
+                est[i] = t
+            i0 = min(ready, key=lambda i: (est[i], -pri[i], i))
+            q = ops[i0][0]
+            i = max([k for k in ready if ops[k][0] == q and est[k] <= est[i0] + min(slack, ops[i0][5])],
+                    key=lambda k: (pri[k], -k))
+            ready.remove(i)
+            order.append(i)
+            free[q] = est[i] + ops[i][5]
+            fin[i] = free[q] + ops[i][6]
+            for b in pb[i]:
+                bank.setdefault(b, {})[q] = fin[i]
+            for k in suc[i]:
+                base[k] = max(base[k], fin[i] + (0 if ops[k][0] == "p" == q else HOP))
+                left[k] -= 1
+                if not left[k]:
+                    ready.append(k)
+        return max(fin), order
+
+    if not ORDER:
+        best = None
+        for slack, mix in TRY:
+            pri = chains(list(range(n)), 0.0)
+            for it in range(ROUNDS):
+                t, order = run(pri, slack)
+                if best is None or t < best[0]:
+                    best = (t, order, slack, mix, it)
+                new = chains(order, mix)
+                pri = [0.5 * (x + y) for x, y in zip(pri, new)]
+        ORDER.append(best)
+    return [ops[i] for i in ORDER[0][1]]
+
+
+ORDER = []
+TRY = [(100.0, 0.5), (300.0, 0.5), (300.0, 0.9), (600.0, 0.9)]
+ROUNDS = 8
+
+
+def rank_program(g, core, T, topo):
+    rank = T.rank_of(core)
+    if rank is None:
+        for c in T.cores:
+            if helper_of(c, T, topo) == core:
+                helper_program(g, core, c, T, topo)
+        return
+    N = len(T.cores)
+    ops = []
+
+    def s(n, a=0, b=None, st=1):
+        b = SCRATCH[n][1][1] if b is None else b
+        return (T[n][:, a:b] if st == 1 else T[n][:, a:b:st], [(n, a, b)], [], len(range(a, b, st)))
+
+    def ind(w, o):
+        return (w[0].indirect(o[0]), w[1], o[1], 16 * o[3])
+
+    def rec(q, fn, outs, ins, c, tok=None, lat=0.0, aft=None):
+        rd, wr = [], []
+        for x in ins:
+            if isinstance(x, tuple):
+                rd += x[1] + x[2]
+        for x in outs:
+            wr += x[1]
+            rd += x[2]
+        ops.append((q, fn, rd, wr, tok, c, lat, aft))
+        return len(ops) - 1
+
+    def v(x):
+        return x[0] if isinstance(x, tuple) else x
+
+    def cost(o, a, f=1.0):
+        if o[2]:
+            return FIX + o[3] * SCA * CYC
+        if a[2]:
+            return FIX + o[3] * GAT * CYC
+        return FIX + max(64, o[3] * f) * CYC
+
+    def half(*x):
+        return 0.5 if all(SCRATCH[y[1][0][0]][2] in (BF, F16, U16) for y in x) else 1.0
+
+    def tt(o, a, b, op):
+        f = 1.0 if "psum" in (SCRATCH[a[1][0][0]][0], SCRATCH[b[1][0][0]][0]) else 2.0
+        rec("v", lambda: g.vector.tensor_tensor(o[0], a[0], b[0], op), [o], [a, b], cost(o, a, f))
+
+    def ts(o, a, s1, op0, s2=None, op1=None):
+        if op1 is None:
+            rec("v", lambda: g.vector.tensor_scalar(o[0], a[0], v(s1), None, op0), [o], [a, s1], cost(o, a, half(o, a)))
+        else:
+            rec("v", lambda: g.vector.tensor_scalar(o[0], a[0], v(s1), v(s2), op0, op1), [o], [a, s1, s2],
+                cost(o, a, half(o, a)))
+
+    def cp(o, a):
+        rec("v", lambda: g.vector.tensor_copy(o[0], a[0]), [o], [a], cost(o, a, half(o, a)))
+
+    def ms(o, c):
+        rec("v", lambda: g.vector.memset(o[0], c), [o], [], cost(o, o, half(o)))
+
+    def tr(o, a):
+        rec("v", lambda: g.vector.transpose(o[0], a[0]), [o], [a], cost(o, a))
+
+    def scan(o, a, b, op0, op1):
+        rec("v", lambda: g.vector.tensor_tensor_scan(o[0], a[0], b[0], 0.0, op0, op1), [o], [a, b], cost(o, a, half(o, a, b)))
+
+    def act(o, a, f=AF.Identity, bias=0.0, scale=1.0, acc=None):
+        if acc is None:
+            rec("a", lambda: g.scalar.activation(o[0], a[0], f, v(bias), v(scale)), [o], [a, bias, scale], cost(o, a))
+        else:
+            rec("a", lambda: g.scalar.activation(o[0], a[0], f, v(bias), v(scale), accum_out=acc[0]), [o, acc],
+                [a, bias, scale], cost(o, a))
+
+    def mm(o, l, r, st, sp):
+        rec("p", lambda: g.tensor.matmul(o[0], l[0], r[0], st, sp), [o], [l, r],
+            max(64, r[3]) * PEC * (4 if SCRATCH[r[1][0][0]][2] == F32 else 1))
+
+    def iota(o, pat, base, cm, fl=True):
+        if fl:
+            rec("g", lambda: g.iota(o[0], pat, base, cm, allow_small_or_imprecise_dtypes=True), [o], [], 130 + 2 * o[3])
+        else:
+            rec("g", lambda: g.iota(o[0], pat, base, cm), [o], [], 130 + 2 * o[3])
+
+    def dma(q, o, a, sem, lat, **kw):
+        e = {"s": g.sync, "a": g.scalar, "g": g}[q]
+        rec(q, lambda: e.dma_start(o[0], a[0], **kw).then_inc(T.sem[sem], 16), [o], [a], 100.0, (sem, 16), lat)
+
+    nloc = [0]
+
+    def send(dst, src, o, a, sem):
+        rid, pid = topo.addr(dst, core)
+        eng = topo.engines(core, dst)[:8]
+        nloc[0] += len(eng)
+        i = rec("g", lambda: g.remote_dma(o[0], a[0], T.sem[sem], T.sem.loc, pid, rid, bits(eng)), [], [a], 300.0, ("loc", 0))
+        rec("x", None, [o], [], 0.0, (sem, len(topo.engines(src, core)[:8])), REM, i)
+
+    prv, nxt = T.cores[(rank - 1) % N], T.cores[(rank + 1) % N]
+    hlp = helper_of(core, T, topo)
+    heng = topo.engines(core, hlp)
+    heng = heng[len(heng) // 2:]
+    nfold = [0, 0]
+
+    def fold(h):
+        pr = "PR%d" % (h & 1)
+        src = [s(pr, k * 128, (k + 1) * 128) for k in range(16)]
+        if h >= 2:
+            src.append(s("AC", (h - 2) * 128, (h - 1) * 128))
+        rid, pid = topo.addr(hlp, core)
+        nfold[h & 1] += len(heng)
+        t = RemoteDMATransfer(dst_ids=[DstId(rid=rid, pnc=pid)], dma_engine_mask=bits(heng), remote_sem=T.sem["fa%d" % h],
+                              srcs=[x[0] for x in src], dsts=[T.HB[:, h * 128:(h + 1) * 128]], alu_op=1)
+        i = rec("g", lambda: g.remote_dma_fused([t], local_sem=T.sem["fl%d" % (h & 1)]), [], src, 300.0,
+                ("fl%d" % (h & 1), nfold[h & 1]), 3500.0)
+        rec("x", None, [s("AC", h * 128, (h + 1) * 128)], [], 0.0, ("fb%d" % h, len(heng)), REM, i)
+
+    def dr(t):
+        return (t, [], [], 0)
+
+    add, sub, mul, mx, mn = ALU.add, ALU.subtract, ALU.mult, ALU.max, ALU.min
+    dma("s", s("PEPO", 8, 16), dr(T.po[:]), "dpo", 2000.0)
+    for c in range(4):
+        dma("s", s("LK", c * 512, (c + 1) * 512), dr(T.lk[:, c * 512:(c + 1) * 512]), "dl%d" % c, 2400.0 + 450 * c)
+    dma("s", s("EM"), dr(T.em[:]), "dem", 4500.0)
+    dma("a", s("PEPO", 0, 8), dr(T.pe[:]), "dpe", 2000.0)
+    dma("a", s("OB", 0, 256), dr(T.ob[:]), "dob", 2500.0)
+    for i, t in enumerate((T.nua, T.nub, T.vd)):
+        dma("a", s("RN", i * 48, (i + 1) * 48), dr(t[:]), "dn%d" % i, 2500.0)
+    iota(s("PI", 0, 1), [[0, 1]], 0, 1, False)
+    iota(s("COLG"), [[1, 8], [0, 16]], 0, 0)
+    iota(s("COLK"), [[0, 8], [1, 16]], 0, 0)
+    prv, nxt = T.cores[(rank - 1) % N], T.cores[(rank + 1) % N]
+    send(nxt, prv, s("POX"), s("PEPO", 8, 16), "pox")
+    iota(s("C2"), [[2, 8]], 0, 0)
+    dma("g", s("XB"), dr(T.xb[:]), "dxb", 3000.0, allow_slow_non_contiguous=True)
+    iota(s("POSB"), [[2, 128]], -128, 0)
+    iota(s("DUM"), [[2, 128]], H, 0)
+    iota(s("CV"), [[512, 96]], 512 * S0 + 128, 0)
+    for w in (1, 2):
+        send(T.cores[(rank - w) % N], T.cores[(rank + w) % N], s("OB", w * 256, (w + 1) * 256), s("OB", 0, 256), "ob%d" % w)
+
+    def pc(i):
+        return s("PC", i, i + 1)
+
+    def rm(i):
+        return s("RM", i, i + 1)
+
+    def st(k):
+        return s("ST", k * 128, (k + 1) * 128)
+
+    for n in ("ZS", "AB", "ZP", "ZERO"):
+        ms(s(n), 0.0)
+    p0 = s("PI", 0, 1)
+    ts(s("PI", 1, 2), p0, 15, ALU.bitwise_and)
+    ts(s("PI", 2, 3), p0, 4, ALU.arith_shift_right)
+    ts(s("PI", 3, 4), p0, 7, ALU.bitwise_and)
+    ts(s("PI", 4, 5), p0, 3, ALU.arith_shift_right, 1, ALU.bitwise_and)
+    tt(s("PI", 5, 6), p0, s("PI", 2, 3), add)
+    ts(s("PI", 6, 7), s("PI", 5, 6), 1, ALU.bitwise_and)
+    cp(s("PC", 0, 7), s("PI", 0, 7))
+    ts(s("BO"), s("COLG"), pc(2), ALU.is_equal)
+    ts(s("RM"), s("COLK", 0, 16), pc(1), ALU.is_equal)
+    for k in range(16):
+        act(st(k), s("BO"), scale=rm(k))
+    ts(pc(7), pc(6), 144.0, mul, pc(4), add)
+    ts(pc(8), pc(3), 16.0, mul, pc(7), add)
+    ts(s("PERM"), s("C2"), pc(8), add)
+    cp(s("ZS", 15, 143, 16), s("BO", 0, 128, 16))
+    ts(pc(9), pc(1), 15.0, ALU.is_lt)
+    ts(pc(10), pc(1), 0.5, add)
+    ts(pc(11), pc(1), 0.0, ALU.is_gt)
+    ts(pc(12), rm(0), 128.0, mul)
+    tt(pc(13), rm(15), rm(14), sub)
+    ts(pc(14), pc(1), 2.0, mul)
+    ms(pc(15), 128.0)
+    ts(s("POSK"), s("C2"), 16.0, mul, pc(14), add)
+    ts(s("ZP", 0, 8), s("POSK"), 1.0 / 512, mul)
+    ts(s("ZP", 392, 400), s("POSK"), 1.0 / 512, mul)
+    for a in (136, 400):
+        act(s("ZP", a, a + 128), s("POSB"), scale=1.0 / 512)
+    for a in (0, 144, 288):
+        ms(s("CR", a, a + 8), 0.0)
+    ms(s("EQ0", 0, 1), 0.0)
+    cp(s("LU", 8, 16), s("PEPO", 0, 8))
+    cp(s("LU", 24, 32), s("PEPO", 8, 16))
+    cp(s("L16", 0, 16), s("PEPO"))
+    ts(s("T2", 0, 8), s("PEPO", 8, 16), 512.0, mul)
+    tt(s("RX", SL + 132, SL + 140), s("T2", 0, 8), s("POSK"), add)
+    MAG = 1.5 * 2.0 ** 31
+    for c in range(4):
+        a, b = c * 512, (c + 1) * 512
+        ts(s("CW", a, b), s("LK", a, b), -128.0, add, MAG, add)
+        act(s("P%d" % (2 + (c & 1))), s("CW", a, b), bias=-MAG)
+        tt(s("TB", a, b), s("LK", a, b), s("P%d" % (2 + (c & 1))), add)
+    act(s("BO15"), s("BO"), scale=pc(9))
+    ms(pc(0), 256.0)
+    ts(s("T0"), s("COLK"), pc(1), sub)
+    ts(s("T1"), s("T0"), 0.0, ALU.is_equal)
+    tt(s("ID32"), s("T1"), s("BO"), mul)
+    for r in range(16):
+        mm(s("P7", r, 256, 16), st(r), s("L16", 0, 16), True, True)
+    act(s("RX", 12, 140), s("P7", 0, 128), scale=512.0)
+    act(s("RX", SL + 4, SL + 132), s("P7", 128, 256), scale=512.0)
+    cp(s("LU", 22, 24), s("POX", 6, 8))
+    cp(s("L16", 16, 18), s("POX", 6, 8))
+    mm(s("P7", 256, 258), st(15), s("L16", 16, 18), True, True)
+    act(s("RX", SL + 3, SL + 4), s("P7", 257, 258), scale=512.0)
+    ts(s("RB"), s("RN"), 1.0 / 256, mul)
+    cp(s("ID"), s("ID32"))
+    act(s("ZX"), s("ZS", 0, 128), scale=s("XB"))
+    ts(s("ZH"), s("ZS"), pc(9), mul, 4096.0, mul)
+    ms(s("KM"), -1.0 / 8192)
+    for n, c in (("K256", 256), ("K16", 16), ("KM8", -8)):
+        iota(s(n), [[0, s(n)[3]]], c, 0)
+    act(s("BO32"), s("BO"))
+    act(s("Z1"), s("ZS"), scale=rm(0))
+    act(s("R0M"), s("BO"), scale=rm(0))
+    ts(s("ASKM"), s("BO"), pc(13), mul, 2048.0, mul)
+    act(s("BO4"), s("BO"), scale=4096.0)
+    for n, c in (("ID128", 128.0), ("IDN", -1.0), ("IC1", 2832.0), ("IC2", 7.125), ("IDS", 1.0 / 512)):
+        act(s(n), s("ID32"), scale=c)
+    act(s("DN"), s("ID32"), scale=pc(11))
+    act(s("D0"), s("ID32"), scale=rm(0))
+    act(s("ASK", 128, 144), s("RM"), scale=16.0)
+    for f in ("FA", "FB"):
+        act(s(f, 1920, 2048), s("ZERO", 0, 128), bias=s("XB"))
+    ts(s("T2"), s("T0"), 0.0, ALU.is_ge)
+    tt(s("TRI"), s("T2"), s("BO"), mul)
+    ts(s("T2"), s("T0"), 1.0, ALU.is_equal)
+    tt(s("T1"), s("T1"), s("T2"), sub)
+    tt(s("DIF"), s("T1"), s("BO"), mul)
+    ms(s("DIF", 15, 128, 16), 0.0)
+    act(s("DIFX"), s("DIF"), scale=1.0 / 512)
+    ts(s("BM", 0, 8), s("COLK", 0, 8), pc(1), ALU.is_equal)
+    cp(s("BM", 8, 16), s("BM", 0, 8))
+    ms(s("CUM", 0, 1), 0.0)
+    ms(s("NN", 128, 144), 0.0)
+
+    TBW = s("TB", 0, 2048)
+    CH = [(0, 4), (4, 8), (8, 12), (12, 15)]
+
+    def names(lst, a, par):
+        a0, t0 = 176 * par, 288 * par
+        act(s("AB", a0 + a, a0 + 160 + (a & 1)), ind(TBW, lst))
+        tr(s("TT", t0, t0 + 128), s("AB", a0 + 32, a0 + 160))
+        tr(s("TT", t0 + 128, t0 + 288), s("AB", a0 + 16, a0 + 176))
+        ts(s("NL", 128 * par, 128 * par + 128), ind(s("TT", t0, t0 + 288), s("PERM")), 1.0 / 512, mul)
+        return s("AB", a0 + 32, a0 + 160)
+
+    def gat(dst, win, c, par, bias=0.0):
+        a, b = CH[c]
+        act(s(dst, a * 128, b * 128), ind(win, s("NL", 128 * par + a * 8, 128 * par + b * 8)), bias=bias)
+
+    def repeats(kb, k0, start):
+        pos = [0]
+        for c in range(8):
+            n = 128 - 16 * c
+            act(s("EA", pos[c], pos[c] + n), s("P7", 512 - n, 512), AF.Abs, bias=s(kb, k0 + c, k0 + c + 1), scale=-512.0)
+            pos.append(pos[c] + n)
+        act(s("EQ", 0, pos[8]), s("EA", 0, pos[8]), AF.Relu, bias=pc(15), scale=-1.0)
+        for c in range(8):
+            mm(s("P7", 16 * c, 128), s("BO4"), s("EQ", pos[c], pos[c + 1]), start and c == 0, c == 7)
+
+    def targets(h):
+        tt(s("OF"), s("DUM"), s("P7", 0, 128), mn)
+        for r in range(16):
+            mm(s("P7", 128, 136), s("Z1", 15 - r, 143 - r), s("OF", r, 128, 16), r == 0, r == 15)
+        cp(s("OFU", 8 * (h & 1), 8 * (h & 1) + 8), s("P7", 128, 136))
+
+    mm(s("P7", 384, 512), s("ID"), s("ZP", 136, 264), True, False)
+    mm(s("P7", 384, 512), s("IDS"), s("RX", SL + 4, SL + 132), False, True)
+    repeats("RX", SL + 132, True)
+    act(s("CR", 8, 136), s("P7", 0, 128))
+
+    def chance(h):
+        for i in range(3):
+            c = h * 128
+            while c < (h + 1) * 128:
+                x = c // 48
+                e = min((x + 1) * 48, (h + 1) * 128)
+                mm(s("P4", i * 128 + c - h * 128, i * 128 + e - h * 128), st(x),
+                   s("RB", i * 48 + c - x * 48, i * 48 + e - x * 48), True, True)
+                c = e
+        act(s("ABV", 384 * (h & 1), 384 * (h & 1) + 384), s("P4", 0, 384))
+
+    for h in range(NH):
+        w, par = h >> 1, h & 1
+        m0 = S0 + 16 * h
+        F = "FB" if par else "FA"
+        y0, n0 = 144 * par, 384 * par
+        Y = s("YS", y0, y0 + 128)
+        act(Y, s("OB", w * 256 + par, (w + 1) * 256, 2))
+        act(s("YS", y0 + 128, y0 + 144), s("EM", m0, m0 + 16))
+        for r in range(4):
+            mm(s("P1", r * 128, (r + 1) * 128), s("ID"), Y, True, True)
+        if h == 0:
+            chance(0)
+        r1, r2, k1 = (h + 1) * SL, h * SL, (h - 1) * SL
+        if par == 0:
+            s512, q512, l512 = s("RX", r2 + 12, r2 + 140), s("RX", r1 + 4, r1 + 132), s("RX", r1 + 3, r1 + 131)
+            if h:
+                ts(s("LU", (h + 1) * 16 + 8, (h + 2) * 16), s("RX", r1 + 132, r1 + 140), 1.0 / 512, mul)
+                A = names(s("LU", (h + 1) * 16 + 6, (h + 2) * 16), 1, par)
+            else:
+                cp(s("AB", 177, 337), ind(s("LK"), s("LU", 22, 32)))
+                tr(s("TT", 0, 128), s("AB", 208, 336))
+                tr(s("TT", 128, 288), s("AB", 192, 352))
+                ts(s("NL", 0, 128), ind(s("TT", 0, 288), s("PERM")), 1.0 / 256, mul, -0.498, add)
+                act(s("AB", 1, 161), ind(TBW, s("LU", 22, 32)))
+                A = s("AB", 32, 160)
+            ts(s("EQ0", 1, 128), s("RX", r1 + 4, r1 + 131), s("RX", r1 + 3, r1 + 4), ALU.is_equal, 4096.0, mul)
+            mm(s("P7", 0, 128), s("IDS"), l512, True, False)
+            mm(s("P7", 0, 128), s("ID"), s("CR", 144 * w + 7, 144 * w + 135), False, False)
+            mm(s("P7", 0, 128), st(15), s("EQ0"), False, True)
+            targets(h)
+        else:
+            s512, q512, l512 = s("RX", r2 + 4, r2 + 132), s("PK", k1 + 13, k1 + 141), s("PK", k1 + 12, k1 + 140)
+            A = names(s("PU", 8 * h - 8, 8 * h), 32, par)
+            cp(s("PK", k1 + 140, k1 + 141), s("RX", r1 + 12, r1 + 13))
+            if h < NH - 1:
+                ts(s("LU", (h + 1) * 16 + 8, (h + 2) * 16), s("RX", r1 + 4, r1 + 12), 1.0 / 512, mul)
+        for c in range(4):
+            gat(F, s("EM"), c, par)
+        tt(s("DD", 0, 128), A, s512, sub)
+        tt(s("DD", 128, 256), ind(TBW, s("LU", h * 16 + 8, h * 16 + 16)), q512, sub)
+        mm(s("P0"), s("ID"), s("ZERO"), True, False)
+        for r in range(4):
+            mm(s("P0", r * 128, (r + 1) * 128), s("ID32"), q512, False, False)
+        act(s("GT"), s("DD"), AF.Abs, bias=-256.0)
+        act(s("CL"), s("GT"), AF.Relu, bias=pc(0), scale=-1.0)
+        mm(s("P6", 0, 256), s("BO15"), s("CL"), True, True)
+        NM = s("P2", 128, 256)
+        act(s("NM", 0, 128), A, bias=2 * MAG)
+        act(NM, s("NM", 0, 128), bias=-2 * MAG)
+        tt(s("WT"), A, NM, sub)
+        tt(s("VM"), NM, s512, sub)
+        tt(s("P6", 0, 256), s("P6", 0, 256), s("ABV", n0, n0 + 256), mul)
+        ts(s("U2"), s("P6", 128, 256), 255.0, mn, 1535.502, add)
+        for r in range(4):
+            mm(s("P0", r * 128, (r + 1) * 128), s("ID"), s("U2"), False, r == 3)
+        tt(s("SVW"), s("WT"), s("P6", 0, 128), ALU.is_gt)
+        act(s("ND0"), s("WT"), AF.Relu, bias=-239.0)
+        act(s("ND"), s("ND0"), bias=-16.0)
+        mm(s("P6", 256, 384), s("DN"), A, True, False)
+        mm(s("P6", 256, 384), s("D0"), q512, False, True)
+        act(s("AQ", 0, 128), s("P6", 256, 384), bias=pc(12))
+        act(s("P2", 384, 512), s512, bias=float(1 - m0), scale=1.0 / 512)
+        mm(s("P3", 0, 128), s("ZX"), Y, True, False)
+        for c in range(4):
+            a, b = CH[c]
+            tt(s("PW", a * 128, b * 128), s(F, a * 128, b * 128), s("P1", 0, (b - a) * 128), mul)
+            for k in range(a, b):
+                mm(s("P3", 0, 128), s("ZS", 15 - k, 143 - k), s("PW", k * 128, (k + 1) * 128), False, k == 14)
+        mm(s("P2", 0, 128), s("ZS", 0, 128), s("K256"), True, False)
+        for c in range(4):
+            a, b = CH[c]
+            gat("CW", TBW, c, par, 34431.5)
+            tt(s("XW", a * 128, b * 128), s("CW", a * 128, b * 128), s("P0", 0, (b - a) * 128), sub)
+            if c == 0:
+                continue
+            a = 0 if c == 1 else a
+            ts(s("IW", a * 128, b * 128), s("XW", a * 128, b * 128), 33024.0, ALU.is_equal)
+            for k in range(a, b):
+                mm(s("P2", 0, 128), s("ZH", 15 - k, 143 - k), s("IW", k * 128, (k + 1) * 128), False, k == 14)
+        tt(s("SV"), s("SVW"), s("P2", 0, 128), mn)
+        tt(s("SE"), s("SV"), s("P3", 0, 128), mul)
+        mm(s("P7", 128, 256), s("BO32"), s("SE"), True, True)
+        mm(s("P7", 0, 128), s("TRI"), s("SE"), True, True)
+        act(s("ES"), s("P3", 0, 128))
+        mm(s("P3", 128, 256), s("IC1"), s("SV"), True, False)
+        mm(s("P3", 128, 256), s("IC2"), s("SV"), False, False)
+        mm(s("P3", 128, 256), s("ID32"), s("ES"), False, True)
+        gb = math.log(0.5 ** (3 - w))
+        act(s("P2", 256, 384), s("P3", 128, 256), AF.Exp, bias=gb, scale=1.0 / 4096)
+        GH, GL = s("GH", 128 * par, 128 * par + 128), s("GL", 128 * par, 128 * par + 128)
+        act(GH, s("P2", 256, 384))
+        tt(GL, s("P2", 256, 384), GH, sub)
+        tt(s("VC"), s("ABV", n0 + 256, n0 + 384), s("P7", 128, 256), mul)
+        tt(s("HIT"), s("P7", 0, 128), s("VC"), ALU.is_gt)
+        mm(s("P0", 0, 128), s("ASKM"), s("HIT"), True, True)
+        mm(s("P0", 128, 256), s("DIFX"), s("HIT"), True, False)
+        mm(s("P0", 128, 256), s("ZS", 0, 128), s("KM"), False, True)
+        mm(s("P0", 256, 384), s("DIF"), s("HIT"), True, True)
+        tt(s("ASK", 0, 128), s("P0", 0, 128), s("OF"), ALU.is_gt)
+        tt(s("XX"), s("VM"), s("P0", 128, 256), mul)
+        tt(s("NN", 0, 128), s("ND"), s("P0", 256, 384), mul)
+        l0, b0 = (248, 256) if par == 0 else (376, 248)
+        PL, PB = s("P7", l0, l0 + 8), s("P7", b0, b0 + 128)
+        mm(s("P7", 248, 512), s("ID"), s("ZP", 264 * par, 264 * par + 264), True, False)
+        mm(PB, s("BO"), s("XX"), False, False)
+        mm(s("P7", 384, 512), s("BO"), s("XX"), False, False)
+        for r in range(16):
+            mm(PL, s("ZS", 15 - r, 143 - r), s("XX", r, 128, 16), False, False)
+        scan(s("CUM", 1, 145), s("ASK"), s("K16"), add, mn)
+        act(s("JK"), s("CUM", 1, 145), AF.Sign, bias=pc(10), scale=-1.0, acc=s("IAC"))
+        mm(s("P1", 0, 128), s("ID"), s("CUM", 1, 129), True, False)
+        mm(s("P1", 0, 128), s("IDN"), s("CUM", 0, 128), False, True)
+        tt(s("ZZ"), s("CUM", 1, 129), s("P2", 384, 512), sub)
+        tt(s("YY"), s("ZZ"), s("P1", 0, 128), mul)
+        mm(PB, s("R0M"), s("YY"), False, False)
+        mm(s("P7", 384, 512), s("R0M"), s("YY"), False, False)
+        for r in range(16):
+            mm(PL, s("Z1", 15 - r, 143 - r), s("YY", r, 128, 16), False, r == 15)
+        k0 = h * SL
+        if h < NH - 1:
+            act(s("PK", k0 + 4, k0 + 140), s("P7", 248, 384), scale=512.0)
+            send(prv, nxt, s("RX", (h + 2) * SL + 4, (h + 2) * SL + 140), s("PK", k0 + 4, k0 + 140), "rx%d" % h)
+        if par == 0 or h == NH - 1:
+            cp(s("PU", 8 * h, 8 * h + 8), PL)
+        else:
+            cp(s("LU", (h + 2) * 16 + 6, (h + 2) * 16 + 8), s("P7", 382, 384))
+            act(s("RX", (h + 2) * SL + 3, (h + 2) * SL + 4), s("P7", 375, 376), scale=512.0)
+        IDX = s("IDX", 0, 1)
+        ts(IDX, s("IAC"), 0.5, mul, 72.0, add)
+        tt(s("G1"), ind(s("AB", 176 * par + 32, 176 * par + 176), IDX), s("CV", 16 * h, 16 * h + 16), sub)
+        act(s("EM", m0, m0 + 16), ind(s("YS", y0, y0 + 144), IDX))
+        tt(ind(s("NN"), IDX), s("G1"), s("BM"), mul)
+        tt(ind(s("TB"), s("OFU", 8 * par, 8 * par + 8)), A, s("NN", 0, 128), sub)
+        cp(s("AQ", 128, 144), s("TB", m0, m0 + 16))
+        cp(s("TB", m0, m0 + 16), ind(s("AQ"), IDX))
+        if par == 0:
+            mm(s("P7", 0, 128), s("IDS"), s("PK", k0 + 12, k0 + 140), True, False)
+            repeats("PK", k0 + 4, False)
+            targets(h + 1)
+        elif h < NH - 1:
+            repeats("PK", k0 + 132, True)
+            act(s("CS", 128 * w, 128 * w + 128), s("P7", 0, 128))
+            send(prv, nxt, s("CR", 144 * w + 152, 144 * w + 280), s("CS", 128 * w, 128 * w + 128), "cx%d" % w)
+        if h < NH - 1:
+            chance(h + 1)
+        for c in range(4):
+            bk = "P%d" % (4 + (c & 1))
+            for k in range(4 * c, 4 * c + 4):
+                o = s(bk, (k & 3) * 128, (k & 3) * 128 + 128)
+                mm(o, st(k), GH, True, False)
+                mm(o, st(k), GL, False, True)
+            a, b = CH[c]
+            tt(s("PR%d" % par, a * 128, b * 128), s(F, a * 128, b * 128), s(bk, 0, (b - a) * 128), mul)
+        act(s("PR%d" % par, 1920, 2048), s("P5", 384, 512), scale=s("XB"))
+        fold(h)
+    for par in range(2):
+        F = "FB" if par else "FA"
+        A = names(s("PU", 32 + 8 * par, 40 + 8 * par), 32, par)
+        for c in range(3):
+            gat(F, s("EM"), c, par)
+        cp(s(F, 1536, 1920), ind(s("EM"), s("NL", 128 * par + 96, 128 * par + 120)))
+        a0 = 128 * par
+        ts(s("NM", a0, a0 + 128), A, 2 * MAG, add, 2 * MAG, sub)
+        tt(s("WB", a0, a0 + 128), A, s("NM", a0, a0 + 128), sub)
+        for c in range(4):
+            bk = "P%d" % (6 * par + (c & 1))
+            mm(s(bk), s("BO"), s("KM8"), True, False)
+            for k in range(4 * c, 4 * c + 4):
+                mm(s(bk, (k & 3) * 128, (k & 3) * 128 + 128), st(k), s("WB", a0, a0 + 128), False, (k & 3) == 3)
+            tt(s("PZ", c * 512, (c + 1) * 512), s(F, c * 512, (c + 1) * 512), s(bk), mul)
+            for k in range(4 * c, 4 * c + 4):
+                mm(s("P%d" % (2 + par), 0, 128), s("ID128"), s(F, k * 128, (k + 1) * 128), k == 0, False)
+                mm(s("P%d" % (2 + par), 0, 128), s("ID"), s("PZ", k * 128, (k + 1) * 128), False, k == 15)
+        act(s("YA", par, 256, 2), s("AC", (4 + par) * 128, (5 + par) * 128))
+        act(s("YZ", par, 256, 2), s("P%d" % (2 + par), 0, 128))
+    dma("s", dr(T.ya[:]), s("YA"), "dya", 2000.0)
+    dma("s", dr(T.yz[:]), s("YZ"), "dyz", 2000.0)
+
+    ops = schedule(ops)
+    deps = depends(ops, True)
+    clock = {q: {} for q in "vapgsx"}
+    at, waits, need = [], [], set()
+    for i, o in enumerate(ops):
+        ck = clock[o[0]]
+        ws = []
+        for j in sorted(deps[i], reverse=True):
+            key = ops[j][0] if ops[j][4] is None else ops[j][4][0]
+            if ck.get(key, -1) >= j:
+                continue
+            ws.append(j)
+            need.add(j)
+            ck[key] = j
+            for k2, v2 in at[j].items():
+                if ck.get(k2, -1) < v2:
+                    ck[k2] = v2
+        waits.append(ws)
+        at.append(dict(ck) if o[0] != "x" else {})
+    eng = {"v": g.vector, "a": g.scalar, "p": g.tensor, "g": g, "s": g.sync}
+    cnt = {q: 0 for q in "vapg"}
+    val, top = {}, {}
+    for i, o in enumerate(ops):
+        q, tok = o[0], o[4]
+        if tok is not None:
+            val[i] = tok
+            top[tok[0]] = tok[1]
+        if q == "x":
+            continue
+        for j in waits[i]:
+            eng[q].wait_ge(T.sem[val[j][0]], val[j][1])
+        ins = o[1]()
+        if tok is None and i in need:
+            cnt[q] += 1
+            ins.then_inc(T.sem["q" + q], 1)
+            val[i] = ("q" + q, cnt[q])
+    top["loc"] = nloc[0]
+    for q in "vapg":
+        top["q" + q] = cnt[q]
+    for n in top:
+        if top[n] and n not in ("dya", "dyz"):
+            g.wait_ge(T.sem[n], top[n])
+    g.wait_ge(T.sem.dya, 16)
+    g.wait_ge(T.sem.dyz, 16)

@@ -4,29 +4,28 @@ from concourse.mybir import AluOpType as ALU, ActivationFunctionType as AF
 
 F32, BF, F16, I32, U16 = "float32", "bfloat16", "float16", "int32", "uint16"
 H, S0, NH = 2048, 1952, 6
-SL = 144
+SL = 160
 SB = {
-    "LK": (2048, I32), "TB": (2304, F32), "EM": (2048, BF), "OB": (768, BF), "XB": (1, F32),
-    "PEPO": (16, I32), "POX": (8, I32), "RN": (144, I32), "RB": (144, BF), "L16": (18, F16),
-    "RX": (7 * SL, F32), "PK": (6 * SL, F32), "LU": (7 * 16, U16), "PU": (48, U16), "CR": (432, BF), "CS": (256, BF), "EQ0": (128, BF),
-    "AB": (352, F32), "TT": (576, F32), "NL": (256, U16), "PERM": (8, U16),
+    "LK": (2048, I32), "TB": (2320, F32), "EM": (2048, BF), "OB": (768, BF), "XB": (1, F32),
+    "PEPO": (16, I32), "RN": (384, I32), "RB": (384, BF), "L16": (18, F16), "INI": (256, F16),
+    "RX": (5 * SL, F16), "PK": (6 * SL, F16), "LU": (7 * 16, U16), "PU": (48, U16), "CR": (432, BF), "CS": (256, BF),
+    "EQ0": (128, BF), "KB": (7 * 16, F32), "AB": (352, F32), "DG": (128, F32), "TT": (576, F32), "NL": (256, U16), "PERM": (8, U16),
     "FA": (2048, BF), "FB": (2048, BF), "CW": (2048, F32), "XW": (2048, BF), "IW": (2048, BF), "PW": (2048, BF),
     "PR0": (2048, F32), "PR1": (2048, F32), "PZ": (2048, F16), "HB": (768, F32), "AC": (768, F32),
-    "DD": (256, BF), "CL": (256, BF), "GT": (256, BF), "U2": (128, F16), "NM": (256, F32),
-    "WT": (128, F32), "WB": (256, BF), "SVW": (128, F32), "ND": (128, F32), "ND0": (128, F32),
-    "VM": (128, F32), "AQ": (144, F32), "YS": (288, BF), "ABV": (768, F32), "EA": (704, BF), "EQ": (704, BF),
-    "OF": (128, F16), "OFU": (16, U16), "SV": (128, BF), "SE": (128, F32), "GH": (256, BF),
-    "GL": (256, BF), "VC": (128, F32), "HIT": (128, BF), "ASK": (144, BF), "CUM": (145, BF),
-    "ZZ": (128, F32), "XX": (128, F16), "YY": (128, F16), "NN": (144, F32), "JK": (144, BF), "IAC": (1, F32),
-    "IDX": (2, U16), "G1": (16, F32), "YA": (256, F32), "YZ": (256, F32),
-    "PI": (8, I32), "PC": (16, F32), "RM": (16, F32), "BM": (16, F32), "COLG": (128, F32), "COLK": (128, F32),
-    "DUM": (128, F32), "CV": (96, F32), "C2": (8, F32), "POSK": (8, F32), "T0": (128, F32), "T1": (128, F32),
-    "T2": (128, F32), "BO": (128, BF), "BO32": (128, F32), "BO15": (128, BF), "IDS": (128, F32), "BO4": (128, BF),
-    "ES": (128, F32), "ZS": (143, BF), "ZH": (143, BF), "Z1": (143, BF), "ZX": (128, BF), "TRI": (128, F32),
-    "DIF": (128, BF), "DIFX": (128, BF), "ASKM": (128, BF), "ID": (128, BF), "IDN": (128, BF), "ID32": (128, F32),
-    "ID128": (128, BF), "IC1": (128, BF), "IC2": (128, BF), "DN": (128, F32), "D0": (128, F32), "ST": (2048, BF),
-    "ZERO": (512, BF), "ZP": (528, BF), "POSB": (128, BF), "K256": (128, BF), "KM": (128, BF),
-    "K16": (144, BF), "KM8": (512, BF), "R0M": (128, BF),
+    "CL": (256, BF), "GT": (256, BF), "CB": (256, F32), "U2": (128, F16), "NM": (128, F32),
+    "WT": (128, BF), "WB": (256, BF), "SG": (128, BF), "ND": (128, BF), "AQ": (144, F32), "YS": (6 * 144, BF),
+    "EA": (704, BF), "EQ": (704, BF), "OF": (128, F16), "OFU": (16, U16), "SV": (128, BF), "SE": (128, F32), "SW": (128, F32),
+    "GS": (128, F32), "ES": (128, F32), "GH": (256, BF), "GL": (256, BF), "HIT": (128, BF), "ASK": (144, BF), "CUM": (145, BF), "BN": (128, BF),
+    "ZZ": (128, F32), "XX": (128, F16), "YY": (128, F16), "NN": (144, F32), "JK": (144, BF), "IAC": (2, F32),
+    "IDX": (4, U16), "G1": (16, F32), "YA": (256, F32), "YZ": (256, F32),
+    "PI": (8, I32), "PC": (24, F32), "RM": (16, F32), "BM": (16, F32), "COLG": (128, F32), "COLK": (16, F32),
+    "DUM": (128, F32), "CV": (96, F32), "C2": (8, F32), "BO": (128, BF), "BO32": (128, F32), "BO4": (128, BF),
+    "ZS": (143, BF), "Z1": (143, BF), "ZX": (128, BF), "TRI": (128, F32), "DIF": (128, BF), "DT": (128, BF), "DT32": (128, F32),
+    "DTN": (128, BF), "L14": (128, BF), "S2K": (128, BF), "XBN": (128, BF), "ZH": (143, BF), "D16": (128, BF),
+    "IS1": (128, BF), "IS2": (128, BF), "ID2K": (128, BF), "IDB": (128, BF), "NZ": (128, BF), "E1": (128, F32), "EV": (128, F32),
+    "G2": (16, F32), "ID": (128, BF), "IDN": (128, BF), "IDM": (128, BF), "ID32": (128, F32),
+    "ID128": (128, BF), "IC1": (128, BF), "IC2": (128, BF), "DN": (128, F32), "D0": (128, BF), "ST": (2048, BF), "SEL": (768, BF),
+    "ZB": (144, BF), "Z32": (128, F32), "ZP": (272, BF), "POSB": (128, BF), "K16": (144, BF), "KT": (128, BF),
 }
 SCRATCH = {n: ("sbuf", [128, w], d) for n, (w, d) in SB.items()}
 for _b in range(8):
@@ -34,7 +33,10 @@ for _b in range(8):
 DMAS = ["dpo", "dpe", "dl0", "dl1", "dl2", "dl3", "dem", "dob", "dn0", "dn1", "dn2", "dxb", "dya", "dyz"]
 SEMAPHORES = (["qv", "qa", "qp", "qg", "loc", "pox", "ob1", "ob2", "fl0", "fl1", "cx0", "cx1"] + DMAS + ["rx%d" % h for h in range(5)]
               + ["fa%d" % h for h in range(NH)] + ["fb%d" % h for h in range(NH)])
-CYC, PEC, FIX, GAT, SCA, HOP, REM = 1.0, 0.5, 60.0, 1.56, 3.8, 70.0, 2500.0
+CYC, PEC, FIXV, FIXA, GAT, SCA, HOP, REM = 0.88, 0.44, 25.0, 25.0, 1.56, 3.8, 200.0, 2000.0
+OPT = {"born": "v", "gl": "v", "nm": "v", "ag": "a", "tbm": "a", "chf": [(0, 4), (4, 8), (8, 12), (12, 15)],
+       "chc": [(0, 4), (4, 8), (8, 12), (12, 14), (14, 15)], "stv": 8, "cl": "v",
+       "chg": [(0, 2), (2, 4), (4, 6), (6, 8), (8, 10), (10, 12), (12, 14), (14, 15)], "gorder": "ffcfccfcc"}
 
 
 def bits(engines):
@@ -51,12 +53,11 @@ def helper_of(c, T, topo):
 def helper_program(g, core, owner, T, topo):
     rid, pid = topo.addr(owner, core)
     eng = topo.engines(core, owner)
-    eng = eng[len(eng) // 2:]
     for h in range(NH):
-        g.wait_ge(T.sem["fa%d" % h], len(eng))
+        g.wait_ge(T.sem["fa%d" % h], len(eng) if h == NH - 1 else len(eng) // 2)
         g.remote_dma(T.AC[:, h * 128:(h + 1) * 128], T.HB[:, h * 128:(h + 1) * 128], T.sem["fb%d" % h], T.sem.loc,
-                     pid, rid, bits(eng))
-    g.wait_ge(T.sem.loc, NH * len(eng))
+                     pid, rid, bits(eng[len(eng) // 2:]))
+    g.wait_ge(T.sem.loc, NH * (len(eng) // 2))
 
 
 def hit(x, y):
@@ -112,11 +113,14 @@ def schedule(ops):
             suc[j].append(i)
     pb = [set(r[0] for r in o[2] + o[3] if SCRATCH[r[0]][0] == "psum") for o in ops]
 
+    def gap(i, k):
+        return -ops[i][6] if ops[k][0] == "p" == ops[i][0] else HOP
+
     def chains(order, mix):
         pri, nxt = [0.0] * n, {}
         for i in reversed(order):
             q = ops[i][0]
-            p = ops[i][6] + max([pri[k] + (0 if ops[k][0] == "p" == q else HOP) for k in suc[i]] + [0.0])
+            p = ops[i][6] + max([pri[k] + gap(i, k) for k in suc[i]] + [0.0])
             if q in nxt and q != "x":
                 p = max(p, (1 - mix) * p + mix * pri[nxt[q]])
             pri[i] = ops[i][5] + p
@@ -125,33 +129,35 @@ def schedule(ops):
 
     def run(pri, slack):
         left = [len(d) for d in deps]
-        ready = [i for i in range(n) if not left[i]]
+        ready = {}
+        for i in range(n):
+            if not left[i]:
+                ready.setdefault(ops[i][0], []).append(i)
         fin, free, bank, order, base = [0.0] * n, {}, {}, [], [0.0] * n
-        while ready:
+        while len(order) < n:
             est = {}
-            for i in ready:
-                q = ops[i][0]
-                t = max(base[i], free.get(q, 0.0) if q != "x" else 0.0)
-                for b in pb[i]:
-                    for q2, f in bank.get(b, {}).items():
-                        if q2 != q:
-                            t = max(t, f + HOP)
-                est[i] = t
-            i0 = min(ready, key=lambda i: (est[i], -pri[i], i))
+            for q in ready:
+                for i in ready[q]:
+                    t = max(base[i], free.get(q, 0.0) if q != "x" else 0.0)
+                    for b in pb[i]:
+                        for q2, f in bank.get(b, {}).items():
+                            if q2 != q:
+                                t = max(t, f + HOP)
+                    est[i] = t
+            i0 = min(est, key=lambda i: (est[i], -pri[i], i))
             q = ops[i0][0]
-            i = max([k for k in ready if ops[k][0] == q and est[k] <= est[i0] + min(slack, ops[i0][5])],
-                    key=lambda k: (pri[k], -k))
-            ready.remove(i)
+            i = max([k for k in ready[q] if est[k] <= est[i0] + min(slack, ops[i0][5])], key=lambda k: (pri[k], -k))
+            ready[q].remove(i)
             order.append(i)
             free[q] = est[i] + ops[i][5]
             fin[i] = free[q] + ops[i][6]
             for b in pb[i]:
                 bank.setdefault(b, {})[q] = fin[i]
             for k in suc[i]:
-                base[k] = max(base[k], fin[i] + (0 if ops[k][0] == "p" == q else HOP))
+                base[k] = max(base[k], fin[i] + gap(i, k))
                 left[k] -= 1
                 if not left[k]:
-                    ready.append(k)
+                    ready.setdefault(ops[k][0], []).append(k)
         return max(fin), order
 
     if not ORDER:
@@ -168,9 +174,102 @@ def schedule(ops):
     return [ops[i] for i in ORDER[0][1]]
 
 
+def schedule(ops, turn):
+    if ORDER:
+        return [ops[i] for i in ORDER[0][1]]
+    n = len(ops)
+    deps = depends(ops, False)
+    for i in range(n):
+        if ops[i][7] is not None:
+            deps[i].add(ops[i][7])
+    suc = [[] for _ in range(n)]
+    for i in range(n):
+        for j in deps[i]:
+            suc[j].append(i)
+    use = []
+    for o in ops:
+        u = [] if o[0] == "x" else [(o[0], o[5])]
+        if o[0] in "va":
+            u += [(b, o[5] + HOP) for b in set(r[0] for r in o[2] + o[3] if SCRATCH[r[0]][0] == "psum")]
+        use.append(u)
+
+    def lag(i, k):
+        return ops[i][5] + (0.0 if ops[k][0] == "p" == ops[i][0] else ops[i][6] + HOP)
+
+    def place(key, back):
+        before, after = (suc, deps) if back else (deps, suc)
+        left = [len(b) for b in before]
+        ready = sorted((key[i], i) for i in range(n) if not left[i])
+        t, held = [0.0] * n, {}
+        while ready:
+            i = ready.pop(0)[1]
+            if back:
+                x = max([t[k] + lag(i, k) for k in before[i]] + [ops[i][5] + ops[i][6]]) - ops[i][5]
+            else:
+                x = max([t[j] + lag(j, i) for j in before[i]] + [0.0])
+            moved = True
+            while moved:
+                moved = False
+                for r, d in use[i]:
+                    a0 = x - (d - ops[i][5]) if back else x
+                    lst = held.setdefault(r, [])
+                    lo, hi = 0, len(lst)
+                    while lo < hi:
+                        m = (lo + hi) // 2
+                        if lst[m][1] <= a0 + 1e-6:
+                            lo = m + 1
+                        else:
+                            hi = m
+                    a = a0
+                    while lo < len(lst) and lst[lo][0] < a + d - 1e-6:
+                        if lst[lo][2] != ops[i][0] or r == ops[i][0]:
+                            a = max(a, lst[lo][1])
+                        lo += 1
+                    if a > a0:
+                        x += a - a0
+                        moved = True
+            for r, d in use[i]:
+                a = x - (d - ops[i][5]) if back else x
+                lst = held[r]
+                m = len(lst)
+                while m and lst[m - 1][:2] > (a, a + d):
+                    m -= 1
+                lst.insert(m, (a, a + d, ops[i][0]))
+            t[i] = x + ops[i][5] if back else x
+            for k in after[i]:
+                left[k] -= 1
+                if not left[k]:
+                    e, lo, hi = (key[k], k), 0, len(ready)
+                    while lo < hi:
+                        m = (lo + hi) // 2
+                        if ready[m] < e:
+                            lo = m + 1
+                        else:
+                            hi = m
+                    ready.insert(lo, e)
+        return t
+
+    chain = [0.0] * n
+    for i in reversed(range(n)):
+        chain[i] = max([chain[k] + lag(i, k) for k in suc[i]] + [ops[i][5] + ops[i][6]])
+    key = list(turn)
+    for i in reversed(range(n)):
+        key[i] = min([key[i]] + [key[k] for k in suc[i]])
+    key, best = [(key[i], -chain[i]) for i in range(n)], None
+    for it in range(ROUNDS):
+        t = place(key, False)
+        end = max(t[i] + ops[i][5] + ops[i][6] for i in range(n))
+        if best is None or end < best[0]:
+            best = (end, sorted(range(n), key=lambda i: (t[i], i)), it)
+        key = [-x for x in place([-(t[i] + ops[i][5]) for i in range(n)], True)]
+    ORDER.append(best)
+    return [ops[i] for i in best[1]]
+
+
 ORDER = []
-TRY = [(100.0, 0.5), (300.0, 0.5), (300.0, 0.9), (600.0, 0.9)]
-ROUNDS = 8
+ROUNDS = 4
+STEP = {"names": 0, "d": 1, "f0": 2, "fit": 3, "f1": 4, "slice": 5, "gather": 6, "test": 7, "side": 8, "first": 8.5, "draw": 9,
+        "g": 9.5, "repeats": 100.5, "sums": 107.5, "hit": 9.1, "kb": 101.5, "list": 8.5, "const": 50, "late": 90}
 
 
 def rank_program(g, core, T, topo):
@@ -181,11 +280,12 @@ def rank_program(g, core, T, topo):
                 helper_program(g, core, c, T, topo)
         return
     N = len(T.cores)
+    turn, now = [], [0]
     ops = []
 
-    def s(n, a=0, b=None, st=1):
+    def s(n, a=0, b=None, st=1, rows=128):
         b = SCRATCH[n][1][1] if b is None else b
-        return (T[n][:, a:b] if st == 1 else T[n][:, a:b:st], [(n, a, b)], [], len(range(a, b, st)))
+        return (T[n][0:rows, a:b] if st == 1 else T[n][0:rows, a:b:st], [(n, a, b)], [], len(range(a, b, st)))
 
     def ind(w, o):
         return (w[0].indirect(o[0]), w[1], o[1], 16 * o[3])
@@ -199,17 +299,21 @@ def rank_program(g, core, T, topo):
             wr += x[1]
             rd += x[2]
         ops.append((q, fn, rd, wr, tok, c, lat, aft))
+        turn.append(now[0])
         return len(ops) - 1
+
+    def at(h, step):
+        now[0] = 100 * h + STEP[step]
 
     def v(x):
         return x[0] if isinstance(x, tuple) else x
 
-    def cost(o, a, f=1.0):
+    def cost(o, a, f=1.0, fix=FIXV):
         if o[2]:
-            return FIX + o[3] * SCA * CYC
+            return fix + o[3] * SCA * CYC
         if a[2]:
-            return FIX + o[3] * GAT * CYC
-        return FIX + max(64, o[3] * f) * CYC
+            return fix + o[3] * GAT * CYC
+        return fix + max(64, o[3] * f) * CYC
 
     def half(*x):
         return 0.5 if all(SCRATCH[y[1][0][0]][2] in (BF, F16, U16) for y in x) else 1.0
@@ -237,43 +341,60 @@ def rank_program(g, core, T, topo):
     def scan(o, a, b, op0, op1):
         rec("v", lambda: g.vector.tensor_tensor_scan(o[0], a[0], b[0], 0.0, op0, op1), [o], [a, b], cost(o, a, half(o, a, b)))
 
-    def act(o, a, f=AF.Identity, bias=0.0, scale=1.0, acc=None):
+    def act(o, a, f=AF.Identity, bias=0.0, scale=1.0, acc=None, more=0.0, aft=None):
         if acc is None:
-            rec("a", lambda: g.scalar.activation(o[0], a[0], f, v(bias), v(scale)), [o], [a, bias, scale], cost(o, a))
+            return rec("a", lambda: g.scalar.activation(o[0], a[0], f, v(bias), v(scale)), [o], [a, bias, scale],
+                       cost(o, a, 1.0, FIXA) + more, None, 0.0, aft)
         else:
             rec("a", lambda: g.scalar.activation(o[0], a[0], f, v(bias), v(scale), accum_out=acc[0]), [o, acc],
-                [a, bias, scale], cost(o, a))
+                [a, bias, scale], cost(o, a, 1.0, FIXA) + 20)
+
+    def mv(q, o, a):
+        (act if q == "a" else cp)(o, a)
 
     def mm(o, l, r, st, sp):
         rec("p", lambda: g.tensor.matmul(o[0], l[0], r[0], st, sp), [o], [l, r],
-            max(64, r[3]) * PEC * (4 if SCRATCH[r[1][0][0]][2] == F32 else 1))
+            max(64, r[3]) * PEC * (4 if SCRATCH[r[1][0][0]][2] == F32 else 1), None, 60.0)
+
+    def group(o, pairs):
+        for i, (l, r) in enumerate(pairs):
+            mm(o, l, r, i == 0, i == len(pairs) - 1)
 
     def iota(o, pat, base, cm, fl=True):
         if fl:
-            rec("g", lambda: g.iota(o[0], pat, base, cm, allow_small_or_imprecise_dtypes=True), [o], [], 130 + 2 * o[3])
+            rec("g", lambda: g.iota(o[0], pat, base, cm, allow_small_or_imprecise_dtypes=True), [o], [], 130 + 2 * CYC * o[3])
         else:
-            rec("g", lambda: g.iota(o[0], pat, base, cm), [o], [], 130 + 2 * o[3])
+            rec("g", lambda: g.iota(o[0], pat, base, cm), [o], [], 130 + 2 * CYC * o[3])
 
-    def dma(q, o, a, sem, lat, **kw):
+    def sel(o, a, pat, op, fill, base, cm, more=()):
+        rec("g", lambda: g.affine_select(o[0], a[0], pat, op, fill, base, cm), [o], [a] + list(more), 170 + 2 * CYC * o[3])
+
+    def gcopy(o, a):
+        sel(o, a, [[0, o[3]]], ALU.is_ge, 0.0, 0, 0)
+
+    def diag(o, a, c, off=0):
+        sel(o, a, [[-1, 128]], ALU.not_equal, c, -off, 1)
+
+    def dma(q, o, a, sem, lat, c=80.0, **kw):
         e = {"s": g.sync, "a": g.scalar, "g": g}[q]
-        rec(q, lambda: e.dma_start(o[0], a[0], **kw).then_inc(T.sem[sem], 16), [o], [a], 100.0, (sem, 16), lat)
+        rec(q, lambda: e.dma_start(o[0], a[0], **kw).then_inc(T.sem[sem], 16), [o], [a], c, (sem, 16), lat)
 
     nloc = [0]
 
-    def send(dst, src, o, a, sem):
+    def send(dst, src, o, a, sem, c=300.0):
         rid, pid = topo.addr(dst, core)
         eng = topo.engines(core, dst)[:8]
         nloc[0] += len(eng)
-        i = rec("g", lambda: g.remote_dma(o[0], a[0], T.sem[sem], T.sem.loc, pid, rid, bits(eng)), [], [a], 300.0, ("loc", 0))
+        i = rec("g", lambda: g.remote_dma(o[0], a[0], T.sem[sem], T.sem.loc, pid, rid, bits(eng)), [], [a], c, ("loc", 0))
         rec("x", None, [o], [], 0.0, (sem, len(topo.engines(src, core)[:8])), REM, i)
 
     prv, nxt = T.cores[(rank - 1) % N], T.cores[(rank + 1) % N]
     hlp = helper_of(core, T, topo)
-    heng = topo.engines(core, hlp)
-    heng = heng[len(heng) // 2:]
+    hall = topo.engines(core, hlp)
     nfold = [0, 0]
 
     def fold(h):
+        heng = hall if h == NH - 1 else hall[len(hall) // 2:]
         pr = "PR%d" % (h & 1)
         src = [s(pr, k * 128, (k + 1) * 128) for k in range(16)]
         if h >= 2:
@@ -283,33 +404,22 @@ def rank_program(g, core, T, topo):
         t = RemoteDMATransfer(dst_ids=[DstId(rid=rid, pnc=pid)], dma_engine_mask=bits(heng), remote_sem=T.sem["fa%d" % h],
                               srcs=[x[0] for x in src], dsts=[T.HB[:, h * 128:(h + 1) * 128]], alu_op=1)
         i = rec("g", lambda: g.remote_dma_fused([t], local_sem=T.sem["fl%d" % (h & 1)]), [], src, 300.0,
-                ("fl%d" % (h & 1), nfold[h & 1]), 3500.0)
-        rec("x", None, [s("AC", h * 128, (h + 1) * 128)], [], 0.0, ("fb%d" % h, len(heng)), REM, i)
+                ("fl%d" % (h & 1), nfold[h & 1]), 5000.0)
+        rec("x", None, [s("AC", h * 128, (h + 1) * 128)], [], 0.0, ("fb%d" % h, len(hall) // 2), 2500.0, i)
 
     def dr(t):
         return (t, [], [], 0)
 
     add, sub, mul, mx, mn = ALU.add, ALU.subtract, ALU.mult, ALU.max, ALU.min
-    dma("s", s("PEPO", 8, 16), dr(T.po[:]), "dpo", 2000.0)
+    MAG, MG1 = 1.5 * 2.0 ** 31, 1.5 * 2.0 ** 23
+    dma("s", s("PEPO", 8, 16), dr(T.po[:]), "dpo", 1900.0)
     for c in range(4):
-        dma("s", s("LK", c * 512, (c + 1) * 512), dr(T.lk[:, c * 512:(c + 1) * 512]), "dl%d" % c, 2400.0 + 450 * c)
-    dma("s", s("EM"), dr(T.em[:]), "dem", 4500.0)
-    dma("a", s("PEPO", 0, 8), dr(T.pe[:]), "dpe", 2000.0)
-    dma("a", s("OB", 0, 256), dr(T.ob[:]), "dob", 2500.0)
-    for i, t in enumerate((T.nua, T.nub, T.vd)):
-        dma("a", s("RN", i * 48, (i + 1) * 48), dr(t[:]), "dn%d" % i, 2500.0)
-    iota(s("PI", 0, 1), [[0, 1]], 0, 1, False)
-    iota(s("COLG"), [[1, 8], [0, 16]], 0, 0)
-    iota(s("COLK"), [[0, 8], [1, 16]], 0, 0)
-    prv, nxt = T.cores[(rank - 1) % N], T.cores[(rank + 1) % N]
-    send(nxt, prv, s("POX"), s("PEPO", 8, 16), "pox")
-    iota(s("C2"), [[2, 8]], 0, 0)
-    dma("g", s("XB"), dr(T.xb[:]), "dxb", 3000.0, allow_slow_non_contiguous=True)
-    iota(s("POSB"), [[2, 128]], -128, 0)
-    iota(s("DUM"), [[2, 128]], H, 0)
-    iota(s("CV"), [[512, 96]], 512 * S0 + 128, 0)
-    for w in (1, 2):
-        send(T.cores[(rank - w) % N], T.cores[(rank + w) % N], s("OB", w * 256, (w + 1) * 256), s("OB", 0, 256), "ob%d" % w)
+        dma("s", s("LK", c * 512, (c + 1) * 512), dr(T.lk[:, c * 512:(c + 1) * 512]), "dl%d" % c, 2200.0 + 400 * c)
+    dma("s", s("EM"), dr(T.em[:]), "dem", 4300.0)
+    dma("a", s("PEPO", 0, 8), dr(T.pe[:]), "dpe", 1900.0)
+    dma("s", s("OB", 0, 256), dr(T.ob[:]), "dob", 4400.0)
+    for i, t in enumerate((T.nub, T.nua, T.vd)):
+        dma("s", s("RN", i * 128, (i + 1) * 128, rows=48), dr(t[:]), "dn%d" % i, 4500.0)
 
     def pc(i):
         return s("PC", i, i + 1)
@@ -320,8 +430,23 @@ def rank_program(g, core, T, topo):
     def st(k):
         return s("ST", k * 128, (k + 1) * 128)
 
-    for n in ("ZS", "AB", "ZP", "ZERO"):
+    at(0, "const")
+    ZB, ID, ID32, IDN, IDM, BO = s("ZB", 0, 128), s("ID"), s("ID32"), s("IDN"), s("IDM"), s("BO")
+    for n in ("ZB", "Z32", "ZS", "Z1", "AB", "ZP"):
         ms(s(n), 0.0)
+    act(s("K16"), s("ZB"), AF.Exp, bias=math.log(16.0), more=1300.0)
+    iota(s("PI", 0, 1), [[0, 1]], 0, 1, False)
+    iota(s("COLG"), [[1, 8], [0, 16]], 0, 0)
+    iota(s("COLK"), [[1, 16]], 0, 0)
+    iota(s("C2"), [[2, 8]], 0, 0)
+    cp(s("LU", 24, 32), s("PEPO", 8, 16))
+    send(nxt, prv, s("LU", 16, 24), s("LU", 24, 32), "pox", 1300.0)
+    cp(s("LU", 8, 16), s("PEPO", 0, 8))
+    cp(s("L16", 0, 16), s("PEPO"))
+    diag(ID32, s("Z32"), 1.0)
+    for n, c in (("IDM", -512.0), ("ID", 1.0), ("IDN", -1.0), ("ID128", 128.0), ("IC1", 2832.0), ("IC2", 7.125),
+                 ("IS1", -3456.0), ("IS2", -11.5625), ("ID2K", 2048.0), ("IDB", 65536.0)):
+        diag(s(n), ZB, c)
     p0 = s("PI", 0, 1)
     ts(s("PI", 1, 2), p0, 15, ALU.bitwise_and)
     ts(s("PI", 2, 3), p0, 4, ALU.arith_shift_right)
@@ -330,310 +455,365 @@ def rank_program(g, core, T, topo):
     tt(s("PI", 5, 6), p0, s("PI", 2, 3), add)
     ts(s("PI", 6, 7), s("PI", 5, 6), 1, ALU.bitwise_and)
     cp(s("PC", 0, 7), s("PI", 0, 7))
-    ts(s("BO"), s("COLG"), pc(2), ALU.is_equal)
-    ts(s("RM"), s("COLK", 0, 16), pc(1), ALU.is_equal)
+    ts(BO, s("COLG"), pc(2), ALU.is_equal)
+    ts(s("RM"), s("COLK"), pc(1), ALU.is_equal)
     for k in range(16):
-        act(st(k), s("BO"), scale=rm(k))
+        if k < OPT["stv"]:
+            ts(st(k), BO, rm(k), mul)
+        else:
+            act(st(k), BO, scale=rm(k))
     ts(pc(7), pc(6), 144.0, mul, pc(4), add)
     ts(pc(8), pc(3), 16.0, mul, pc(7), add)
     ts(s("PERM"), s("C2"), pc(8), add)
-    cp(s("ZS", 15, 143, 16), s("BO", 0, 128, 16))
-    ts(pc(9), pc(1), 15.0, ALU.is_lt)
-    ts(pc(10), pc(1), 0.5, add)
-    ts(pc(11), pc(1), 0.0, ALU.is_gt)
-    ts(pc(12), rm(0), 128.0, mul)
-    tt(pc(13), rm(15), rm(14), sub)
-    ts(pc(14), pc(1), 2.0, mul)
-    ms(pc(15), 128.0)
-    ts(s("POSK"), s("C2"), 16.0, mul, pc(14), add)
-    ts(s("ZP", 0, 8), s("POSK"), 1.0 / 512, mul)
-    ts(s("ZP", 392, 400), s("POSK"), 1.0 / 512, mul)
-    for a in (136, 400):
-        act(s("ZP", a, a + 128), s("POSB"), scale=1.0 / 512)
+    ts(pc(9), rm(15), 2.0 ** 20, mul, -MAG, add)
+    act(pc(10), pc(1), bias=0.5)
+    act(pc(11), rm(0), bias=1.0, scale=-1.0)
+    act(pc(12), rm(0), scale=128.0)
+    act(pc(13), pc(1), bias=128.0)
+    act(pc(20), rm(15), bias=1.0, scale=-1.0)
+    act(pc(21), rm(15), bias=-1.0)
+    act(pc(14), rm(15), bias=-16.0, scale=16.0)
+    act(pc(15), pc(1), bias=31.0, scale=16.0)
+    act(pc(16), rm(15), bias=pc(15), scale=1649.0)
+    act(pc(17), pc(1), scale=1.0 / 256)
+    act(pc(18), rm(0), scale=512.0)
+    act(pc(19), rm(14), scale=-1.0)
+    for a in (0, 136):
+        act(s("ZP", a, a + 8), s("C2"), bias=pc(17), scale=1.0 / 32)
+    iota(s("POSB"), [[2, 128]], -128, 0)
+    ts(s("ZP", 144, 272), s("POSB"), 1.0 / 512, mul)
     for a in (0, 144, 288):
         ms(s("CR", a, a + 8), 0.0)
-    ms(s("EQ0", 0, 1), 0.0)
-    cp(s("LU", 8, 16), s("PEPO", 0, 8))
-    cp(s("LU", 24, 32), s("PEPO", 8, 16))
-    cp(s("L16", 0, 16), s("PEPO"))
-    ts(s("T2", 0, 8), s("PEPO", 8, 16), 512.0, mul)
-    tt(s("RX", SL + 132, SL + 140), s("T2", 0, 8), s("POSK"), add)
-    MAG = 1.5 * 2.0 ** 31
     for c in range(4):
         a, b = c * 512, (c + 1) * 512
         ts(s("CW", a, b), s("LK", a, b), -128.0, add, MAG, add)
-        act(s("P%d" % (2 + (c & 1))), s("CW", a, b), bias=-MAG)
-        tt(s("TB", a, b), s("LK", a, b), s("P%d" % (2 + (c & 1))), add)
-    act(s("BO15"), s("BO"), scale=pc(9))
-    ms(pc(0), 256.0)
-    ts(s("T0"), s("COLK"), pc(1), sub)
-    ts(s("T1"), s("T0"), 0.0, ALU.is_equal)
-    tt(s("ID32"), s("T1"), s("BO"), mul)
+        act(s("P%d" % (4 + (c & 1))), s("CW", a, b), bias=pc(9))
+        tt(s("TB", a, b), s("LK", a, b), s("P%d" % (4 + (c & 1))), add)
     for r in range(16):
-        mm(s("P7", r, 256, 16), st(r), s("L16", 0, 16), True, True)
-    act(s("RX", 12, 140), s("P7", 0, 128), scale=512.0)
-    act(s("RX", SL + 4, SL + 132), s("P7", 128, 256), scale=512.0)
-    cp(s("LU", 22, 24), s("POX", 6, 8))
-    cp(s("L16", 16, 18), s("POX", 6, 8))
-    mm(s("P7", 256, 258), st(15), s("L16", 16, 18), True, True)
-    act(s("RX", SL + 3, SL + 4), s("P7", 257, 258), scale=512.0)
-    ts(s("RB"), s("RN"), 1.0 / 256, mul)
-    cp(s("ID"), s("ID32"))
+        mm(s("P6", r, 256, 16), st(r), s("L16", 0, 16), True, True)
+    cp(s("INI"), s("P6", 0, 256))
+    cp(s("L16", 16, 18), s("LU", 22, 24))
+    for i, c in enumerate((1.0, -1.0, -1.0) if OPT["cl"] == "a" else (-1.0, 1.0, -1.0)):
+        ts(s("RB", i * 128, (i + 1) * 128, rows=48), s("RN", i * 128, (i + 1) * 128, rows=48), c / 256, mul)
+    dma("g", s("XB"), dr(T.xb[:]), "dxb", 2500.0, 1000.0, allow_slow_non_contiguous=True)
+    gcopy(s("ZS", 15, 143, 16), s("BO", 0, 128, 16))
+    gcopy(s("Z1", 15, 143, 16), s("ST", 0, 128, 16))
     act(s("ZX"), s("ZS", 0, 128), scale=s("XB"))
-    ts(s("ZH"), s("ZS"), pc(9), mul, 4096.0, mul)
-    ms(s("KM"), -1.0 / 8192)
-    for n, c in (("K256", 256), ("K16", 16), ("KM8", -8)):
-        iota(s(n), [[0, s(n)[3]]], c, 0)
-    act(s("BO32"), s("BO"))
-    act(s("Z1"), s("ZS"), scale=rm(0))
-    act(s("R0M"), s("BO"), scale=rm(0))
-    ts(s("ASKM"), s("BO"), pc(13), mul, 2048.0, mul)
-    act(s("BO4"), s("BO"), scale=4096.0)
-    for n, c in (("ID128", 128.0), ("IDN", -1.0), ("IC1", 2832.0), ("IC2", 7.125), ("IDS", 1.0 / 512)):
-        act(s(n), s("ID32"), scale=c)
-    act(s("DN"), s("ID32"), scale=pc(11))
-    act(s("D0"), s("ID32"), scale=rm(0))
+    act(s("BO32"), BO)
+    act(s("BO4"), BO, scale=4096.0)
+    act(s("TRI"), BO, scale=pc(21))
+    sel(s("TRI"), s("TRI"), [[-1, 128]], ALU.is_gt, 0.0, 0, 1)
+    gcopy(s("TRI", 15, 128, 16), s("ID32", 15, 128, 16))
+    diag(s("DIF"), ID, -1.0, -1)
+    gcopy(s("DIF", 0, 128, 16), s("ID", 0, 128, 16))
+    diag(s("DT"), ID, -1.0, 1)
+    gcopy(s("DT", 14, 128, 16), s("ID", 14, 128, 16))
+    gcopy(s("DT", 15, 128, 16), s("ZB", 0, 8))
+    act(s("DT32"), s("DT"), scale=1.0 / 512)
+    ts(s("DTN"), s("DT"), -1.0 / 512, mul)
+    ts(s("L14"), ID, pc(19), mul)
+    ts(s("D0"), ID, pc(18), mul)
+    act(s("DN"), ID32, scale=pc(11))
+    sel(s("S2K"), ZB, [[-16, 8], [0, 16]], ALU.not_equal, -2048.0, -15, 1)
+    ts(s("XBN"), BO, s("XB"), mul, -1.0, mul)
+    ts(s("ZH"), s("ZS"), 4096.0, mul)
+    ts(s("D16"), ID, pc(20), mul, 1.0 / 16, mul)
+    ms(s("AQ", 128, 144), 0.0)
+    for h in range(NH):
+        sel(s("SEL", h * 128, (h + 1) * 128), ZB, [[-NH, 8], [0, 16]], ALU.not_equal, 1.0, -h, 1)
+    act(s("KT"), ZB, bias=pc(16))
+    iota(s("DUM"), [[2, 128]], H, 0)
+    iota(s("CV"), [[512, 96]], 512 * S0 + 128, 0)
     act(s("ASK", 128, 144), s("RM"), scale=16.0)
     for f in ("FA", "FB"):
-        act(s(f, 1920, 2048), s("ZERO", 0, 128), bias=s("XB"))
-    ts(s("T2"), s("T0"), 0.0, ALU.is_ge)
-    tt(s("TRI"), s("T2"), s("BO"), mul)
-    ts(s("T2"), s("T0"), 1.0, ALU.is_equal)
-    tt(s("T1"), s("T1"), s("T2"), sub)
-    tt(s("DIF"), s("T1"), s("BO"), mul)
-    ms(s("DIF", 15, 128, 16), 0.0)
-    act(s("DIFX"), s("DIF"), scale=1.0 / 512)
+        act(s(f, 1920, 2048), ZB, bias=s("XB"))
     ts(s("BM", 0, 8), s("COLK", 0, 8), pc(1), ALU.is_equal)
-    cp(s("BM", 8, 16), s("BM", 0, 8))
+    gcopy(s("BM", 8, 16), s("BM", 0, 8))
     ms(s("CUM", 0, 1), 0.0)
     ms(s("NN", 128, 144), 0.0)
+    for w in (1, 2):
+        send(T.cores[(rank - w) % N], T.cores[(rank + w) % N], s("OB", w * 256, (w + 1) * 256), s("OB", 0, 256), "ob%d" % w)
 
     TBW = s("TB", 0, 2048)
     CH = [(0, 4), (4, 8), (8, 12), (12, 15)]
 
-    def names(lst, a, par):
+    def names(lst, a, par, q):
         a0, t0 = 176 * par, 288 * par
-        act(s("AB", a0 + a, a0 + 160 + (a & 1)), ind(TBW, lst))
+        mv(q, s("AB", a0 + a, a0 + 160 + (a & 1)), ind(TBW, lst))
         tr(s("TT", t0, t0 + 128), s("AB", a0 + 32, a0 + 160))
         tr(s("TT", t0 + 128, t0 + 288), s("AB", a0 + 16, a0 + 176))
         ts(s("NL", 128 * par, 128 * par + 128), ind(s("TT", t0, t0 + 288), s("PERM")), 1.0 / 512, mul)
         return s("AB", a0 + 32, a0 + 160)
 
-    def gat(dst, win, c, par, bias=0.0):
-        a, b = CH[c]
-        act(s(dst, a * 128, b * 128), ind(win, s("NL", 128 * par + a * 8, 128 * par + b * 8)), bias=bias)
+    def gat(dst, win, a, b, par, bias=0.0, aft=None):
+        return act(s(dst, a * 128, b * 128), ind(win, s("NL", 128 * par + a * 8, 128 * par + b * 8)), bias=bias, aft=aft)
 
-    def repeats(kb, k0, start):
-        pos = [0]
+    def weights(o, A, P):
+        if OPT["nm"] == "v":
+            ts(P, A, 2 * MAG, add, 2 * MAG, sub)
+        else:
+            act(s("NM"), A, bias=2 * MAG)
+            act(P, s("NM"), bias=-2 * MAG)
+        tt(o, A, P, sub)
+
+    CNT = s("P6", 0, 128)
+
+    def repeats(k0, stop):
         for c in range(8):
-            n = 128 - 16 * c
-            act(s("EA", pos[c], pos[c] + n), s("P7", 512 - n, 512), AF.Abs, bias=s(kb, k0 + c, k0 + c + 1), scale=-512.0)
-            pos.append(pos[c] + n)
-        act(s("EQ", 0, pos[8]), s("EA", 0, pos[8]), AF.Relu, bias=pc(15), scale=-1.0)
+            act(s("EA", pos[c], pos[c + 1]), s("P7", 384 + 16 * c, 512), AF.Abs, bias=s("KB", k0 + c, k0 + c + 1), scale=-512.0)
+        for a, b in ((0, 3), (3, 8)):
+            act(s("EQ", pos[a], pos[b]), s("EA", pos[a], pos[b]), AF.Relu, bias=128.0, scale=-1.0)
+        counts(0, True, stop)
+
+    pos = [sum(128 - 16 * x for x in range(c)) for c in range(9)]
+
+    def counts(a, start, stop):
         for c in range(8):
-            mm(s("P7", 16 * c, 128), s("BO4"), s("EQ", pos[c], pos[c + 1]), start and c == 0, c == 7)
+            mm(s("P6", a + 16 * c, a + 128), s("BO4"), s("EQ", pos[c], pos[c + 1]), start and c == 0, stop and c == 7)
 
     def targets(h):
-        tt(s("OF"), s("DUM"), s("P7", 0, 128), mn)
+        tt(s("OF"), s("DUM"), CNT, mn)
+        at(h, "list")
         for r in range(16):
-            mm(s("P7", 128, 136), s("Z1", 15 - r, 143 - r), s("OF", r, 128, 16), r == 0, r == 15)
-        cp(s("OFU", 8 * (h & 1), 8 * (h & 1) + 8), s("P7", 128, 136))
+            mm(s("P6", 128, 136), s("Z1", 15 - r, 143 - r), s("OF", r, 128, 16), r == 0, r == 15)
+        cp(s("OFU", 8 * (h & 1), 8 * (h & 1) + 8), s("P6", 128, 136))
 
-    mm(s("P7", 384, 512), s("ID"), s("ZP", 136, 264), True, False)
-    mm(s("P7", 384, 512), s("IDS"), s("RX", SL + 4, SL + 132), False, True)
-    repeats("RX", SL + 132, True)
-    act(s("CR", 8, 136), s("P7", 0, 128))
-
-    def chance(h):
-        for i in range(3):
-            c = h * 128
-            while c < (h + 1) * 128:
-                x = c // 48
-                e = min((x + 1) * 48, (h + 1) * 128)
-                mm(s("P4", i * 128 + c - h * 128, i * 128 + e - h * 128), st(x),
-                   s("RB", i * 48 + c - x * 48, i * 48 + e - x * 48), True, True)
-                c = e
-        act(s("ABV", 384 * (h & 1), 384 * (h & 1) + 384), s("P4", 0, 384))
+    mm(s("P7", 240, 512), ID, s("ZP"), True, False)
+    mm(s("P7", 376, 384), ID, s("L16", 8, 16), False, False)
+    mm(s("P7", 375, 376), st(15), s("L16", 17, 18), False, False)
+    mm(s("P7", 384, 512), ID, s("INI", 128, 256), False, True)
+    act(s("KB", 0, 9), s("P7", 375, 384), scale=512.0)
 
     for h in range(NH):
         w, par = h >> 1, h & 1
         m0 = S0 + 16 * h
         F = "FB" if par else "FA"
-        y0, n0 = 144 * par, 384 * par
+        y0 = 144 * h
+        at(h, "names")
         Y = s("YS", y0, y0 + 128)
-        act(Y, s("OB", w * 256 + par, (w + 1) * 256, 2))
-        act(s("YS", y0 + 128, y0 + 144), s("EM", m0, m0 + 16))
-        for r in range(4):
-            mm(s("P1", r * 128, (r + 1) * 128), s("ID"), Y, True, True)
-        if h == 0:
-            chance(0)
-        r1, r2, k1 = (h + 1) * SL, h * SL, (h - 1) * SL
+        gcopy(Y, s("OB", w * 256 + par, (w + 1) * 256, 2))
+        gcopy(s("YS", y0 + 128, y0 + 144), s("EM", m0, m0 + 16))
+        r1, r2, k1, k0 = (h - 1) * SL, (h - 2) * SL, (h - 1) * SL, h * SL
         if par == 0:
-            s512, q512, l512 = s("RX", r2 + 12, r2 + 140), s("RX", r1 + 4, r1 + 132), s("RX", r1 + 3, r1 + 131)
             if h:
-                ts(s("LU", (h + 1) * 16 + 8, (h + 2) * 16), s("RX", r1 + 132, r1 + 140), 1.0 / 512, mul)
-                A = names(s("LU", (h + 1) * 16 + 6, (h + 2) * 16), 1, par)
+                sa, sl, qa = s("RX", r2 + 16, r2 + 144), s("RX", r2 + 8, r2 + 16), s("RX", r1 + 8, r1 + 136)
+                lr = s("RX", r1 + 8, r1 + 135)
+                cp(s("LU", (h + 1) * 16 + 8, (h + 2) * 16), s("RX", r1 + 136, r1 + 144))
+                A = names(s("LU", (h + 1) * 16 + 6, (h + 2) * 16), 1, par, OPT["ag"])
             else:
+                sa, sl, qa, lr = s("INI", 0, 128), s("L16", 0, 8), s("INI", 128, 256), s("INI", 128, 255)
                 cp(s("AB", 177, 337), ind(s("LK"), s("LU", 22, 32)))
                 tr(s("TT", 0, 128), s("AB", 208, 336))
                 tr(s("TT", 128, 288), s("AB", 192, 352))
                 ts(s("NL", 0, 128), ind(s("TT", 0, 288), s("PERM")), 1.0 / 256, mul, -0.498, add)
                 act(s("AB", 1, 161), ind(TBW, s("LU", 22, 32)))
                 A = s("AB", 32, 160)
-            ts(s("EQ0", 1, 128), s("RX", r1 + 4, r1 + 131), s("RX", r1 + 3, r1 + 4), ALU.is_equal, 4096.0, mul)
-            mm(s("P7", 0, 128), s("IDS"), l512, True, False)
-            mm(s("P7", 0, 128), s("ID"), s("CR", 144 * w + 7, 144 * w + 135), False, False)
-            mm(s("P7", 0, 128), st(15), s("EQ0"), False, True)
-            targets(h)
         else:
-            s512, q512, l512 = s("RX", r2 + 4, r2 + 132), s("PK", k1 + 13, k1 + 141), s("PK", k1 + 12, k1 + 140)
-            A = names(s("PU", 8 * h - 8, 8 * h), 32, par)
-            cp(s("PK", k1 + 140, k1 + 141), s("RX", r1 + 12, r1 + 13))
+            if h > 1:
+                sa, sl = s("RX", r2 + 8, r2 + 136), s("RX", r2 + 136, r2 + 144)
+            else:
+                sa, sl = s("INI", 128, 256), s("L16", 8, 16)
+            qa = s("PK", k1 + 17, k1 + 145)
+            A = names(s("PU", 8 * h - 8, 8 * h), 32, par, OPT["ag"])
+            at(h, "d")
+            cp(s("PK", k1 + 144, k1 + 145), s("RX", r1 + 16, r1 + 17))
             if h < NH - 1:
-                ts(s("LU", (h + 1) * 16 + 8, (h + 2) * 16), s("RX", r1 + 4, r1 + 12), 1.0 / 512, mul)
-        for c in range(4):
-            gat(F, s("EM"), c, par)
-        tt(s("DD", 0, 128), A, s512, sub)
-        tt(s("DD", 128, 256), ind(TBW, s("LU", h * 16 + 8, h * 16 + 16)), q512, sub)
-        mm(s("P0"), s("ID"), s("ZERO"), True, False)
+                at(h, "side")
+                cp(s("LU", (h + 1) * 16 + 8, (h + 2) * 16), s("RX", r1 + 8, r1 + 16))
+        at(h, "d")
         for r in range(4):
-            mm(s("P0", r * 128, (r + 1) * 128), s("ID32"), q512, False, False)
-        act(s("GT"), s("DD"), AF.Abs, bias=-256.0)
-        act(s("CL"), s("GT"), AF.Relu, bias=pc(0), scale=-1.0)
-        mm(s("P6", 0, 256), s("BO15"), s("CL"), True, True)
-        NM = s("P2", 128, 256)
-        act(s("NM", 0, 128), A, bias=2 * MAG)
-        act(NM, s("NM", 0, 128), bias=-2 * MAG)
-        tt(s("WT"), A, NM, sub)
-        tt(s("VM"), NM, s512, sub)
-        tt(s("P6", 0, 256), s("P6", 0, 256), s("ABV", n0, n0 + 256), mul)
-        ts(s("U2"), s("P6", 128, 256), 255.0, mn, 1535.502, add)
+            mm(s("P1", r * 128, (r + 1) * 128), ID, Y, True, True)
+        left, aft = {"f": list(OPT["chf"]), "c": list(OPT["chc"])}, None
+        for n, x in enumerate(OPT["gorder"]):
+            at(h, ("f0", "f1", "gather")[min(n, 2)])
+            a, b = left[x].pop(0)
+            aft = gat(F, s("EM"), a, b, par, 0.0, aft) if x == "f" else gat("CW", TBW, a, b, par, 34431.5, aft)
+        at(h, "d")
+        SEL = s("SEL", h * 128, (h + 1) * 128, rows=48)
+        mm(s("P0", 0, 256), SEL, s("RB", 0, 256, rows=48), True, True)
+        act(s("DG"), ind(TBW, s("LU", h * 16 + 8, h * 16 + 16)))
+        at(h, "fit")
+        group(s("P6", 384, 512), [(IDM, sa), (ID32, A)])
+        group(s("P6", 256, 384), [(ID32, s("DG")), (IDM, qa)])
+        act(s("GT"), s("P6", 256, 512), AF.Abs, bias=-256.0)
+        if OPT["cl"] == "a":
+            act(s("CL"), s("GT"), AF.Relu, bias=256.0, scale=-1.0)
+        else:
+            ts(s("CL"), s("GT"), 256.0, mn, -256.0, add)
+        at(h, "slice")
+        weights(s("WT"), A, s("P0", 384, 512))
+        tt(s("CB"), s("CL"), s("P0", 0, 256), mul)
+        mm(s("P0", 256, 384), s("BO32"), s("CB", 0, 128), True, True)
+        ts(s("U2"), s("P0", 256, 384), 255.0, mn, 1535.502, add)
         for r in range(4):
-            mm(s("P0", r * 128, (r + 1) * 128), s("ID"), s("U2"), False, r == 3)
-        tt(s("SVW"), s("WT"), s("P6", 0, 128), ALU.is_gt)
-        act(s("ND0"), s("WT"), AF.Relu, bias=-239.0)
-        act(s("ND"), s("ND0"), bias=-16.0)
-        mm(s("P6", 256, 384), s("DN"), A, True, False)
-        mm(s("P6", 256, 384), s("D0"), q512, False, True)
-        act(s("AQ", 0, 128), s("P6", 256, 384), bias=pc(12))
-        act(s("P2", 384, 512), s512, bias=float(1 - m0), scale=1.0 / 512)
+            group(s("P0", r * 128, (r + 1) * 128), [(IDM, qa), (IDN, s("U2"))])
+        at(h, "side")
+        group(s("P6", 256, 384), [(ID, s("WT")), (s("BO32"), s("CB", 128, 256))])
+        act(s("SG"), s("P6", 256, 384), AF.Sign, bias=-1.0 / 512)
+        group(s("P6", 384, 512), [(s("D0"), qa), (s("DN"), A)])
+        act(s("AQ", 0, 128), s("P6", 384, 512), bias=pc(12))
+        ts(s("ND"), s("WT"), -255.0, add, pc(14), mx)
+        group(s("P2", 128, 256), [(s("L14"), sa), (s("DT32"), A), (s("DTN"), s("WT"))])
+        at(h, "first")
+        if par == 0:
+            if h == 0:
+                repeats(1, True)
+                act(s("CR", 8, 136), CNT)
+            kb = 16 * h
+            ts(s("EQ0", 1, 128), lr, 512.0, mul, s("KB", kb, kb + 1), ALU.is_equal)
+            mm(CNT, ID, s("CR", 144 * w + 7, 144 * w + 135), True, False)
+            mm(s("P6", 1, 128), ID, lr, False, False)
+            if h:
+                mm(s("P6", 0, 1), ID, s("PK", k1 + 135, k1 + 136), False, False)
+            else:
+                mm(s("P6", 0, 1), st(15), s("L16", 17, 18), False, False)
+            mm(s("P6", 1, 128), s("BO4"), s("EQ0", 1, 128), False, True)
+        else:
+            repeats(16 * h + 1, False)
+            mm(CNT, ID, s("PK", k1 + 16, k1 + 144), False, True)
+        mm(s("P6", 256, 384), s("XBN"), Y, True, False)
+        if par == 0:
+            mm(s("P6", 256, 384), ID, s("CR", 144 * w + 7, 144 * w + 135), False, False)
+            mm(s("P6", 257, 384), s("BO4"), s("EQ0", 1, 128), False, False)
+        else:
+            counts(256, False, False)
+        mm(s("P6", 256, 384), s("S2K"), s("SG"), False, True)
+        act(s("NZ"), s("P6", 256, 384), AF.Relu, bias=2049.0)
+        targets(h)
+        at(h, "test")
+        group(s("P3", 384, 512), [(SEL, s("RB", 256, 384, rows=48)), (s("D16"), s("K16", 0, 128))])
         mm(s("P3", 0, 128), s("ZX"), Y, True, False)
-        for c in range(4):
-            a, b = CH[c]
+        for a, b in OPT["chf"]:
             tt(s("PW", a * 128, b * 128), s(F, a * 128, b * 128), s("P1", 0, (b - a) * 128), mul)
             for k in range(a, b):
-                mm(s("P3", 0, 128), s("ZS", 15 - k, 143 - k), s("PW", k * 128, (k + 1) * 128), False, k == 14)
-        mm(s("P2", 0, 128), s("ZS", 0, 128), s("K256"), True, False)
-        for c in range(4):
-            a, b = CH[c]
-            gat("CW", TBW, c, par, 34431.5)
-            tt(s("XW", a * 128, b * 128), s("CW", a * 128, b * 128), s("P0", 0, (b - a) * 128), sub)
-            if c == 0:
-                continue
-            a = 0 if c == 1 else a
+                mm(s("P3", 0, 128), s("ZS", 15 - k, 143 - k), s("PW", k * 128, (k + 1) * 128), False, False)
+        mm(s("P3", 0, 128), s("ID2K"), s("SG"), False, True)
+        act(s("E1"), s("P3", 0, 128), AF.Relu, bias=-2048.0)
+        tt(s("EV"), s("E1"), s("P3", 384, 512), mul)
+        mm(s("P2", 0, 128), s("ZH", 0, 128), s("K16", 0, 128), True, False)
+        for a, b in OPT["chc"]:
+            tt(s("XW", a * 128, b * 128), s("CW", a * 128, b * 128), s("P0", 0, (b - a) * 128), add)
             ts(s("IW", a * 128, b * 128), s("XW", a * 128, b * 128), 33024.0, ALU.is_equal)
             for k in range(a, b):
                 mm(s("P2", 0, 128), s("ZH", 15 - k, 143 - k), s("IW", k * 128, (k + 1) * 128), False, k == 14)
-        tt(s("SV"), s("SVW"), s("P2", 0, 128), mn)
-        tt(s("SE"), s("SV"), s("P3", 0, 128), mul)
-        mm(s("P7", 128, 256), s("BO32"), s("SE"), True, True)
-        mm(s("P7", 0, 128), s("TRI"), s("SE"), True, True)
+        at(h, "draw")
+        mm(s("P0", 0, 128), s("IDB"), s("NZ"), True, False)
+        tt(s("SW"), s("EV"), s("P2", 0, 128), mn)
+        mm(s("P0", 0, 128), s("BO32"), s("SW"), False, True)
+        ts(s("ASK", 0, 128), s("P0", 0, 128), 0.0, ALU.is_le)
+        at(h, "hit")
+        tt(s("SE"), s("E1"), s("P2", 0, 128), mn)
+        group(s("P1", 0, 128), [(s("BO32"), s("SW")), (s("TRI"), s("SE"))])
+        ts(s("HIT"), s("P1", 0, 128), 0.0, ALU.is_gt)
+        mm(s("P1", 128, 256), s("DIF"), s("HIT"), True, True)
+        tt(s("NN", 0, 128), s("ND"), s("P1", 128, 256), mul)
+        at(h, "g")
+        tt(s("SV"), s("SG"), s("P2", 0, 128), mn)
         act(s("ES"), s("P3", 0, 128))
-        mm(s("P3", 128, 256), s("IC1"), s("SV"), True, False)
-        mm(s("P3", 128, 256), s("IC2"), s("SV"), False, False)
-        mm(s("P3", 128, 256), s("ID32"), s("ES"), False, True)
-        gb = math.log(0.5 ** (3 - w))
-        act(s("P2", 256, 384), s("P3", 128, 256), AF.Exp, bias=gb, scale=1.0 / 4096)
+        group(s("P3", 256, 384), [(ID32, s("ES")), (s("IS1"), s("SG")), (s("IS2"), s("SG")), (s("IC1"), s("SV")), (s("IC2"), s("SV"))])
+        at(h, "hit")
+        tt(s("XX"), s("HIT"), s("P2", 128, 256), mul)
+        at(h, "g")
+        gb = math.log(0.5 ** (3 - w)) + 1419.5625 / 4096
         GH, GL = s("GH", 128 * par, 128 * par + 128), s("GL", 128 * par, 128 * par + 128)
-        act(GH, s("P2", 256, 384))
-        tt(GL, s("P2", 256, 384), GH, sub)
-        tt(s("VC"), s("ABV", n0 + 256, n0 + 384), s("P7", 128, 256), mul)
-        tt(s("HIT"), s("P7", 0, 128), s("VC"), ALU.is_gt)
-        mm(s("P0", 0, 128), s("ASKM"), s("HIT"), True, True)
-        mm(s("P0", 128, 256), s("DIFX"), s("HIT"), True, False)
-        mm(s("P0", 128, 256), s("ZS", 0, 128), s("KM"), False, True)
-        mm(s("P0", 256, 384), s("DIF"), s("HIT"), True, True)
-        tt(s("ASK", 0, 128), s("P0", 0, 128), s("OF"), ALU.is_gt)
-        tt(s("XX"), s("VM"), s("P0", 128, 256), mul)
-        tt(s("NN", 0, 128), s("ND"), s("P0", 256, 384), mul)
-        l0, b0 = (248, 256) if par == 0 else (376, 248)
-        PL, PB = s("P7", l0, l0 + 8), s("P7", b0, b0 + 128)
-        mm(s("P7", 248, 512), s("ID"), s("ZP", 264 * par, 264 * par + 264), True, False)
-        mm(PB, s("BO"), s("XX"), False, False)
-        mm(s("P7", 384, 512), s("BO"), s("XX"), False, False)
+        if OPT["gl"] == "v":
+            act(s("P3", 128, 256), s("P3", 256, 384), AF.Exp, bias=gb, scale=1.0 / 4096)
+            act(GH, s("P3", 128, 256))
+            tt(GL, s("P3", 128, 256), GH, sub)
+        else:
+            act(s("GS"), s("P3", 256, 384), AF.Exp, bias=gb, scale=1.0 / 4096)
+            act(GH, s("GS"))
+            group(s("P3", 128, 256), [(ID32, s("GS")), (IDN, GH)])
+            act(GL, s("P3", 128, 256))
+        at(h, "draw")
+        l0 = 376 if par else 240
+        PL, PB, PX = s("P7", l0, l0 + 8), s("P7", 248, 376), s("P7", 384, 512)
+        last = h == NH - 1
+        mm(s("P7", 240, 512), ID, s("ZP"), True, False)
+        mm(PL, ID, sl, False, False)
+        for o in () if last else (PB, PX):
+            mm(o, ID, sa, False, False)
         for r in range(16):
             mm(PL, s("ZS", 15 - r, 143 - r), s("XX", r, 128, 16), False, False)
+        for o in () if last else (PB, PX):
+            mm(o, BO, s("XX"), False, False)
+        TZ = s("P0", 128, 256)
+        mm(TZ, st(h), s("KT"), True, False)
+        mm(TZ, st(15), s("KT"), False, False)
+        mm(TZ, IDN, sa, False, OPT["born"] == "v")
         scan(s("CUM", 1, 145), s("ASK"), s("K16"), add, mn)
-        act(s("JK"), s("CUM", 1, 145), AF.Sign, bias=pc(10), scale=-1.0, acc=s("IAC"))
-        mm(s("P1", 0, 128), s("ID"), s("CUM", 1, 129), True, False)
-        mm(s("P1", 0, 128), s("IDN"), s("CUM", 0, 128), False, True)
-        tt(s("ZZ"), s("CUM", 1, 129), s("P2", 384, 512), sub)
-        tt(s("YY"), s("ZZ"), s("P1", 0, 128), mul)
-        mm(PB, s("R0M"), s("YY"), False, False)
-        mm(s("P7", 384, 512), s("R0M"), s("YY"), False, False)
+        act(s("JK"), s("CUM", 1, 145), AF.Sign, bias=pc(10), scale=-1.0, acc=s("IAC", 0, 1))
+        group(s("P2", 384, 512), [(ID, s("CUM", 1, 129)), (IDN, s("CUM", 0, 128))])
+        if OPT["born"] == "v":
+            tt(s("ZZ"), s("CUM", 1, 129), TZ, add)
+            tt(s("YY"), s("ZZ"), s("P2", 384, 512), mul)
+        else:
+            mm(TZ, ID, s("CUM", 1, 129), False, True)
+            act(s("BN"), s("P2", 384, 512))
+            tt(s("YY"), s("BN"), TZ, mul)
+        for o in () if last else (PB, PX):
+            mm(o, st(0), s("YY"), False, False)
         for r in range(16):
             mm(PL, s("Z1", 15 - r, 143 - r), s("YY", r, 128, 16), False, r == 15)
-        k0 = h * SL
-        if h < NH - 1:
-            act(s("PK", k0 + 4, k0 + 140), s("P7", 248, 384), scale=512.0)
-            send(prv, nxt, s("RX", (h + 2) * SL + 4, (h + 2) * SL + 140), s("PK", k0 + 4, k0 + 140), "rx%d" % h)
-        if par == 0 or h == NH - 1:
+        if par == 0 or last:
             cp(s("PU", 8 * h, 8 * h + 8), PL)
-        else:
-            cp(s("LU", (h + 2) * 16 + 6, (h + 2) * 16 + 8), s("P7", 382, 384))
-            act(s("RX", (h + 2) * SL + 3, (h + 2) * SL + 4), s("P7", 375, 376), scale=512.0)
+        if not last:
+            p0 = 248 if par else 240
+            ts(s("PK", k0 + 8, k0 + 144), s("P7", p0, p0 + 136), MG1, add, MG1, sub)
+            send(prv, nxt, s("RX", k0 + 8, k0 + 144), s("PK", k0 + 8, k0 + 144), "rx%d" % h)
+            at(h, "repeats" if par else "kb")
+            if par:
+                cp(s("LU", (h + 2) * 16 + 6, (h + 2) * 16 + 8), s("P7", 382, 384))
+                act(s("KB", 16 * h + 16, 16 * h + 25), s("P7", 375, 384), scale=512.0)
+            else:
+                act(s("KB", 16 * h + 17, 16 * h + 25), PL, scale=512.0)
+        at(h, "draw")
         IDX = s("IDX", 0, 1)
-        ts(IDX, s("IAC"), 0.5, mul, 72.0, add)
+        ts(IDX, s("IAC", 0, 1), 0.5, mul, 72.0, add)
         tt(s("G1"), ind(s("AB", 176 * par + 32, 176 * par + 176), IDX), s("CV", 16 * h, 16 * h + 16), sub)
         act(s("EM", m0, m0 + 16), ind(s("YS", y0, y0 + 144), IDX))
         tt(ind(s("NN"), IDX), s("G1"), s("BM"), mul)
         tt(ind(s("TB"), s("OFU", 8 * par, 8 * par + 8)), A, s("NN", 0, 128), sub)
-        cp(s("AQ", 128, 144), s("TB", m0, m0 + 16))
-        cp(s("TB", m0, m0 + 16), ind(s("AQ"), IDX))
-        if par == 0:
-            mm(s("P7", 0, 128), s("IDS"), s("PK", k0 + 12, k0 + 140), True, False)
-            repeats("PK", k0 + 4, False)
-            targets(h + 1)
-        elif h < NH - 1:
-            repeats("PK", k0 + 132, True)
-            act(s("CS", 128 * w, 128 * w + 128), s("P7", 0, 128))
+        act(s("IAC", 1, 2), s("IAC", 0, 1), AF.Sign, bias=-111.0)
+        ts(s("IDX", 2, 3), s("IAC", 1, 2), 128.0, mul, pc(13), add)
+        mv(OPT["tbm"], s("G2"), ind(s("AQ"), IDX))
+        cp(ind(s("TB", m0, m0 + 272), s("IDX", 2, 3)), s("G2"))
+        if par and not last:
+            at(h, "repeats")
+            repeats(16 * h + 17, True)
+            act(s("CS", 128 * w, 128 * w + 128), CNT)
             send(prv, nxt, s("CR", 144 * w + 152, 144 * w + 280), s("CS", 128 * w, 128 * w + 128), "cx%d" % w)
-        if h < NH - 1:
-            chance(h + 1)
-        for c in range(4):
+        at(h, "g" if last else "sums")
+        for c, (a, b) in enumerate(OPT["chg"]):
             bk = "P%d" % (4 + (c & 1))
-            for k in range(4 * c, 4 * c + 4):
-                o = s(bk, (k & 3) * 128, (k & 3) * 128 + 128)
-                mm(o, st(k), GH, True, False)
-                mm(o, st(k), GL, False, True)
-            a, b = CH[c]
+            for k in range(a, b + (b == 15)):
+                group(s(bk, (k - a) * 128, (k - a) * 128 + 128), [(st(k), GH), (st(k), GL)])
             tt(s("PR%d" % par, a * 128, b * 128), s(F, a * 128, b * 128), s(bk, 0, (b - a) * 128), mul)
-        act(s("PR%d" % par, 1920, 2048), s("P5", 384, 512), scale=s("XB"))
+        act(s("PR%d" % par, 1920, 2048), s(bk, (15 - a) * 128, (16 - a) * 128), scale=s("XB"))
         fold(h)
+    at(NH, "names")
     for par in range(2):
         F = "FB" if par else "FA"
-        A = names(s("PU", 32 + 8 * par, 40 + 8 * par), 32, par)
-        for c in range(3):
-            gat(F, s("EM"), c, par)
-        cp(s(F, 1536, 1920), ind(s("EM"), s("NL", 128 * par + 96, 128 * par + 120)))
-        a0 = 128 * par
-        ts(s("NM", a0, a0 + 128), A, 2 * MAG, add, 2 * MAG, sub)
-        tt(s("WB", a0, a0 + 128), A, s("NM", a0, a0 + 128), sub)
+        A = names(s("PU", 32 + 8 * par, 40 + 8 * par), 32, par, "a")
+        for a, b in CH:
+            gat(F, s("EM"), a, b, par)
+        WB = s("WB", 128 * par, 128 * par + 128)
+        weights(s("WT"), A, s("P%d" % (2 + par), 128, 256))
+        ts(WB, s("WT"), -128.0, add)
         for c in range(4):
             bk = "P%d" % (6 * par + (c & 1))
-            mm(s(bk), s("BO"), s("KM8"), True, False)
             for k in range(4 * c, 4 * c + 4):
-                mm(s(bk, (k & 3) * 128, (k & 3) * 128 + 128), st(k), s("WB", a0, a0 + 128), False, (k & 3) == 3)
+                mm(s(bk, (k & 3) * 128, (k & 3) * 128 + 128), st(k), WB, True, True)
             tt(s("PZ", c * 512, (c + 1) * 512), s(F, c * 512, (c + 1) * 512), s(bk), mul)
             for k in range(4 * c, 4 * c + 4):
                 mm(s("P%d" % (2 + par), 0, 128), s("ID128"), s(F, k * 128, (k + 1) * 128), k == 0, False)
-                mm(s("P%d" % (2 + par), 0, 128), s("ID"), s("PZ", k * 128, (k + 1) * 128), False, k == 15)
-        act(s("YA", par, 256, 2), s("AC", (4 + par) * 128, (5 + par) * 128))
+                mm(s("P%d" % (2 + par), 0, 128), ID, s("PZ", k * 128, (k + 1) * 128), False, k == 15)
+        gcopy(s("YA", par, 256, 2), s("AC", (4 + par) * 128, (5 + par) * 128))
         act(s("YZ", par, 256, 2), s("P%d" % (2 + par), 0, 128))
     dma("s", dr(T.ya[:]), s("YA"), "dya", 2000.0)
     dma("s", dr(T.yz[:]), s("YZ"), "dyz", 2000.0)
 
-    ops = schedule(ops)
+    ops = schedule(ops, turn)
     deps = depends(ops, True)
     clock = {q: {} for q in "vapgsx"}
     at, waits, need = [], [], set()

@@ -4,39 +4,46 @@ from concourse.mybir import AluOpType as ALU, ActivationFunctionType as AF
 
 F32, BF, F16, I32, U16 = "float32", "bfloat16", "float16", "int32", "uint16"
 H, S0, NH = 2048, 1952, 6
-SL = 160
+FW = 256
+SL = 144
 SB = {
     "LK": (2048, I32), "TB": (2320, F32), "EM": (2048, BF), "OB": (768, BF), "XB": (1, F32),
-    "PEPO": (16, I32), "RN": (384, I32), "RB": (384, BF), "L16": (18, F16), "INI": (256, F16),
-    "RX": (5 * SL, F16), "PK": (6 * SL, F16), "LU": (7 * 16, U16), "PU": (48, U16), "CR": (432, BF), "CS": (256, BF),
+    "PEPO": (16, I32), "RN": (384, I32), "RB": (384, BF), "L16": (20, F16), "INI": (256, F16),
+    "RX": (5 * SL, F16), "PK": (6 * SL, F16), "LU": (32, U16), "SU": (6 * SL, U16), "RU": (5 * SL, U16), "CR": (432, BF), "CS": (256, BF),
     "EQ0": (128, BF), "KB": (7 * 16, F32), "AB": (352, F32), "DG": (128, F32), "TT": (576, F32), "NL": (256, U16), "PERM": (8, U16),
     "FA": (2048, BF), "FB": (2048, BF), "CW": (2048, F32), "XW": (2048, BF), "IW": (2048, BF), "PW": (2048, BF),
-    "PR0": (2048, F32), "PR1": (2048, F32), "PZ": (2048, F16), "HB": (768, F32), "AC": (768, F32),
-    "CL": (256, BF), "GT": (256, BF), "CB": (256, F32), "U2": (128, F16), "NM": (128, F32),
+    "PR0": (2048, F32), "PR1": (2048, F32), "PZ": (4096, F16), "HB": (NH * FW, F32), "AC": (NH * FW, F32),
+    "CL": (256, BF), "GT": (256, BF), "CB": (256, F32), "U2": (128, F16),
     "WT": (128, BF), "WB": (256, BF), "SG": (128, BF), "ND": (128, BF), "AQ": (144, F32), "YS": (6 * 144, BF),
     "EA": (704, BF), "EQ": (704, BF), "OF": (128, F16), "OFU": (16, U16), "SV": (128, BF), "SE": (128, F32), "SW": (128, F32),
-    "GS": (128, F32), "ES": (128, F32), "GH": (256, BF), "GL": (256, BF), "HIT": (128, BF), "ASK": (144, BF), "CUM": (145, BF), "BN": (128, BF),
-    "ZZ": (128, F32), "XX": (128, F16), "YY": (128, F16), "NN": (144, F32), "JK": (144, BF), "IAC": (2, F32),
-    "IDX": (4, U16), "G1": (16, F32), "YA": (256, F32), "YZ": (256, F32),
+    "ES": (128, F32), "GH": (256, BF), "GL": (256, BF), "HIT": (128, BF), "ASK": (144, BF), "CUM": (145, BF), "E0": (40, F16), "R0": (24, F16),
+    "ZZ": (128, F32), "XR": (128, BF), "XX": (128, F16), "YY": (128, F16), "NN": (144, F32), "JK": (144, BF), "IAC": (2, F32),
+    "IDX": (4, U16), "G1": (40, F32), "YA": (256, F32), "YZ": (256, F32),
     "PI": (8, I32), "PC": (24, F32), "RM": (16, F32), "BM": (16, F32), "COLG": (128, F32), "COLK": (16, F32),
     "DUM": (128, F32), "CV": (96, F32), "C2": (8, F32), "BO": (128, BF), "BO32": (128, F32), "BO4": (128, BF),
     "ZS": (143, BF), "Z1": (143, BF), "ZX": (128, BF), "TRI": (128, F32), "DIF": (128, BF), "DT": (128, BF), "DT32": (128, F32),
     "DTN": (128, BF), "L14": (128, BF), "S2K": (128, BF), "XBN": (128, BF), "ZH": (143, BF), "D16": (128, BF),
-    "IS1": (128, BF), "IS2": (128, BF), "ID2K": (128, BF), "IDB": (128, BF), "NZ": (128, BF), "E1": (128, F32), "EV": (128, F32),
-    "G2": (16, F32), "ID": (128, BF), "IDN": (128, BF), "IDM": (128, BF), "ID32": (128, F32),
-    "ID128": (128, BF), "IC1": (128, BF), "IC2": (128, BF), "DN": (128, F32), "D0": (128, BF), "ST": (2048, BF), "SEL": (768, BF),
-    "ZB": (144, BF), "Z32": (128, F32), "ZP": (272, BF), "POSB": (128, BF), "K16": (144, BF), "KT": (128, BF),
+    "IS1": (128, F16), "ID2K": (128, BF), "IDB": (128, BF), "NZ": (128, BF), "E1": (128, F32), "EV": (128, F32),
+    "ID": (128, BF), "IDN": (128, BF), "IDM": (128, BF), "ID32": (128, F32),
+    "BO8": (128, BF), "IC1": (128, F16), "IDE": (128, F32), "DN": (128, F32), "D0": (128, BF), "ST": (2048, BF), "SEL": (768, BF),
+    "ZB": (512, BF), "Z32": (128, F32), "ZP": (272, BF), "POSB": (128, BF), "K16": (144, BF), "KT": (128, F16),
 }
 SCRATCH = {n: ("sbuf", [128, w], d) for n, (w, d) in SB.items()}
 for _b in range(8):
     SCRATCH["P%d" % _b] = ("psum", [128, 512], F32)
-DMAS = ["dpo", "dpe", "dl0", "dl1", "dl2", "dl3", "dem", "dob", "dn0", "dn1", "dn2", "dxb", "dya", "dyz"]
-SEMAPHORES = (["qv", "qa", "qp", "qg", "loc", "pox", "ob1", "ob2", "fl0", "fl1", "cx0", "cx1"] + DMAS + ["rx%d" % h for h in range(5)]
+DMAS = ["dpo", "dpe", "dl0", "dl1", "dl2", "dem", "dob", "dn0", "dn1", "dn2", "dxb", "dya", "dyz"]
+SEMAPHORES = (["qv", "qa", "qp", "qg", "loc", "pox", "ob1", "ob2", "fl0", "fl1", "cx0", "cx1"] + DMAS + ["rx%d" % h for h in range(5)] + ["re%d" % h for h in range(5)]
               + ["fa%d" % h for h in range(NH)] + ["fb%d" % h for h in range(NH)])
-CYC, PEC, FIXV, FIXA, GAT, SCA, HOP, REM = 0.88, 0.44, 25.0, 25.0, 1.56, 3.8, 200.0, 2000.0
-OPT = {"born": "v", "gl": "v", "nm": "v", "ag": "a", "tbm": "a", "chf": [(0, 4), (4, 8), (8, 12), (12, 15)],
-       "chc": [(0, 4), (4, 8), (8, 12), (12, 14), (14, 15)], "stv": 8, "cl": "v",
-       "chg": [(0, 2), (2, 4), (4, 6), (6, 8), (8, 10), (10, 12), (12, 14), (14, 15)], "gorder": "ffcfccfcc"}
+CYC, PEC, FIXV, FIXA, FIXG, GAT, SCA, HOP, REM, PLAT = 0.85, 0.43, 15.0, 15.0, 60.0, 1.56, 3.8, 220.0, 1800.0, 0.0
+KINDS = ("first", "odd", "even", "last")
+OPT = {"late": 99, "pe1": 0, "pe2": 0, "nd": "a", "dg": "a", "nm": "a", "ag": "a", "tbm": "a", "stv": 12, "cl": "v",
+       "chf": {k: [(0, 4, "a"), (4, 8, "a" if k == "last" else "v"), (8, 12, "a"), (12, 15, "a")] for k in KINDS},
+       "chc": {k: [(0, 4, "a"), (4, 8, "a"), (8, 12, "a"), (12, 14, "a"), (14, 15, "a")] for k in KINDS},
+       "chi": {k: [(0, 4), (4, 8), (8, 12), (12, 14), (14, 15)] for k in KINDS},
+       "chg": [[(0, 4), (4, 8), (8, 12), (12, 15)], [(0, 2), (2, 4), (4, 6), (6, 8), (8, 10), (10, 12), (12, 14), (14, 15)]],
+       "chl": [(0, 4), (4, 8), (8, 12), (12, 15)], "lf": 8,
+       "zq": [[(0, 4, "a"), (4, 8, "a"), (8, 12, "a"), (12, 15, "a")], [(12, 15, "a"), (0, 4, "a"), (4, 8, "a"), (8, 11, "a"), (11, 12, "a")]],
+       "zp": [[(0, 4), (4, 8), (8, 12), (12, 16)], [(12, 16), (0, 4), (4, 8), (8, 11), (11, 12)]]}
 
 
 def bits(engines):
@@ -53,15 +60,21 @@ def helper_of(c, T, topo):
 def helper_program(g, core, owner, T, topo):
     rid, pid = topo.addr(owner, core)
     eng = topo.engines(core, owner)
-    for h in range(NH):
-        g.wait_ge(T.sem["fa%d" % h], len(eng) if h == NH - 1 else len(eng) // 2)
-        g.remote_dma(T.AC[:, h * 128:(h + 1) * 128], T.HB[:, h * 128:(h + 1) * 128], T.sem["fb%d" % h], T.sem.loc,
+    nf = NH if OPT["lf"] else NH - 1
+    for h in range(nf):
+        g.wait_ge(T.sem["fa%d" % h], len(eng) if h >= NH - 2 else len(eng) // 2)
+        g.remote_dma(T.AC[:, h * FW:(h + 1) * FW], T.HB[:, h * FW:(h + 1) * FW], T.sem["fb%d" % h], T.sem.loc,
                      pid, rid, bits(eng[len(eng) // 2:]))
-    g.wait_ge(T.sem.loc, NH * (len(eng) // 2))
+    g.wait_ge(T.sem.loc, nf * (len(eng) // 2))
 
 
 def hit(x, y):
     return x[1] < y[2] and y[1] < x[2]
+
+
+def soft(a, b):
+    return (a[0] == b[0] and a[0] in "va" and a[4] is None
+            and not any(x[0] == y[0] and hit(x, y) for u, w in ((a[3], b[2] + b[3]), (a[2], b[3])) for x in u for y in w))
 
 
 def depends(ops, banks):
@@ -174,7 +187,7 @@ def schedule(ops):
     return [ops[i] for i in ORDER[0][1]]
 
 
-def schedule(ops, turn):
+def schedule(ops, turn, edges):
     if ORDER:
         return [ops[i] for i in ORDER[0][1]]
     n = len(ops)
@@ -182,7 +195,9 @@ def schedule(ops, turn):
     for i in range(n):
         if ops[i][7] is not None:
             deps[i].add(ops[i][7])
-    suc = [[] for _ in range(n)]
+    for j, i in edges:
+        deps[i].add(j)
+    suc, margin = [[] for _ in range(n)], [0.0]
     for i in range(n):
         for j in deps[i]:
             suc[j].append(i)
@@ -194,7 +209,7 @@ def schedule(ops, turn):
         use.append(u)
 
     def lag(i, k):
-        return ops[i][5] + (0.0 if ops[k][0] == "p" == ops[i][0] else ops[i][6] + HOP)
+        return ops[i][5] + (0.0 if near[k][i] else ops[i][6] + HOP)
 
     def place(key, back):
         before, after = (suc, deps) if back else (deps, suc)
@@ -221,7 +236,7 @@ def schedule(ops, turn):
                         else:
                             hi = m
                     a = a0
-                    while lo < len(lst) and lst[lo][0] < a + d - 1e-6:
+                    while lo < len(lst) and lst[lo][0] < a + d + margin[0] - 1e-6:
                         if lst[lo][2] != ops[i][0] or r == ops[i][0]:
                             a = max(a, lst[lo][1])
                         lo += 1
@@ -249,27 +264,74 @@ def schedule(ops, turn):
                     ready.insert(lo, e)
         return t
 
-    chain = [0.0] * n
-    for i in reversed(range(n)):
+    def replay(order, f, hop, rem, call, gf):
+        end, free, bank = [0.0] * n, {}, {}
+        for i in order:
+            q = ops[i][0]
+            x = max([end[j] + (-ops[j][6] if near[i][j] else hop) for j in deps[i]] + [free.get(q, 0.0) if q != "x" else 0.0])
+            for r, d in use[i][1:]:
+                x = max([x] + [e + hop for q2, e in bank.get(r, {}).items() if q2 != q])
+            free[q] = x + ops[i][5] * f * (gf if byidx[i] else 1.0) + (call if q == "g" and ops[i][4] else 0.0)
+            end[i] = free[q] + ops[i][6] + (rem if q == "x" else 0.0)
+            for r, d in use[i][1:]:
+                bank.setdefault(r, {})[q] = end[i]
+        return max(end)
+
+    byidx = [o[0] in "va" and any(SCRATCH[r[0]][2] == U16 for r in o[2]) and not any(SCRATCH[r[0]][2] == F16 for r in o[3]) for o in ops]
+    near = [{j: ops[j][0] == ops[i][0] and (ops[i][0] in "ps" or ops[j][0] == "a" and not ops[j][2]) or soft(ops[j], ops[i])
+             for j in deps[i]} for i in range(n)]
+    left, topo_order = [len(d) for d in deps], [i for i in range(n) if not deps[i]]
+    for i in topo_order:
+        for k in suc[i]:
+            left[k] -= 1
+            if not left[k]:
+                topo_order.append(k)
+    assert len(topo_order) == n, "the named order contradicts the calls' needs"
+    chain, step = [0.0] * n, list(turn)
+    for i in reversed(topo_order):
         chain[i] = max([chain[k] + lag(i, k) for k in suc[i]] + [ops[i][5] + ops[i][6]])
-    key = list(turn)
-    for i in reversed(range(n)):
-        key[i] = min([key[i]] + [key[k] for k in suc[i]])
-    key, best = [(key[i], -chain[i]) for i in range(n)], None
-    for it in range(ROUNDS):
-        t = place(key, False)
-        end = max(t[i] + ops[i][5] + ops[i][6] for i in range(n))
-        if best is None or end < best[0]:
-            best = (end, sorted(range(n), key=lambda i: (t[i], i)), it)
-        key = [-x for x in place([-(t[i] + ops[i][5]) for i in range(n)], True)]
+        step[i] = min([step[i]] + [step[k] for k in suc[i]])
+    best = None
+    for kind, room in TRY:
+        margin[0] = room
+        key = [(step[i] if kind else 0, -chain[i]) for i in range(n)]
+        for it in range(ROUNDS):
+            t = place(key, False)
+            order = sorted(range(n), key=lambda i: (t[i], i))
+            end = sum(replay(order, *m) for m in MACHINES) / len(MACHINES)
+            if best is None or end < best[0]:
+                best = (end, order, kind, room, it)
+            if it < ROUNDS - 1:
+                key = [-x for x in place([-(t[i] + ops[i][5]) for i in range(n)], True)]
     ORDER.append(best)
     return [ops[i] for i in best[1]]
 
 
+TRY = [(0, 0.0), (1, 0.0)]
+MACHINES = [(1.0, 220.0, 0.0, 0.0, 1.0), (1.3, 30.0, 0.0, 0.0, 0.75), (1.2, 40.0, 0.0, 0.0, 1.1), (1.3, 220.0, 800.0, 300.0, 1.2)]
+
+
 ORDER = []
-ROUNDS = 4
+ROUNDS = 3
+LINE = {
+    "v": {"start": "ZB PI PI AB PC BO RM ST ST ST ST ST ST ST ST ST ST ST ST LU L16 CW CW INI CW TB CW TB TB TB",
+          "even": "RX TT TT NL WT F CL CB PW U2 PW XW PW IW XW PW IW XW XW IW XW IW IW OF EV "
+                  "SW SE SV ASK CUM E OFU HIT ZZ XX IDX NN YY G E IDX NN GL TB SU TB PK",
+          "odd": "TT TT NL WT F CL PW CB RX U2 PW PW XW XW IW PW IW XW XW IW XW IW IW EV OF "
+                 "SW SE SV ASK OFU CUM HIT ZZ XX YY IDX G NN IDX GL NN SU TB TB",
+          "last": "TT TT NL WT -PR CL CB PW -PR U2 -PR PW PW XW IW XW PW IW -PR XW XW IW XW IW IW EV "
+                  "SW SE SV ASK CUM HIT ZZ XX IDX YY NN G GL NN TB SU TB",
+          "end": "-PR -PR TT TT NL WB TT TT -PR NL PZ WB -PR PZ PZ PZ PZ PZ PZ PZ PZ YA"},
+    "a": {"start": "PC ST ST ST ST",
+          "even": "AB DG AB ZZ P0 GT F CW F SG CW F CW CW CW E NZ ES JK ND AQ JK IAC P3 GH",
+          "first": "EA EA EA EA EA EA EA EA EQ EQ AB AB ZZ DG P0 GT F F CW SG CW F NZ CW CW CW E ES JK ND AQ JK P3 IAC GH",
+          "odd": "-KB AB DG ZZ EA P0 EA EA EA EA F GT CW EA EA EA EQ F EQ CW SG F CW CW CW E NZ ES JK ND AQ JK P3 IAC GH",
+          "last": "AB DG ZZ -KB P0 EA EA EA EA EA F GT F EA EA EA EQ F SG EQ CW CW F NZ CW CW CW E ES JK ND AQ JK P3 IAC GH",
+          "end": "AB AB ZZ P2 ZZ P3 FA FA -PR FA FA PW PW PW PW PW -YA YZ YZ"}}
+LINE["v"]["first"] = LINE["v"]["even"]
+KIND = {-9: "start", 0: "first", 1: "odd", 2: "even", 3: "odd", 4: "even", 5: "last", 6: "end"}
 STEP = {"names": 0, "d": 1, "f0": 2, "fit": 3, "f1": 4, "slice": 5, "gather": 6, "test": 7, "side": 8, "first": 8.5, "draw": 9,
-        "g": 9.5, "repeats": 100.5, "sums": 107.5, "hit": 9.1, "kb": 101.5, "list": 8.5, "const": 50, "late": 90}
+        "g": 9.5, "repeats": 100.5, "sums": 109.8, "sums1": 109.8, "hit": 9.1, "early": 9.2, "kb": 101.5, "list": 8.5, "const": 50, "late": 90}
 
 
 def rank_program(g, core, T, topo):
@@ -280,7 +342,7 @@ def rank_program(g, core, T, topo):
                 helper_program(g, core, c, T, topo)
         return
     N = len(T.cores)
-    turn, now = [], [0]
+    turn, now, edges, named = [], [0, -9], [], {}
     ops = []
 
     def s(n, a=0, b=None, st=1, rows=128):
@@ -300,19 +362,24 @@ def rank_program(g, core, T, topo):
             rd += x[2]
         ops.append((q, fn, rd, wr, tok, c, lat, aft))
         turn.append(now[0])
+        if q in "va" and outs[0][1]:
+            x = outs[0][1][0][0]
+            named.setdefault((now[1], q, x if SCRATCH[x][0] == "psum" else x.rstrip("01")), []).append(len(ops) - 1)
         return len(ops) - 1
 
     def at(h, step):
         now[0] = 100 * h + STEP[step]
+        now[1] = -9 if step == "const" else h
 
     def v(x):
         return x[0] if isinstance(x, tuple) else x
 
-    def cost(o, a, f=1.0, fix=FIXV):
+    def cost(o, a, f=1.0, fix=None):
+        fix = FIXV if fix is None else fix
         if o[2]:
-            return fix + o[3] * SCA * CYC
+            return FIXG + o[3] * SCA * CYC
         if a[2]:
-            return fix + o[3] * GAT * CYC
+            return FIXG + o[3] * GAT * CYC
         return fix + max(64, o[3] * f) * CYC
 
     def half(*x):
@@ -320,17 +387,16 @@ def rank_program(g, core, T, topo):
 
     def tt(o, a, b, op):
         f = 1.0 if "psum" in (SCRATCH[a[1][0][0]][0], SCRATCH[b[1][0][0]][0]) else 2.0
-        rec("v", lambda: g.vector.tensor_tensor(o[0], a[0], b[0], op), [o], [a, b], cost(o, a, f))
+        return rec("v", lambda: g.vector.tensor_tensor(o[0], a[0], b[0], op), [o], [a, b], cost(o, a, f))
 
     def ts(o, a, s1, op0, s2=None, op1=None):
         if op1 is None:
-            rec("v", lambda: g.vector.tensor_scalar(o[0], a[0], v(s1), None, op0), [o], [a, s1], cost(o, a, half(o, a)))
-        else:
-            rec("v", lambda: g.vector.tensor_scalar(o[0], a[0], v(s1), v(s2), op0, op1), [o], [a, s1, s2],
-                cost(o, a, half(o, a)))
+            return rec("v", lambda: g.vector.tensor_scalar(o[0], a[0], v(s1), None, op0), [o], [a, s1], cost(o, a, half(o, a)))
+        return rec("v", lambda: g.vector.tensor_scalar(o[0], a[0], v(s1), v(s2), op0, op1), [o], [a, s1, s2],
+                   cost(o, a, half(o, a)))
 
     def cp(o, a):
-        rec("v", lambda: g.vector.tensor_copy(o[0], a[0]), [o], [a], cost(o, a, half(o, a)))
+        return rec("v", lambda: g.vector.tensor_copy(o[0], a[0]), [o], [a], cost(o, a, half(o, a)))
 
     def ms(o, c):
         rec("v", lambda: g.vector.memset(o[0], c), [o], [], cost(o, o, half(o)))
@@ -353,12 +419,11 @@ def rank_program(g, core, T, topo):
         (act if q == "a" else cp)(o, a)
 
     def mm(o, l, r, st, sp):
-        rec("p", lambda: g.tensor.matmul(o[0], l[0], r[0], st, sp), [o], [l, r],
-            max(64, r[3]) * PEC * (4 if SCRATCH[r[1][0][0]][2] == F32 else 1), None, 60.0)
+        return rec("p", lambda: g.tensor.matmul(o[0], l[0], r[0], st, sp), [o], [l, r],
+                   max(64, r[3]) * PEC * (4 if SCRATCH[r[1][0][0]][2] == F32 else 1), None, PLAT)
 
     def group(o, pairs):
-        for i, (l, r) in enumerate(pairs):
-            mm(o, l, r, i == 0, i == len(pairs) - 1)
+        return [mm(o, l, r, i == 0, i == len(pairs) - 1) for i, (l, r) in enumerate(pairs)]
 
     def iota(o, pat, base, cm, fl=True):
         if fl:
@@ -367,10 +432,10 @@ def rank_program(g, core, T, topo):
             rec("g", lambda: g.iota(o[0], pat, base, cm), [o], [], 130 + 2 * CYC * o[3])
 
     def sel(o, a, pat, op, fill, base, cm, more=()):
-        rec("g", lambda: g.affine_select(o[0], a[0], pat, op, fill, base, cm), [o], [a] + list(more), 170 + 2 * CYC * o[3])
+        return rec("g", lambda: g.affine_select(o[0], a[0], pat, op, fill, base, cm), [o], [a] + list(more), 170 + 2 * CYC * o[3])
 
     def gcopy(o, a):
-        sel(o, a, [[0, o[3]]], ALU.is_ge, 0.0, 0, 0)
+        return sel(o, a, [[0, o[3]]], ALU.is_ge, 0.0, 0, 0)
 
     def diag(o, a, c, off=0):
         sel(o, a, [[-1, 128]], ALU.not_equal, c, -off, 1)
@@ -387,6 +452,7 @@ def rank_program(g, core, T, topo):
         nloc[0] += len(eng)
         i = rec("g", lambda: g.remote_dma(o[0], a[0], T.sem[sem], T.sem.loc, pid, rid, bits(eng)), [], [a], c, ("loc", 0))
         rec("x", None, [o], [], 0.0, (sem, len(topo.engines(src, core)[:8])), REM, i)
+        return i
 
     prv, nxt = T.cores[(rank - 1) % N], T.cores[(rank + 1) % N]
     hlp = helper_of(core, T, topo)
@@ -394,31 +460,34 @@ def rank_program(g, core, T, topo):
     nfold = [0, 0]
 
     def fold(h):
-        heng = hall if h == NH - 1 else hall[len(hall) // 2:]
+        heng = hall if h >= NH - 2 else hall[len(hall) // 2:]
         pr = "PR%d" % (h & 1)
-        src = [s(pr, k * 128, (k + 1) * 128) for k in range(16)]
+        src = [s(pr, k * 128, k * 128 + FW) for k in range(0, OPT["lf"] if h == NH - 1 else 16, FW // 128)]
         if h >= 2:
-            src.append(s("AC", (h - 2) * 128, (h - 1) * 128))
+            src.append(s("AC", (h - 2) * FW, (h - 1) * FW))
         rid, pid = topo.addr(hlp, core)
         nfold[h & 1] += len(heng)
         t = RemoteDMATransfer(dst_ids=[DstId(rid=rid, pnc=pid)], dma_engine_mask=bits(heng), remote_sem=T.sem["fa%d" % h],
-                              srcs=[x[0] for x in src], dsts=[T.HB[:, h * 128:(h + 1) * 128]], alu_op=1)
+                              srcs=[x[0] for x in src], dsts=[T.HB[:, h * FW:(h + 1) * FW]], alu_op=1)
         i = rec("g", lambda: g.remote_dma_fused([t], local_sem=T.sem["fl%d" % (h & 1)]), [], src, 300.0,
-                ("fl%d" % (h & 1), nfold[h & 1]), 5000.0)
-        rec("x", None, [s("AC", h * 128, (h + 1) * 128)], [], 0.0, ("fb%d" % h, len(hall) // 2), 2500.0, i)
+                ("fl%d" % (h & 1), nfold[h & 1]), 1200.0 + 20.0 * FW * len(src) / len(heng))
+        rec("x", None, [s("AC", h * FW, (h + 1) * FW)], [], 0.0, ("fb%d" % h, len(hall) // 2), 2300.0 + 2 * FW, i)
+        return i
 
     def dr(t):
         return (t, [], [], 0)
 
     add, sub, mul, mx, mn = ALU.add, ALU.subtract, ALU.mult, ALU.max, ALU.min
     MAG, MG1 = 1.5 * 2.0 ** 31, 1.5 * 2.0 ** 23
-    dma("s", s("PEPO", 8, 16), dr(T.po[:]), "dpo", 1900.0)
-    for c in range(4):
-        dma("s", s("LK", c * 512, (c + 1) * 512), dr(T.lk[:, c * 512:(c + 1) * 512]), "dl%d" % c, 2200.0 + 400 * c)
-    dma("s", s("EM"), dr(T.em[:]), "dem", 4300.0)
-    dma("a", s("PEPO", 0, 8), dr(T.pe[:]), "dpe", 1900.0)
-    dma("s", s("OB", 0, 256), dr(T.ob[:]), "dob", 4400.0)
+    dma("a", s("PEPO", 8, 16), dr(T.po[:]), "dpo", 1700.0)
+    dma("a", s("PEPO", 0, 8), dr(T.pe[:]), "dpe", 1700.0)
+    for c, (a, b) in enumerate(((0, 512), (512, 1024), (1024, 2048))):
+        dma("s", s("LK", a, b), dr(T.lk[:, a:b]), "dl%d" % c, 1650.0 + 0.8 * b)
+    dma("s", s("EM"), dr(T.em[:]), "dem", 4100.0)
     for i, t in enumerate((T.nub, T.nua, T.vd)):
+        if i == 2:
+            dma("s", s("OB", 0, 256), dr(T.ob[:]), "dob", 4400.0)
+            dma("s", s("XR", rows=1), dr(T.xb[:, 0]), "dxb", 4400.0)
         dma("s", s("RN", i * 128, (i + 1) * 128, rows=48), dr(t[:]), "dn%d" % i, 4500.0)
 
     def pc(i):
@@ -432,9 +501,11 @@ def rank_program(g, core, T, topo):
 
     at(0, "const")
     ZB, ID, ID32, IDN, IDM, BO = s("ZB", 0, 128), s("ID"), s("ID32"), s("IDN"), s("IDM"), s("BO")
-    for n in ("ZB", "Z32", "ZS", "Z1", "AB", "ZP"):
+    ms(s("ZB", 0, 144), 0.0)
+    k16 = act(s("K16"), s("ZB", 0, 144), AF.Exp, bias=math.log(16.0), more=1300.0)
+    ms(s("ZB", 144, 512), 0.0)
+    for n in ("Z32", "ZS", "Z1", "AB", "ZP"):
         ms(s(n), 0.0)
-    act(s("K16"), s("ZB"), AF.Exp, bias=math.log(16.0), more=1300.0)
     iota(s("PI", 0, 1), [[0, 1]], 0, 1, False)
     iota(s("COLG"), [[1, 8], [0, 16]], 0, 0)
     iota(s("COLK"), [[1, 16]], 0, 0)
@@ -444,9 +515,13 @@ def rank_program(g, core, T, topo):
     cp(s("LU", 8, 16), s("PEPO", 0, 8))
     cp(s("L16", 0, 16), s("PEPO"))
     diag(ID32, s("Z32"), 1.0)
-    for n, c in (("IDM", -512.0), ("ID", 1.0), ("IDN", -1.0), ("ID128", 128.0), ("IC1", 2832.0), ("IC2", 7.125),
-                 ("IS1", -3456.0), ("IS2", -11.5625), ("ID2K", 2048.0), ("IDB", 65536.0)):
+    for n, c in (("IDM", -512.0), ("ID", 1.0)):
         diag(s(n), ZB, c)
+    diag(s("IDE"), s("Z32"), 1143 / (4096 * math.log(2.0)))
+    for n, c in (("IC1", 1143.0), ("IS1", -1396.0)):
+        ts(s(n), ID, c, mul)
+    for n, c in (("IDN", -1.0), ("ID2K", 2048.0), ("IDB", 65536.0)):
+        act(s(n), ID, scale=c)
     p0 = s("PI", 0, 1)
     ts(s("PI", 1, 2), p0, 15, ALU.bitwise_and)
     ts(s("PI", 2, 3), p0, 4, ALU.arith_shift_right)
@@ -454,7 +529,8 @@ def rank_program(g, core, T, topo):
     ts(s("PI", 4, 5), p0, 3, ALU.arith_shift_right, 1, ALU.bitwise_and)
     tt(s("PI", 5, 6), p0, s("PI", 2, 3), add)
     ts(s("PI", 6, 7), s("PI", 5, 6), 1, ALU.bitwise_and)
-    cp(s("PC", 0, 7), s("PI", 0, 7))
+    cp(s("PC", 1, 3), s("PI", 1, 3))
+    cp(s("PC", 3, 7), s("PI", 3, 7))
     ts(BO, s("COLG"), pc(2), ALU.is_equal)
     ts(s("RM"), s("COLK"), pc(1), ALU.is_equal)
     for k in range(16):
@@ -465,7 +541,7 @@ def rank_program(g, core, T, topo):
     ts(pc(7), pc(6), 144.0, mul, pc(4), add)
     ts(pc(8), pc(3), 16.0, mul, pc(7), add)
     ts(s("PERM"), s("C2"), pc(8), add)
-    ts(pc(9), rm(15), 2.0 ** 20, mul, -MAG, add)
+    act(pc(9), rm(15), bias=-MAG, scale=2.0 ** 20)
     act(pc(10), pc(1), bias=0.5)
     act(pc(11), rm(0), bias=1.0, scale=-1.0)
     act(pc(12), rm(0), scale=128.0)
@@ -473,29 +549,30 @@ def rank_program(g, core, T, topo):
     act(pc(20), rm(15), bias=1.0, scale=-1.0)
     act(pc(21), rm(15), bias=-1.0)
     act(pc(14), rm(15), bias=-16.0, scale=16.0)
-    act(pc(15), pc(1), bias=31.0, scale=16.0)
-    act(pc(16), rm(15), bias=pc(15), scale=1649.0)
+    act(pc(16), pc(1), bias=S0 - 1.0, scale=16.0)
     act(pc(17), pc(1), scale=1.0 / 256)
     act(pc(18), rm(0), scale=512.0)
     act(pc(19), rm(14), scale=-1.0)
-    for a in (0, 136):
-        act(s("ZP", a, a + 8), s("C2"), bias=pc(17), scale=1.0 / 32)
+    act(s("ZP", 136, 144), s("C2"), bias=pc(17), scale=1.0 / 32)
     iota(s("POSB"), [[2, 128]], -128, 0)
     ts(s("ZP", 144, 272), s("POSB"), 1.0 / 512, mul)
-    for a in (0, 144, 288):
+    for a in (144, 288):
         ms(s("CR", a, a + 8), 0.0)
     for c in range(4):
         a, b = c * 512, (c + 1) * 512
+        bk = s(("P4", "P5", "P0", "P1")[c])
         ts(s("CW", a, b), s("LK", a, b), -128.0, add, MAG, add)
-        act(s("P%d" % (4 + (c & 1))), s("CW", a, b), bias=pc(9))
-        tt(s("TB", a, b), s("LK", a, b), s("P%d" % (4 + (c & 1))), add)
+        act(bk, s("CW", a, b), bias=pc(9))
+        tt(s("TB", a, b), s("LK", a, b), bk, add)
     for r in range(16):
         mm(s("P6", r, 256, 16), st(r), s("L16", 0, 16), True, True)
     cp(s("INI"), s("P6", 0, 256))
     cp(s("L16", 16, 18), s("LU", 22, 24))
-    for i, c in enumerate((1.0, -1.0, -1.0) if OPT["cl"] == "a" else (-1.0, 1.0, -1.0)):
+    ms(s("E0"), 0.0)
+    for i, c in enumerate((-1.0, 1.0, -1.0)):
         ts(s("RB", i * 128, (i + 1) * 128, rows=48), s("RN", i * 128, (i + 1) * 128, rows=48), c / 256, mul)
-    dma("g", s("XB"), dr(T.xb[:]), "dxb", 2500.0, 1000.0, allow_slow_non_contiguous=True)
+    mm(s("P3", 1, 2), s("XR", rows=1), s("ID", 0, 1, rows=1), True, True)
+    act(s("XB"), s("P3", 1, 2))
     gcopy(s("ZS", 15, 143, 16), s("BO", 0, 128, 16))
     gcopy(s("Z1", 15, 143, 16), s("ST", 0, 128, 16))
     act(s("ZX"), s("ZS", 0, 128), scale=s("XB"))
@@ -514,19 +591,19 @@ def rank_program(g, core, T, topo):
     ts(s("L14"), ID, pc(19), mul)
     ts(s("D0"), ID, pc(18), mul)
     act(s("DN"), ID32, scale=pc(11))
-    sel(s("S2K"), ZB, [[-16, 8], [0, 16]], ALU.not_equal, -2048.0, -15, 1)
+    act(s("S2K"), st(15), scale=-2048.0)
     ts(s("XBN"), BO, s("XB"), mul, -1.0, mul)
     ts(s("ZH"), s("ZS"), 4096.0, mul)
     ts(s("D16"), ID, pc(20), mul, 1.0 / 16, mul)
     ms(s("AQ", 128, 144), 0.0)
-    for h in range(NH):
-        sel(s("SEL", h * 128, (h + 1) * 128), ZB, [[-NH, 8], [0, 16]], ALU.not_equal, 1.0, -h, 1)
-    act(s("KT"), ZB, bias=pc(16))
+    ts(s("KT"), ZB, pc(16), add)
     iota(s("DUM"), [[2, 128]], H, 0)
     iota(s("CV"), [[512, 96]], 512 * S0 + 128, 0)
     act(s("ASK", 128, 144), s("RM"), scale=16.0)
-    for f in ("FA", "FB"):
-        act(s(f, 1920, 2048), ZB, bias=s("XB"))
+    act(pc(22), s("XB"), bias=-8.0)
+    for f in ("FA", "PW"):
+        act(s(f, 1920, 2048), ZB, bias=pc(22))
+    ts(s("BO8"), BO, 8.0, mul)
     ts(s("BM", 0, 8), s("COLK", 0, 8), pc(1), ALU.is_equal)
     gcopy(s("BM", 8, 16), s("BM", 0, 8))
     ms(s("CUM", 0, 1), 0.0)
@@ -539,7 +616,7 @@ def rank_program(g, core, T, topo):
 
     def names(lst, a, par, q):
         a0, t0 = 176 * par, 288 * par
-        mv(q, s("AB", a0 + a, a0 + 160 + (a & 1)), ind(TBW, lst))
+        mv(q, s("AB", a0 + a, a0 + a + 128), ind(TBW, lst))
         tr(s("TT", t0, t0 + 128), s("AB", a0 + 32, a0 + 160))
         tr(s("TT", t0 + 128, t0 + 288), s("AB", a0 + 16, a0 + 176))
         ts(s("NL", 128 * par, 128 * par + 128), ind(s("TT", t0, t0 + 288), s("PERM")), 1.0 / 512, mul)
@@ -552,8 +629,8 @@ def rank_program(g, core, T, topo):
         if OPT["nm"] == "v":
             ts(P, A, 2 * MAG, add, 2 * MAG, sub)
         else:
-            act(s("NM"), A, bias=2 * MAG)
-            act(P, s("NM"), bias=-2 * MAG)
+            act(s("ZZ"), A, bias=2 * MAG)
+            act(P, s("ZZ"), bias=-2 * MAG)
         tt(o, A, P, sub)
 
     CNT = s("P6", 0, 128)
@@ -563,13 +640,14 @@ def rank_program(g, core, T, topo):
             act(s("EA", pos[c], pos[c + 1]), s("P7", 384 + 16 * c, 512), AF.Abs, bias=s("KB", k0 + c, k0 + c + 1), scale=-512.0)
         for a, b in ((0, 3), (3, 8)):
             act(s("EQ", pos[a], pos[b]), s("EA", pos[a], pos[b]), AF.Relu, bias=128.0, scale=-1.0)
-        counts(0, True, stop)
+        if stop is not None:
+            counts(0, True, stop)
 
     pos = [sum(128 - 16 * x for x in range(c)) for c in range(9)]
 
-    def counts(a, start, stop):
+    def counts(a, start, stop, shift=0):
         for c in range(8):
-            mm(s("P6", a + 16 * c, a + 128), s("BO4"), s("EQ", pos[c], pos[c + 1]), start and c == 0, stop and c == 7)
+            mm(s("P6", a + 16 * c + shift, a + 128), s("BO4"), s("EQ", pos[c], pos[c + 1] - shift), start and c == 0, stop and c == 7)
 
     def targets(h):
         tt(s("OF"), s("DUM"), CNT, mn)
@@ -578,11 +656,13 @@ def rank_program(g, core, T, topo):
             mm(s("P6", 128, 136), s("Z1", 15 - r, 143 - r), s("OF", r, 128, 16), r == 0, r == 15)
         cp(s("OFU", 8 * (h & 1), 8 * (h & 1) + 8), s("P6", 128, 136))
 
-    mm(s("P7", 240, 512), ID, s("ZP"), True, False)
+    sent, folds = {}, {}
+    mm(s("P7", 248, 512), ID, s("ZP", 8, 272), True, False)
     mm(s("P7", 376, 384), ID, s("L16", 8, 16), False, False)
-    mm(s("P7", 375, 376), st(15), s("L16", 17, 18), False, False)
     mm(s("P7", 384, 512), ID, s("INI", 128, 256), False, True)
-    act(s("KB", 0, 9), s("P7", 375, 384), scale=512.0)
+    act(s("KB", 1, 9), s("P7", 376, 384), scale=512.0)
+    mm(s("P3", 0, 1), st(15), s("L16", 17, 18), True, True)
+    act(s("KB", 0, 1), s("P3", 0, 1), scale=512.0)
 
     for h in range(NH):
         w, par = h >> 1, h & 1
@@ -591,99 +671,111 @@ def rank_program(g, core, T, topo):
         y0 = 144 * h
         at(h, "names")
         Y = s("YS", y0, y0 + 128)
-        gcopy(Y, s("OB", w * 256 + par, (w + 1) * 256, 2))
-        gcopy(s("YS", y0 + 128, y0 + 144), s("EM", m0, m0 + 16))
+        mine = [gcopy(Y, s("OB", w * 256 + par, (w + 1) * 256, 2)), gcopy(s("YS", y0 + 128, y0 + 144), s("EM", m0, m0 + 16)),
+                sel(s("SEL", h * 128, (h + 1) * 128), ZB, [[-NH, 8], [0, 16]], ALU.not_equal, 1.0, -h, 1)]
+        if h > 1:
+            edges.extend((sent[h - 2], i) for i in mine)
         r1, r2, k1, k0 = (h - 1) * SL, (h - 2) * SL, (h - 1) * SL, h * SL
-        if par == 0:
-            if h:
-                sa, sl, qa = s("RX", r2 + 16, r2 + 144), s("RX", r2 + 8, r2 + 16), s("RX", r1 + 8, r1 + 136)
-                lr = s("RX", r1 + 8, r1 + 135)
-                cp(s("LU", (h + 1) * 16 + 8, (h + 2) * 16), s("RX", r1 + 136, r1 + 144))
-                A = names(s("LU", (h + 1) * 16 + 6, (h + 2) * 16), 1, par, OPT["ag"])
-            else:
-                sa, sl, qa, lr = s("INI", 0, 128), s("L16", 0, 8), s("INI", 128, 256), s("INI", 128, 255)
-                cp(s("AB", 177, 337), ind(s("LK"), s("LU", 22, 32)))
-                tr(s("TT", 0, 128), s("AB", 208, 336))
-                tr(s("TT", 128, 288), s("AB", 192, 352))
-                ts(s("NL", 0, 128), ind(s("TT", 0, 288), s("PERM")), 1.0 / 256, mul, -0.498, add)
-                act(s("AB", 1, 161), ind(TBW, s("LU", 22, 32)))
-                A = s("AB", 32, 160)
+        if h > 1:
+            sa, sl, su, s0 = s("RX", r2, r2 + 128), s("RX", r2 + 128, r2 + 136), s("RU", r2 + 128, r2 + 136), s("RX", r2, r2 + 1)
         else:
-            if h > 1:
-                sa, sl = s("RX", r2 + 8, r2 + 136), s("RX", r2 + 136, r2 + 144)
-            else:
-                sa, sl = s("INI", 128, 256), s("L16", 8, 16)
-            qa = s("PK", k1 + 17, k1 + 145)
-            A = names(s("PU", 8 * h - 8, 8 * h), 32, par, OPT["ag"])
-            at(h, "d")
-            cp(s("PK", k1 + 144, k1 + 145), s("RX", r1 + 16, r1 + 17))
-            if h < NH - 1:
-                at(h, "side")
-                cp(s("LU", (h + 1) * 16 + 8, (h + 2) * 16), s("RX", r1 + 8, r1 + 16))
+            sa, sl, su = s("INI", 128 * h, 128 * h + 128), s("L16", 8 * h, 8 * h + 8), s("LU", 16 * h + 8, 16 * h + 16)
+            s0 = s("INI", 0, 1)
+        if par == 0:
+            act(s("AB", 1, 33), ind(TBW, s("SU", k1 + 134, k1 + 136) if h else s("LU", 22, 24)))
+            A = names(s("RU", r1 + 128, r1 + 136) if h else s("LU", 24, 32), 33, par, OPT["ag"])
+            qa, lr = ([(0, 128, s("RX", r1, r1 + 128))], s("RX", r1, r1 + 127)) if h else ([(0, 128, s("INI", 128, 256))], s("INI", 128, 255))
+        else:
+            qa = [(0, 127, s("PK", k1 + 1, k1 + 128)), (127, 128, s("R0", 4 * h - 4, 4 * h - 3))]
+            A = names(s("SU", k1 + 128, k1 + 136), 32, par, OPT["ag"])
+        if 0 < h < NH - 1:
+            at(h, "side" if par else "d")
+            cp(s("RX", r1, r1 + 136), s("RU", r1, r1 + 136))
         at(h, "d")
         for r in range(4):
             mm(s("P1", r * 128, (r + 1) * 128), ID, Y, True, True)
-        left, aft = {"f": list(OPT["chf"]), "c": list(OPT["chc"])}, None
-        for n, x in enumerate(OPT["gorder"]):
-            at(h, ("f0", "f1", "gather")[min(n, 2)])
-            a, b = left[x].pop(0)
-            aft = gat(F, s("EM"), a, b, par, 0.0, aft) if x == "f" else gat("CW", TBW, a, b, par, 34431.5, aft)
+        chf, chc, chi = (OPT[x][KIND[h]] for x in ("chf", "chc", "chi"))
+        at(h, "gather")
+        for a, b, q in chf:
+            mv(q, s(F, a * 128, b * 128), ind(s("EM"), s("NL", 128 * par + a * 8, 128 * par + b * 8)))
+        for a, b, q in chc:
+            if q == "a":
+                gat("CW", TBW, a, b, par, 34431.5)
         at(h, "d")
         SEL = s("SEL", h * 128, (h + 1) * 128, rows=48)
-        mm(s("P0", 0, 256), SEL, s("RB", 0, 256, rows=48), True, True)
-        act(s("DG"), ind(TBW, s("LU", h * 16 + 8, h * 16 + 16)))
+        mm(s("P2", 256, 512), SEL, s("RB", 0, 256, rows=48), True, True)
+        mv(OPT["dg"], s("DG"), ind(TBW, su))
+
+        def withq(bank, a, l, stop):
+            for n, (x, y, q) in enumerate(qa):
+                mm(s(bank, a + x, a + y), l, q, False, stop and n == len(qa) - 1)
+
         at(h, "fit")
+        weights(s("WT"), A, s("P0", 256, 384))
         group(s("P6", 384, 512), [(IDM, sa), (ID32, A)])
-        group(s("P6", 256, 384), [(ID32, s("DG")), (IDM, qa)])
+        mm(s("P6", 256, 384), ID32, s("DG"), True, False)
+        withq("P6", 256, IDM, True)
         act(s("GT"), s("P6", 256, 512), AF.Abs, bias=-256.0)
-        if OPT["cl"] == "a":
-            act(s("CL"), s("GT"), AF.Relu, bias=256.0, scale=-1.0)
-        else:
-            ts(s("CL"), s("GT"), 256.0, mn, -256.0, add)
-        at(h, "slice")
-        weights(s("WT"), A, s("P0", 384, 512))
-        tt(s("CB"), s("CL"), s("P0", 0, 256), mul)
-        mm(s("P0", 256, 384), s("BO32"), s("CB", 0, 128), True, True)
-        ts(s("U2"), s("P0", 256, 384), 255.0, mn, 1535.502, add)
+        ts(s("CL"), s("GT"), 256.0, mn, -256.0, add)
+        tt(s("CB"), s("CL"), s("P2", 256, 512), mul)
+        mm(s("P2", 0, 128), s("BO32"), s("CB", 0, 128), True, True)
+        ts(s("U2"), s("P2", 0, 128), 255.0, mn, 1535.502, add)
+        mm(s("P0"), ID, s("ZB"), True, False)
         for r in range(4):
-            group(s("P0", r * 128, (r + 1) * 128), [(IDM, qa), (IDN, s("U2"))])
-        at(h, "side")
+            withq("P0", r * 128, IDM, False)
+        for r in range(4):
+            mm(s("P0", r * 128, (r + 1) * 128), IDN, s("U2"), False, r == 3)
+        at(h, "slice")
         group(s("P6", 256, 384), [(ID, s("WT")), (s("BO32"), s("CB", 128, 256))])
         act(s("SG"), s("P6", 256, 384), AF.Sign, bias=-1.0 / 512)
-        group(s("P6", 384, 512), [(s("D0"), qa), (s("DN"), A)])
-        act(s("AQ", 0, 128), s("P6", 384, 512), bias=pc(12))
-        ts(s("ND"), s("WT"), -255.0, add, pc(14), mx)
+        at(h, "side")
+        mm(s("P6", 384, 512), s("DN"), A, True, False)
+        withq("P6", 384, s("D0"), True)
+        if OPT["nd"] == "v":
+            ts(s("ND"), s("WT"), -255.0, add, pc(14), mx)
+        else:
+            act(s("JK", 0, 128), s("WT"), AF.Relu, bias=-239.0)
+            act(s("ND"), s("JK", 0, 128), bias=pc(14), scale=pc(20))
         group(s("P2", 128, 256), [(s("L14"), sa), (s("DT32"), A), (s("DTN"), s("WT"))])
+        TZ = s("P2", 256, 384)
+        group(TZ, [(st(h), s("KT")), (IDN, sa)])
         at(h, "first")
         if par == 0:
-            if h == 0:
-                repeats(1, True)
-                act(s("CR", 8, 136), CNT)
             kb = 16 * h
             ts(s("EQ0", 1, 128), lr, 512.0, mul, s("KB", kb, kb + 1), ALU.is_equal)
-            mm(CNT, ID, s("CR", 144 * w + 7, 144 * w + 135), True, False)
+            if h:
+                mm(CNT, ID, s("CR", 144 * w + 7, 144 * w + 135), True, False)
+            else:
+                mm(CNT, ID, ZB, True, False)
+                repeats(1, None)
+                counts(0, False, False, 1)
             mm(s("P6", 1, 128), ID, lr, False, False)
             if h:
-                mm(s("P6", 0, 1), ID, s("PK", k1 + 135, k1 + 136), False, False)
+                mm(s("P6", 0, 1), ID, s("PK", k1, k1 + 1), False, False)
             else:
                 mm(s("P6", 0, 1), st(15), s("L16", 17, 18), False, False)
             mm(s("P6", 1, 128), s("BO4"), s("EQ0", 1, 128), False, True)
         else:
             repeats(16 * h + 1, False)
-            mm(CNT, ID, s("PK", k1 + 16, k1 + 144), False, True)
+            mm(CNT, ID, s("PK", k1, k1 + 128), False, True)
         mm(s("P6", 256, 384), s("XBN"), Y, True, False)
         if par == 0:
-            mm(s("P6", 256, 384), ID, s("CR", 144 * w + 7, 144 * w + 135), False, False)
+            if h:
+                mm(s("P6", 256, 384), ID, s("CR", 144 * w + 7, 144 * w + 135), False, False)
+            else:
+                counts(256, False, False, 1)
             mm(s("P6", 257, 384), s("BO4"), s("EQ0", 1, 128), False, False)
         else:
             counts(256, False, False)
         mm(s("P6", 256, 384), s("S2K"), s("SG"), False, True)
         act(s("NZ"), s("P6", 256, 384), AF.Relu, bias=2049.0)
         targets(h)
+        at(h, "side")
+        act(s("AQ", 0, 128), s("P6", 384, 512), bias=pc(12))
         at(h, "test")
         group(s("P3", 384, 512), [(SEL, s("RB", 256, 384, rows=48)), (s("D16"), s("K16", 0, 128))])
         mm(s("P3", 0, 128), s("ZX"), Y, True, False)
-        for a, b in OPT["chf"]:
+        for a, b, q in chf:
             tt(s("PW", a * 128, b * 128), s(F, a * 128, b * 128), s("P1", 0, (b - a) * 128), mul)
             for k in range(a, b):
                 mm(s("P3", 0, 128), s("ZS", 15 - k, 143 - k), s("PW", k * 128, (k + 1) * 128), False, False)
@@ -691,15 +783,16 @@ def rank_program(g, core, T, topo):
         act(s("E1"), s("P3", 0, 128), AF.Relu, bias=-2048.0)
         tt(s("EV"), s("E1"), s("P3", 384, 512), mul)
         mm(s("P2", 0, 128), s("ZH", 0, 128), s("K16", 0, 128), True, False)
-        for a, b in OPT["chc"]:
+        for a, b, q in chc:
             tt(s("XW", a * 128, b * 128), s("CW", a * 128, b * 128), s("P0", 0, (b - a) * 128), add)
+        for a, b in chi:
             ts(s("IW", a * 128, b * 128), s("XW", a * 128, b * 128), 33024.0, ALU.is_equal)
             for k in range(a, b):
                 mm(s("P2", 0, 128), s("ZH", 15 - k, 143 - k), s("IW", k * 128, (k + 1) * 128), False, k == 14)
         at(h, "draw")
         mm(s("P0", 0, 128), s("IDB"), s("NZ"), True, False)
         tt(s("SW"), s("EV"), s("P2", 0, 128), mn)
-        mm(s("P0", 0, 128), s("BO32"), s("SW"), False, True)
+        ask = mm(s("P0", 0, 128), s("BO32"), s("SW"), False, True)
         ts(s("ASK", 0, 128), s("P0", 0, 128), 0.0, ALU.is_le)
         at(h, "hit")
         tt(s("SE"), s("E1"), s("P2", 0, 128), mn)
@@ -710,26 +803,19 @@ def rank_program(g, core, T, topo):
         at(h, "g")
         tt(s("SV"), s("SG"), s("P2", 0, 128), mn)
         act(s("ES"), s("P3", 0, 128))
-        group(s("P3", 256, 384), [(ID32, s("ES")), (s("IS1"), s("SG")), (s("IS2"), s("SG")), (s("IC1"), s("SV")), (s("IC2"), s("SV"))])
+        arg = group(s("P3", 256, 384), [(s("IDE"), s("ES")), (s("IS1"), s("SG")), (s("IC1"), s("SV"))])
         at(h, "hit")
         tt(s("XX"), s("HIT"), s("P2", 128, 256), mul)
         at(h, "g")
-        gb = math.log(0.5 ** (3 - w)) + 1419.5625 / 4096
+        gb = math.log(0.5 ** (2.5 - w))
         GH, GL = s("GH", 128 * par, 128 * par + 128), s("GL", 128 * par, 128 * par + 128)
-        if OPT["gl"] == "v":
-            act(s("P3", 128, 256), s("P3", 256, 384), AF.Exp, bias=gb, scale=1.0 / 4096)
-            act(GH, s("P3", 128, 256))
-            tt(GL, s("P3", 128, 256), GH, sub)
-        else:
-            act(s("GS"), s("P3", 256, 384), AF.Exp, bias=gb, scale=1.0 / 4096)
-            act(GH, s("GS"))
-            group(s("P3", 128, 256), [(ID32, s("GS")), (IDN, GH)])
-            act(GL, s("P3", 128, 256))
+        act(s("P3", 128, 256), s("P3", 256, 384), AF.Exp, bias=gb, scale=math.log(2.0) / 1143)
+        act(GH, s("P3", 128, 256))
+        tt(GL, s("P3", 128, 256), GH, sub)
         at(h, "draw")
-        l0 = 376 if par else 240
-        PL, PB, PX = s("P7", l0, l0 + 8), s("P7", 248, 376), s("P7", 384, 512)
+        PL, PB, PX = s("P7", 376, 384), s("P7", 248, 376), s("P7", 384, 512)
         last = h == NH - 1
-        mm(s("P7", 240, 512), ID, s("ZP"), True, False)
+        mm(s("P7", 248, 512), ID, s("ZP", 8, 272), True, False)
         mm(PL, ID, sl, False, False)
         for o in () if last else (PB, PX):
             mm(o, ID, sa, False, False)
@@ -737,83 +823,107 @@ def rank_program(g, core, T, topo):
             mm(PL, s("ZS", 15 - r, 143 - r), s("XX", r, 128, 16), False, False)
         for o in () if last else (PB, PX):
             mm(o, BO, s("XX"), False, False)
-        TZ = s("P0", 128, 256)
-        mm(TZ, st(h), s("KT"), True, False)
-        mm(TZ, st(15), s("KT"), False, False)
-        mm(TZ, IDN, sa, False, OPT["born"] == "v")
+        if par == 0:
+            at(h, "early")
+            ts(s("E0", 32, 33), s("P2", 256, 257), 1.0, add, s("ASK", 0, 1), mul)
+            group(s("P6", 256, 257), [(ID, s0), (st(0), s("E0", 32, 33)), (BO, s("XX", 0, 1))])
+            cp(s("E0", 4 * h, 4 * h + 1), s("P6", 256, 257))
+            sent[h] = send(prv, nxt, s("R0", 4 * h, 4 * h + 8), s("E0", 4 * h, 4 * h + 8), "re%d" % h)
+            at(h, "draw")
         scan(s("CUM", 1, 145), s("ASK"), s("K16"), add, mn)
         act(s("JK"), s("CUM", 1, 145), AF.Sign, bias=pc(10), scale=-1.0, acc=s("IAC", 0, 1))
-        group(s("P2", 384, 512), [(ID, s("CUM", 1, 129)), (IDN, s("CUM", 0, 128))])
-        if OPT["born"] == "v":
-            tt(s("ZZ"), s("CUM", 1, 129), TZ, add)
-            tt(s("YY"), s("ZZ"), s("P2", 384, 512), mul)
-        else:
-            mm(TZ, ID, s("CUM", 1, 129), False, True)
-            act(s("BN"), s("P2", 384, 512))
-            tt(s("YY"), s("BN"), TZ, mul)
-        for o in () if last else (PB, PX):
-            mm(o, st(0), s("YY"), False, False)
+        group(s("P0", 128, 256), [(ID, s("CUM", 1, 129)), (IDN, s("CUM", 0, 128))])
+        tt(s("ZZ"), s("CUM", 1, 129), TZ, add)
+        tt(s("YY"), s("ZZ"), s("P0", 128, 256), mul)
         for r in range(16):
-            mm(PL, s("Z1", 15 - r, 143 - r), s("YY", r, 128, 16), False, r == 15)
-        if par == 0 or last:
-            cp(s("PU", 8 * h, 8 * h + 8), PL)
-        if not last:
-            p0 = 248 if par else 240
-            ts(s("PK", k0 + 8, k0 + 144), s("P7", p0, p0 + 136), MG1, add, MG1, sub)
-            send(prv, nxt, s("RX", k0 + 8, k0 + 144), s("PK", k0 + 8, k0 + 144), "rx%d" % h)
+            mm(PL, s("Z1", 15 - r, 143 - r), s("YY", r, 128, 16), False, last and r == 15)
+        for o in () if last else (PB, PX):
+            i = mm(o, st(0), s("YY"), False, o is PX)
+        if last:
+            cp(s("SU", k0 + 128, k0 + 136), PL)
+        else:
+            cp(s("SU", k0, k0 + 136), s("P7", 248, 384))
+            if h != NH - 2:
+                at(h, "draw" if par else "kb")
+                sent[h] = send(prv, nxt, s("RU", k0, k0 + 136), s("SU", k0, k0 + 136), "rx%d" % h)
+            at(h, "repeats" if par else "draw")
+            cp(s("PK", k0, k0 + (1 if par else 128)), s("P7", 375 if par else 248, 376))
             at(h, "repeats" if par else "kb")
-            if par:
-                cp(s("LU", (h + 2) * 16 + 6, (h + 2) * 16 + 8), s("P7", 382, 384))
-                act(s("KB", 16 * h + 16, 16 * h + 25), s("P7", 375, 384), scale=512.0)
-            else:
-                act(s("KB", 16 * h + 17, 16 * h + 25), PL, scale=512.0)
+            act(s("KB", 16 * h + 16, 16 * h + 25), s("P7", 375, 384), scale=512.0)
         at(h, "draw")
         IDX = s("IDX", 0, 1)
         ts(IDX, s("IAC", 0, 1), 0.5, mul, 72.0, add)
-        tt(s("G1"), ind(s("AB", 176 * par + 32, 176 * par + 176), IDX), s("CV", 16 * h, 16 * h + 16), sub)
+        tt(s("G1", 0, 16), ind(s("AB", 176 * par + 32, 176 * par + 176), IDX), s("CV", 16 * h, 16 * h + 16), sub)
         act(s("EM", m0, m0 + 16), ind(s("YS", y0, y0 + 144), IDX))
-        tt(ind(s("NN"), IDX), s("G1"), s("BM"), mul)
+        tt(ind(s("NN"), IDX), s("G1", 0, 16), s("BM"), mul)
         tt(ind(s("TB"), s("OFU", 8 * par, 8 * par + 8)), A, s("NN", 0, 128), sub)
         act(s("IAC", 1, 2), s("IAC", 0, 1), AF.Sign, bias=-111.0)
         ts(s("IDX", 2, 3), s("IAC", 1, 2), 128.0, mul, pc(13), add)
-        mv(OPT["tbm"], s("G2"), ind(s("AQ"), IDX))
-        cp(ind(s("TB", m0, m0 + 272), s("IDX", 2, 3)), s("G2"))
+        mv(OPT["tbm"], s("G1", 16, 32), ind(s("AQ"), IDX))
+        cp(ind(s("TB", m0, m0 + 272), s("IDX", 2, 3)), s("G1", 16, 32))
         if par and not last:
             at(h, "repeats")
             repeats(16 * h + 17, True)
             act(s("CS", 128 * w, 128 * w + 128), CNT)
-            send(prv, nxt, s("CR", 144 * w + 152, 144 * w + 280), s("CS", 128 * w, 128 * w + 128), "cx%d" % w)
-        at(h, "g" if last else "sums")
-        for c, (a, b) in enumerate(OPT["chg"]):
+            sent[h] = send(prv, nxt, s("CR", 144 * w + 152, 144 * w + 280), s("CS", 128 * w, 128 * w + 128), "cx%d" % w)
+        at(h, "g" if last else ("sums", "sums1")[par])
+        for c, (a, b) in enumerate(OPT["chl"] if last else OPT["chg"][par]):
             bk = "P%d" % (4 + (c & 1))
             for k in range(a, b + (b == 15)):
                 group(s(bk, (k - a) * 128, (k - a) * 128 + 128), [(st(k), GH), (st(k), GL)])
             tt(s("PR%d" % par, a * 128, b * 128), s(F, a * 128, b * 128), s(bk, 0, (b - a) * 128), mul)
-        act(s("PR%d" % par, 1920, 2048), s(bk, (15 - a) * 128, (16 - a) * 128), scale=s("XB"))
-        fold(h)
+            if b == 15:
+                act(s("PR%d" % par, 1920, 2048), s(bk, (15 - a) * 128, (16 - a) * 128), scale=s("XB"))
+            if last and b == OPT["lf"]:
+                fold(h)
+            for k in range(a, b + (b == 15)) if last and a >= OPT["lf"] else ():
+                mm(s("P7", 0, 128), ID32, s("PR1", k * 128, (k + 1) * 128), k == OPT["lf"], False)
+        if last:
+            a = h if OPT["lf"] else h - 2
+            for x in range(0, FW, 128):
+                mm(s("P7", 0, 128), ID32, s("AC", a * FW + x, a * FW + x + 128), False, x == FW - 128)
+            act(s("YA", 1, 256, 2), s("P7", 0, 128))
+        else:
+            edges.append((sent[h], fold(h)))
     at(NH, "names")
     for par in range(2):
-        F = "FB" if par else "FA"
-        A = names(s("PU", 32 + 8 * par, 40 + 8 * par), 32, par, "a")
-        for a, b in CH:
-            gat(F, s("EM"), a, b, par)
+        F = "PW" if par else "FA"
+        A = names(s("SU", (4 + par) * SL + 128, (4 + par) * SL + 136), 32, par, "a")
+        for a, b, q in OPT["zq"][par]:
+            if q == "a":
+                gat(F, s("EM"), a, b, par, -8.0)
+            else:
+                ts(s(F, a * 128, b * 128), ind(s("EM"), s("NL", 128 * par + a * 8, 128 * par + b * 8)), -8.0, add)
         WB = s("WB", 128 * par, 128 * par + 128)
-        weights(s("WT"), A, s("P%d" % (2 + par), 128, 256))
-        ts(WB, s("WT"), -128.0, add)
-        for c in range(4):
-            bk = "P%d" % (6 * par + (c & 1))
-            for k in range(4 * c, 4 * c + 4):
-                mm(s(bk, (k & 3) * 128, (k & 3) * 128 + 128), st(k), WB, True, True)
-            tt(s("PZ", c * 512, (c + 1) * 512), s(F, c * 512, (c + 1) * 512), s(bk), mul)
-            for k in range(4 * c, 4 * c + 4):
-                mm(s("P%d" % (2 + par), 0, 128), s("ID128"), s(F, k * 128, (k + 1) * 128), k == 0, False)
-                mm(s("P%d" % (2 + par), 0, 128), ID, s("PZ", k * 128, (k + 1) * 128), False, k == 15)
-        gcopy(s("YA", par, 256, 2), s("AC", (4 + par) * 128, (5 + par) * 128))
+        weights(WB, A, s("P%d" % (2 + par), 128, 256))
+        mm(s("P%d" % (2 + par), 0, 128), s("BO8"), WB, True, False)
+        for c, (a, b) in enumerate(OPT["zp"][par]):
+            bk = ("P0", "P1", "P6")[(len(OPT["zp"][0]) * par + c) % 3]
+            for k in range(a, b):
+                mm(s(bk, (k - a) * 128, (k - a) * 128 + 128), st(k), WB, True, True)
+            z0 = 2048 * par
+            tt(s("PZ", z0 + a * 128, z0 + b * 128), s(F, a * 128, b * 128), s(bk, 0, (b - a) * 128), mul)
+            for k in range(a, b):
+                mm(s("P%d" % (2 + par), 0, 128), ID, s("PZ", z0 + k * 128, z0 + (k + 1) * 128), False,
+                   (a, b) == OPT["zp"][par][-1] and k == b - 1)
         act(s("YZ", par, 256, 2), s("P%d" % (2 + par), 0, 128))
+    tt(s("YA", 0, 256, 2), s("AC", 4 * FW, 4 * FW + 128), s("AC", 4 * FW + 128, 4 * FW + 256), add)
     dma("s", dr(T.ya[:]), s("YA"), "dya", 2000.0)
     dma("s", dr(T.yz[:]), s("YZ"), "dyz", 2000.0)
 
-    ops = schedule(ops, turn)
+    for q in "sa":
+        loads = [i for i in range(k16 + 1) if ops[i][0] == q]
+        edges.extend(zip(loads, loads[1:]))
+    edges.extend((k16, i) for i in range(k16 + 1, len(ops)) if ops[i][0] == "a" and turn[i] < 100)
+    for q in "va":
+        seq = []
+        for h in [-9] + list(range(NH + 1)):
+            for x in LINE[q][KIND[h]].split():
+                k = (h - 1, q, x[1:]) if x[0] == "-" else (h, q, {"F": "FB" if h & 1 else "FA"}.get(x, x))
+                if named.get(k):
+                    seq.append(named[k].pop(0))
+        edges.extend(zip(seq, seq[1:]))
+    ops = schedule(ops, turn, edges)
     deps = depends(ops, True)
     clock = {q: {} for q in "vapgsx"}
     at, waits, need = [], [], set()
@@ -822,7 +932,7 @@ def rank_program(g, core, T, topo):
         ws = []
         for j in sorted(deps[i], reverse=True):
             key = ops[j][0] if ops[j][4] is None else ops[j][4][0]
-            if ck.get(key, -1) >= j:
+            if ck.get(key, -1) >= j or soft(ops[j], o):
                 continue
             ws.append(j)
             need.add(j)

@@ -1,49 +1,47 @@
 import math
-from concourse.bass import DstId, RemoteDMATransfer
 from concourse.mybir import AluOpType as ALU, ActivationFunctionType as AF
 
 F32, BF, F16, I32, U16 = "float32", "bfloat16", "float16", "int32", "uint16"
 H, S0, NH = 2048, 1952, 6
-FW = 256
 SL = 144
 SB = {
-    "LK": (2048, I32), "TB": (2320, F32), "EM": (2048, BF), "OB": (768, BF), "XB": (1, F32),
+    "LK": (2048, I32), "TB": (2320, F32), "EM": (2064, BF), "OB": (768, BF), "XB": (1, F32), "XS": (256, F16), "YB": (2048, BF),
     "PEPO": (16, I32), "RN": (384, I32), "RB": (384, BF), "L16": (20, F16), "INI": (256, F16),
     "RX": (5 * SL, F16), "PK": (6 * SL, F16), "LU": (32, U16), "SU": (6 * SL, U16), "RU": (5 * SL, U16), "CR": (432, BF), "CS": (256, BF),
-    "EQ0": (128, BF), "KB": (7 * 16, F32), "AB": (352, F32), "DG": (128, F32), "TT": (576, F32), "NL": (256, U16), "PERM": (8, U16),
-    "FA": (2048, BF), "FB": (2048, BF), "CW": (2048, F32), "XW": (2048, BF), "IW": (2048, BF), "PW": (2048, BF),
-    "PR0": (2048, F32), "PR1": (2048, F32), "PZ": (4096, F16), "HB": (NH * FW, F32), "AC": (NH * FW, F32),
-    "CL": (256, BF), "GT": (256, BF), "CB": (256, F32), "U2": (128, F16),
+    "EQ0": (128, BF), "KB": (7 * 16, F32), "AB": (352, F32), "DG": (128, F32), "TT": (288, F32), "NL": (128, U16), "PERM": (8, U16),
+    "NS": (352, U16), "NF": (256, F16),
+    "FA": (2048, BF), "FB": (2048, BF), "CW": (2048, F32), "CX": (48, F32), "QS": (256, F32), "XW": (2048, BF), "IW": (2064, BF), "PW": (2048, BF),
+    "SC": (2048, F32), "PR": (7 * 256, F32), "PZ": (4096, F16), "J8": (96, F32), "DR": (384, BF),
+    "CL": (264, BF), "GT": (264, BF), "CB": (264, F32), "U2": (144, F16),
     "WT": (128, BF), "WB": (256, BF), "SG": (128, BF), "ND": (128, BF), "AQ": (144, F32), "YS": (6 * 144, BF),
-    "EA": (704, BF), "EQ": (704, BF), "OF": (128, F16), "OFU": (16, U16), "SV": (128, BF), "SE": (128, F32), "SW": (128, F32),
-    "ES": (128, F32), "GH": (256, BF), "GL": (256, BF), "HIT": (128, BF), "ASK": (144, BF), "CUM": (145, BF), "E0": (40, F16), "R0": (24, F16),
-    "ZZ": (128, F32), "XR": (128, BF), "XX": (128, F16), "YY": (128, F16), "NN": (144, F32), "JK": (144, BF), "IAC": (2, F32),
+    "EA": (128, BF), "OF": (128, F16), "OFU": (16, U16), "SV": (128, BF), "SE": (128, F32), "SW": (128, F32),
+    "ES": (128, F32), "GH": (256, BF), "GL": (512, BF), "HIT": (128, BF), "ASK": (144, BF), "CUM": (145, BF), "E0": (48, F16), "R0": (48, F16),
+    "XR": (128, BF), "XX": (128, F16), "NN": (128, F32), "JK": (144, BF), "JC": (144, BF), "IAC": (2, F32),
     "IDX": (4, U16), "G1": (40, F32), "YA": (256, F32), "YZ": (256, F32),
-    "PI": (8, I32), "PC": (24, F32), "RM": (16, F32), "BM": (16, F32), "COLG": (128, F32), "COLK": (16, F32),
-    "DUM": (128, F32), "CV": (96, F32), "C2": (8, F32), "BO": (128, BF), "BO32": (128, F32), "BO4": (128, BF),
-    "ZS": (143, BF), "Z1": (143, BF), "ZX": (128, BF), "TRI": (128, F32), "DIF": (128, BF), "DT": (128, BF), "DT32": (128, F32),
-    "DTN": (128, BF), "L14": (128, BF), "S2K": (128, BF), "XBN": (128, BF), "ZH": (143, BF), "D16": (128, BF),
-    "IS1": (128, F16), "ID2K": (128, BF), "IDB": (128, BF), "NZ": (128, BF), "E1": (128, F32), "EV": (128, F32),
-    "ID": (128, BF), "IDN": (128, BF), "IDM": (128, BF), "ID32": (128, F32),
-    "BO8": (128, BF), "IC1": (128, F16), "IDE": (128, F32), "DN": (128, F32), "D0": (128, BF), "ST": (2048, BF), "SEL": (768, BF),
-    "ZB": (512, BF), "Z32": (128, F32), "ZP": (272, BF), "POSB": (128, BF), "K16": (144, BF), "KT": (128, F16),
+    "PI": (10, I32), "PC": (40, F32), "RM": (24, F32), "BM": (112, F32), "COLG": (128, F32), "COLK": (16, F32),
+    "DUM": (128, F32), "CV": (96, F32), "C2": (8, F32), "BO": (128, BF), "BO32": (128, F32), "BO4": (384, BF),
+    "ZS": (143, BF), "Z1": (143, BF), "TRI": (128, F32), "DIF": (128, BF), "DT": (128, BF),
+    "L14": (128, BF), "S2K": (128, BF), "XBN": (128, BF), "ZH": (143, BF), "D16": (128, BF), "BB": (384, BF),
+    "ID2K": (128, BF), "IDB": (128, BF), "NZ": (128, BF), "E1": (128, F32), "EV": (128, F32),
+    "ID": (160, BF), "IDN": (128, BF), "IDM": (128, BF), "ID32": (128, F32),
+    "BO8": (128, BF), "IC": (512, F16), "IDE": (256, F32), "DN": (1408, BF), "D0": (128, BF), "ST": (2048, BF), "SEL": (768, BF),
+    "ZB": (160, BF), "POSB": (128, BF), "K16": (144, BF), "KH": (768, BF),
 }
 SCRATCH = {n: ("sbuf", [128, w], d) for n, (w, d) in SB.items()}
+SCRATCH["EQ"] = ("sbuf", [128, 8, 128], BF)
 for _b in range(8):
     SCRATCH["P%d" % _b] = ("psum", [128, 512], F32)
 DMAS = ["dpo", "dpe", "dl0", "dl1", "dl2", "dem", "dob", "dn0", "dn1", "dn2", "dxb", "dya", "dyz"]
-SEMAPHORES = (["qv", "qa", "qp", "qg", "loc", "pox", "ob1", "ob2", "fl0", "fl1", "cx0", "cx1"] + DMAS + ["rx%d" % h for h in range(5)] + ["re%d" % h for h in range(5)]
-              + ["fa%d" % h for h in range(NH)] + ["fb%d" % h for h in range(NH)])
-CYC, PEC, FIXV, FIXA, FIXG, GAT, SCA, HOP, REM, PLAT = 0.85, 0.43, 15.0, 15.0, 60.0, 1.56, 3.8, 220.0, 1800.0, 0.0
-KINDS = ("first", "odd", "even", "last")
-OPT = {"late": 99, "pe1": 0, "pe2": 0, "nd": "a", "dg": "a", "nm": "a", "ag": "a", "tbm": "a", "stv": 12, "cl": "v",
-       "chf": {k: [(0, 4, "a"), (4, 8, "a" if k == "last" else "v"), (8, 12, "a"), (12, 15, "a")] for k in KINDS},
-       "chc": {k: [(0, 4, "a"), (4, 8, "a"), (8, 12, "a"), (12, 14, "a"), (14, 15, "a")] for k in KINDS},
+SEMAPHORES = (["qv", "qa", "qp", "qg", "loc", "pox", "ob1", "ob2", "cx0", "cx1"] + DMAS + ["rx%d" % h for h in (0, 1, 2, 3)]
+              + ["re%d" % h for h in (0, 2, 4)])
+CYC, PEC, FIXV, FIXA, FIXG, FIXP, GAT, SCA, REM = 0.85, 0.43, 15.0, 15.0, 60.0, 2.0, 1.56, 3.8, 1800.0
+KINDS = ("first", "odd", "even", "odd", "even", "last")
+OPT = {"stv": 12, "prv": 0, "sc": [(0, 256), (256, 512)], "late": 12, "yb": ["vvvvaaaa", "aaaaaaaa", "aaaaaaaa"],
+       "chf": {k: [(32, 64, "a"), (64, 96, "a"), (96, 128, "a"), (0, 32, "a")] for k in KINDS},
+       "chc": {k: [(8, 10, "a") if k in ("odd", "last") else (0, 4, "v"), (10, 12, "a"), (12, 14, "a"), (14, 15, "a")] for k in KINDS},
        "chi": {k: [(0, 4), (4, 8), (8, 12), (12, 14), (14, 15)] for k in KINDS},
-       "chg": [[(0, 4), (4, 8), (8, 12), (12, 15)], [(0, 2), (2, 4), (4, 6), (6, 8), (8, 10), (10, 12), (12, 14), (14, 15)]],
-       "chl": [(0, 4), (4, 8), (8, 12), (12, 15)], "lf": 8,
-       "zq": [[(0, 4, "a"), (4, 8, "a"), (8, 12, "a"), (12, 15, "a")], [(12, 15, "a"), (0, 4, "a"), (4, 8, "a"), (8, 11, "a"), (11, 12, "a")]],
-       "zp": [[(0, 4), (4, 8), (8, 12), (12, 16)], [(12, 16), (0, 4), (4, 8), (8, 11), (11, 12)]]}
+       "zq": [[(0, 32, "a"), (32, 64, "a"), (64, 128, "a")], [(0, 32, "a"), (32, 64, "a"), (64, 96, "a"), (96, 128, "a")]],
+       "zp": [[(0, 0, 2), (0, 1, 2), (64, 0, 2), (64, 1, 2)], [(0, 0, 2), (0, 1, 2), (64, 0, 1), (96, 0, 1)]]}
 
 
 def bits(engines):
@@ -51,21 +49,6 @@ def bits(engines):
     for e in engines:
         m |= 1 << e
     return m
-
-
-def helper_of(c, T, topo):
-    return [x for x in topo.cores_of(c) if x not in T.cores and topo.die(x) == topo.die(c)][0]
-
-
-def helper_program(g, core, owner, T, topo):
-    rid, pid = topo.addr(owner, core)
-    eng = topo.engines(core, owner)
-    nf = NH if OPT["lf"] else NH - 1
-    for h in range(nf):
-        g.wait_ge(T.sem["fa%d" % h], len(eng) if h >= NH - 2 else len(eng) // 2)
-        g.remote_dma(T.AC[:, h * FW:(h + 1) * FW], T.HB[:, h * FW:(h + 1) * FW], T.sem["fb%d" % h], T.sem.loc,
-                     pid, rid, bits(eng[len(eng) // 2:]))
-    g.wait_ge(T.sem.loc, nf * (len(eng) // 2))
 
 
 def hit(x, y):
@@ -79,7 +62,7 @@ def soft(a, b):
 
 def depends(ops, banks):
     deps, last, lastmm, others = [], {}, {}, {}
-    for i, (q, fn, rd, wr, tok, c, lat, aft) in enumerate(ops):
+    for i, (q, fn, rd, wr, tok, c, lat) in enumerate(ops):
         d = set()
         for lst, isw in ((rd, False), (wr, True)):
             for r in lst:
@@ -114,245 +97,263 @@ def depends(ops, banks):
     return deps
 
 
-def schedule(ops):
+MACHINES = [(1.0, 1.0, 1.0, 205.0, -100.0, 0.0), (1.3, 1.3, 1.1, 160.0, 500.0, 200.0)]
+MOVES = 100000
+TEMP = 0.002
+ANY = 4
+EVERY = 4
+ORDER = []
+
+
+REST = "SW SE ASK CUM SV OFU HIT IDX XX G1 NN AB %s IDX TB"
+LINE = {
+    "v": {"first": "-ZB -PI -PI -PI -PI -PI -PI -PI -PC -PC -BO -RM -ST -ST -ST -ST -ST -ST -ST -ST -ST -ST -ST -ST -LU -LU -L16 "
+                   "-CW -CW -INI -TB -CW NS -TB -CW -TB -TB NS NF TT TT CL NL CB WT CW U2 CW CL CB XW XW XW XW IW XW IW OF XW XW IW XW EV IW IW "
+                   + REST % "TB SU",
+          "even": "NS RX NS TT TT NF CL NL CB WT CW U2 CW CL CB XW XW XW XW IW XW IW OF XW XW IW XW EV IW IW " + REST % "TB SU",
+          "odd": "NS TT TT NF EQ EQ EQ EQ CL NL CB WT EQ EQ EQ EQ CW U2 CW CL CB CL CB XW XW U2 XW XW JK XW IW IW IW OF XW XW IW XW EV IW IW " + REST % "SU TB",
+          "end": "NS NS NF NF WB WB PW PZ PZ PZ PZ PZ PZ PZ PZ"},
+    "a": {"first": "-P4 -P5 -P0 FA -P1 FA DG AB AB GT FA FA GT QS XS SG CW CW CW NZ E1 JK ND AQ ES IAC IAC G1 EM "
+                   "P3 GH KB",
+          "even": "AB DG AB GT FA FA GT FA QS FA CW XS SG CW CW NZ E1 JK ND AQ ES IAC IAC G1 EM P3 GH KB",
+          "odd": "DG AB GT FB FB GT GT FB QS FB CX EA XS SG CW CW CW CW NZ E1 JK ND AQ ES IAC IAC G1 EM P3 GH KB",
+          "end": "AB AB FA FA FA PW PW PW PW YZ YZ"}}
+for _q in "va":
+    LINE[_q]["last"] = LINE[_q]["odd"]
+
+
+def schedule(ops, edges, line):
+    if ORDER:
+        return [ops[i] for i in ORDER[0]]
     n = len(ops)
     deps = depends(ops, False)
-    for i in range(n):
-        if ops[i][7] is not None:
-            deps[i].add(ops[i][7])
+    data = [set(d) for d in deps]
+    for j, i in edges:
+        deps[i].add(j)
     suc = [[] for _ in range(n)]
     for i in range(n):
         for j in deps[i]:
             suc[j].append(i)
-    pb = [set(r[0] for r in o[2] + o[3] if SCRATCH[r[0]][0] == "psum") for o in ops]
-
-    def gap(i, k):
-        return -ops[i][6] if ops[k][0] == "p" == ops[i][0] else HOP
-
-    def chains(order, mix):
-        pri, nxt = [0.0] * n, {}
-        for i in reversed(order):
-            q = ops[i][0]
-            p = ops[i][6] + max([pri[k] + gap(i, k) for k in suc[i]] + [0.0])
-            if q in nxt and q != "x":
-                p = max(p, (1 - mix) * p + mix * pri[nxt[q]])
-            pri[i] = ops[i][5] + p
-            nxt[q] = i
-        return pri
-
-    def run(pri, slack):
-        left = [len(d) for d in deps]
-        ready = {}
-        for i in range(n):
-            if not left[i]:
-                ready.setdefault(ops[i][0], []).append(i)
-        fin, free, bank, order, base = [0.0] * n, {}, {}, [], [0.0] * n
-        while len(order) < n:
-            est = {}
-            for q in ready:
-                for i in ready[q]:
-                    t = max(base[i], free.get(q, 0.0) if q != "x" else 0.0)
-                    for b in pb[i]:
-                        for q2, f in bank.get(b, {}).items():
-                            if q2 != q:
-                                t = max(t, f + HOP)
-                    est[i] = t
-            i0 = min(est, key=lambda i: (est[i], -pri[i], i))
-            q = ops[i0][0]
-            i = max([k for k in ready[q] if est[k] <= est[i0] + min(slack, ops[i0][5])], key=lambda k: (pri[k], -k))
-            ready[q].remove(i)
-            order.append(i)
-            free[q] = est[i] + ops[i][5]
-            fin[i] = free[q] + ops[i][6]
-            for b in pb[i]:
-                bank.setdefault(b, {})[q] = fin[i]
-            for k in suc[i]:
-                base[k] = max(base[k], fin[i] + gap(i, k))
-                left[k] -= 1
-                if not left[k]:
-                    ready.setdefault(ops[k][0], []).append(k)
-        return max(fin), order
-
-    if not ORDER:
-        best = None
-        for slack, mix in TRY:
-            pri = chains(list(range(n)), 0.0)
-            for it in range(ROUNDS):
-                t, order = run(pri, slack)
-                if best is None or t < best[0]:
-                    best = (t, order, slack, mix, it)
-                new = chains(order, mix)
-                pri = [0.5 * (x + y) for x, y in zip(pri, new)]
-        ORDER.append(best)
-    return [ops[i] for i in ORDER[0][1]]
-
-
-def schedule(ops, turn, edges):
-    if ORDER:
-        return [ops[i] for i in ORDER[0][1]]
-    n = len(ops)
-    deps = depends(ops, False)
-    for i in range(n):
-        if ops[i][7] is not None:
-            deps[i].add(ops[i][7])
-    for j, i in edges:
-        deps[i].add(j)
-    suc, margin = [[] for _ in range(n)], [0.0]
-    for i in range(n):
-        for j in deps[i]:
-            suc[j].append(i)
-    use = []
-    for o in ops:
-        u = [] if o[0] == "x" else [(o[0], o[5])]
-        if o[0] in "va":
-            u += [(b, o[5] + HOP) for b in set(r[0] for r in o[2] + o[3] if SCRATCH[r[0]][0] == "psum")]
-        use.append(u)
-
-    def lag(i, k):
-        return ops[i][5] + (0.0 if near[k][i] else ops[i][6] + HOP)
-
-    def place(key, back):
-        before, after = (suc, deps) if back else (deps, suc)
-        left = [len(b) for b in before]
-        ready = sorted((key[i], i) for i in range(n) if not left[i])
-        t, held = [0.0] * n, {}
-        while ready:
-            i = ready.pop(0)[1]
-            if back:
-                x = max([t[k] + lag(i, k) for k in before[i]] + [ops[i][5] + ops[i][6]]) - ops[i][5]
-            else:
-                x = max([t[j] + lag(j, i) for j in before[i]] + [0.0])
-            moved = True
-            while moved:
-                moved = False
-                for r, d in use[i]:
-                    a0 = x - (d - ops[i][5]) if back else x
-                    lst = held.setdefault(r, [])
-                    lo, hi = 0, len(lst)
-                    while lo < hi:
-                        m = (lo + hi) // 2
-                        if lst[m][1] <= a0 + 1e-6:
-                            lo = m + 1
-                        else:
-                            hi = m
-                    a = a0
-                    while lo < len(lst) and lst[lo][0] < a + d + margin[0] - 1e-6:
-                        if lst[lo][2] != ops[i][0] or r == ops[i][0]:
-                            a = max(a, lst[lo][1])
-                        lo += 1
-                    if a > a0:
-                        x += a - a0
-                        moved = True
-            for r, d in use[i]:
-                a = x - (d - ops[i][5]) if back else x
-                lst = held[r]
-                m = len(lst)
-                while m and lst[m - 1][:2] > (a, a + d):
-                    m -= 1
-                lst.insert(m, (a, a + d, ops[i][0]))
-            t[i] = x + ops[i][5] if back else x
-            for k in after[i]:
-                left[k] -= 1
-                if not left[k]:
-                    e, lo, hi = (key[k], k), 0, len(ready)
-                    while lo < hi:
-                        m = (lo + hi) // 2
-                        if ready[m] < e:
-                            lo = m + 1
-                        else:
-                            hi = m
-                    ready.insert(lo, e)
-        return t
-
-    def replay(order, f, hop, rem, call, gf):
-        end, free, bank = [0.0] * n, {}, {}
-        for i in order:
-            q = ops[i][0]
-            x = max([end[j] + (-ops[j][6] if near[i][j] else hop) for j in deps[i]] + [free.get(q, 0.0) if q != "x" else 0.0])
-            for r, d in use[i][1:]:
-                x = max([x] + [e + hop for q2, e in bank.get(r, {}).items() if q2 != q])
-            free[q] = x + ops[i][5] * f * (gf if byidx[i] else 1.0) + (call if q == "g" and ops[i][4] else 0.0)
-            end[i] = free[q] + ops[i][6] + (rem if q == "x" else 0.0)
-            for r, d in use[i][1:]:
-                bank.setdefault(r, {})[q] = end[i]
-        return max(end)
-
+    Q = {"v": 0, "a": 1, "p": 2, "g": 3, "s": 4, "x": 5}
+    qn = [Q[o[0]] for o in ops]
+    bank = [sorted(set(int(r[0][1]) for r in o[2] + o[3] if SCRATCH[r[0]][0] == "psum")) if o[0] in "va" else [] for o in ops]
     byidx = [o[0] in "va" and any(SCRATCH[r[0]][2] == U16 for r in o[2]) and not any(SCRATCH[r[0]][2] == F16 for r in o[3]) for o in ops]
-    near = [{j: ops[j][0] == ops[i][0] and (ops[i][0] in "ps" or ops[j][0] == "a" and not ops[j][2]) or soft(ops[j], ops[i])
-             for j in deps[i]} for i in range(n)]
-    left, topo_order = [len(d) for d in deps], [i for i in range(n) if not deps[i]]
+    near = [{j: ops[j][0] == ops[i][0] and (ops[i][0] == "p" or j not in data[i]) or soft(ops[j], ops[i]) for j in deps[i]} for i in range(n)]
+    mach = []
+    for f, pf, gf, hop, rem, call in MACHINES:
+        dur = [o[5] * (pf if o[0] == "p" else 1.0 if o[4] else f * (gf if byidx[i] else 1.0)) + (call if o[0] == "g" and o[4] else 0.0)
+               for i, o in enumerate(ops)]
+        lat = [o[6] + (rem if o[0] == "x" else 0.0) for o in ops]
+        mach.append((dur, lat, [[(j, 0.0 if near[i][j] else lat[j] + hop) for j in deps[i]] for i in range(n)], hop))
+
+    def replay(order, a, m, fin, why, z=None):
+        dur, lat, need, hop = m
+        lastq, lastb = [-1] * 6, [-1] * 16
+        for i in order[max(0, a - 100):a]:
+            lastq[qn[i]] = i
+            for b in bank[i]:
+                lastb[2 * b + qn[i]] = i
+        for i in order[a:z]:
+            q = qn[i]
+            x, w = 0.0, -1
+            for j, e in need[i]:
+                if fin[j] + e > x:
+                    x, w = fin[j] + e, j
+            j = lastq[q]
+            if j >= 0 and q != 5 and fin[j] > x:
+                x, w = fin[j], j
+            for b in bank[i]:
+                j = lastb[2 * b + 1 - q]
+                if j >= 0 and fin[j] + hop > x:
+                    x, w = fin[j] + hop, j
+                lastb[2 * b + q] = i
+            lastq[q] = i
+            fin[i] = x + dur[i]
+            why[i] = w
+        return z or max(fin[i] + lat[i] for i in ends) + 0.02 * sum(fin) / n
+
+    ends = [i for i in range(n) if not suc[i]]
+    dur, lat, need, hop = mach[0]
+    need = [list(x) for x in need]
+    for j, i in line:
+        need[i].append((j, 0.0))
+    after = [[] for _ in range(n)]
+    for i in range(n):
+        for j, e in need[i]:
+            after[j].append(i)
+    left, topo_order = [len(d) for d in need], [i for i in range(n) if not need[i]]
     for i in topo_order:
-        for k in suc[i]:
+        for k in after[i]:
             left[k] -= 1
             if not left[k]:
                 topo_order.append(k)
     assert len(topo_order) == n, "the named order contradicts the calls' needs"
-    chain, step = [0.0] * n, list(turn)
+    chain = [0.0] * n
     for i in reversed(topo_order):
-        chain[i] = max([chain[k] + lag(i, k) for k in suc[i]] + [ops[i][5] + ops[i][6]])
-        step[i] = min([step[i]] + [step[k] for k in suc[i]])
-    best = None
-    for kind, room in TRY:
-        margin[0] = room
-        key = [(step[i] if kind else 0, -chain[i]) for i in range(n)]
-        for it in range(ROUNDS):
-            t = place(key, False)
-            order = sorted(range(n), key=lambda i: (t[i], i))
-            end = sum(replay(order, *m) for m in MACHINES) / len(MACHINES)
-            if best is None or end < best[0]:
-                best = (end, order, kind, room, it)
-            if it < ROUNDS - 1:
-                key = [-x for x in place([-(t[i] + ops[i][5]) for i in range(n)], True)]
-    ORDER.append(best)
-    return [ops[i] for i in best[1]]
+        chain[i] += dur[i] + (lat[i] if not suc[i] else 0.0)
+        for j, e in need[i]:
+            chain[j] = max(chain[j], chain[i] + e)
+    left, t, held = [len(d) for d in need], [0.0] * n, [[] for _ in range(6)]
+    ready = [i for i in range(n) if not left[i]]
+    while ready:
+        i = max(ready, key=lambda k: (chain[k], -k))
+        ready.remove(i)
+        x = max([t[j] + dur[j] + e for j, e in need[i]] + [0.0])
+        if qn[i] != 5:
+            for a, b in held[qn[i]]:
+                if a < x + dur[i] and x < b:
+                    x = b
+            held[qn[i]].append((x, x + dur[i]))
+            held[qn[i]].sort()
+        t[i] = x
+        for k in after[i]:
+            left[k] -= 1
+            if not left[k]:
+                ready.append(k)
+    rank_in = {i: k for k, i in enumerate(topo_order)}
+    order = sorted(range(n), key=lambda i: (t[i], rank_in[i]))
+    need = mach[0][2]
+    outs = [[] for _ in range(n)]
+    for i in range(n):
+        for j, e in need[i]:
+            outs[j].append((i, e))
 
+    def anew(order, a, b, fin, seed):
+        tail, nxt = [0.0] * n, [0.0] * 6
+        for k in range(min(n, b + 150) - 1, a - 1, -1):
+            i = order[k]
+            tail[i] = dur[i] + max([lat[i] if not outs[i] else 0.0, nxt[qn[i]]] + [e + tail[x] for x, e in outs[i]])
+            if k >= b and qn[i] != 5:
+                nxt[qn[i]] = tail[i]
+        seg, f, free, used = order[a:b], list(fin), [0.0] * 6, [0.0] * 16
+        for i in order[max(0, a - 100):a]:
+            free[qn[i]] = f[i]
+            for x in bank[i]:
+                used[2 * x + qn[i]] = f[i] + hop
+        wait, noise, reach = {i: 0 for i in seg}, 100.0 * (seed >> 50 & 7), 0.25 * (seed >> 54 & 3) + 0.25
+        for i in seg:
+            seed = (seed * 6364136223846793005 + 1442695040888963407) % 2 ** 64
+            tail[i] += noise * (seed >> 40 & 1023) / 1024.0
+            for x in suc[i]:
+                if x in wait:
+                    wait[x] += 1
+        data = {i: max([f[j] + e for j, e in need[i]] + [0.0]) for i in seg if not wait[i]}
+        new = []
+        while data:
+            est = {i: max([x, free[qn[i]] if qn[i] != 5 else 0.0] + [used[2 * y + 1 - qn[i]] for y in bank[i]]) for i, x in data.items()}
+            i = min(est, key=lambda x: (est[x], x))
+            i = max((x for x in est if qn[x] == qn[i] and est[x] <= est[i] + reach * (dur[i] + hop)), key=lambda x: (tail[x], -x))
+            new.append(i)
+            del data[i]
+            f[i] = free[qn[i]] = est[i] + dur[i]
+            for x in bank[i]:
+                used[2 * x + qn[i]] = f[i] + hop
+            for x in suc[i]:
+                if x in wait:
+                    wait[x] -= 1
+                    if not wait[x]:
+                        data[x] = max([f[j] + e for j, e in need[x]])
+        return new
 
-TRY = [(0, 0.0), (1, 0.0)]
-MACHINES = [(1.0, 220.0, 0.0, 0.0, 1.0), (1.3, 30.0, 0.0, 0.0, 0.75), (1.2, 40.0, 0.0, 0.0, 1.1), (1.3, 220.0, 800.0, 300.0, 1.2)]
-
-
-ORDER = []
-ROUNDS = 3
-LINE = {
-    "v": {"start": "ZB PI PI AB PC BO RM ST ST ST ST ST ST ST ST ST ST ST ST LU L16 CW CW INI CW TB CW TB TB TB",
-          "even": "RX TT TT NL WT F CL CB PW U2 PW XW PW IW XW PW IW XW XW IW XW IW IW OF EV "
-                  "SW SE SV ASK CUM E OFU HIT ZZ XX IDX NN YY G E IDX NN GL TB SU TB PK",
-          "odd": "TT TT NL WT F CL PW CB RX U2 PW PW XW XW IW PW IW XW XW IW XW IW IW EV OF "
-                 "SW SE SV ASK OFU CUM HIT ZZ XX YY IDX G NN IDX GL NN SU TB TB",
-          "last": "TT TT NL WT -PR CL CB PW -PR U2 -PR PW PW XW IW XW PW IW -PR XW XW IW XW IW IW EV "
-                  "SW SE SV ASK CUM HIT ZZ XX IDX YY NN G GL NN TB SU TB",
-          "end": "-PR -PR TT TT NL WB TT TT -PR NL PZ WB -PR PZ PZ PZ PZ PZ PZ PZ PZ YA"},
-    "a": {"start": "PC ST ST ST ST",
-          "even": "AB DG AB ZZ P0 GT F CW F SG CW F CW CW CW E NZ ES JK ND AQ JK IAC P3 GH",
-          "first": "EA EA EA EA EA EA EA EA EQ EQ AB AB ZZ DG P0 GT F F CW SG CW F NZ CW CW CW E ES JK ND AQ JK P3 IAC GH",
-          "odd": "-KB AB DG ZZ EA P0 EA EA EA EA F GT CW EA EA EA EQ F EQ CW SG F CW CW CW E NZ ES JK ND AQ JK P3 IAC GH",
-          "last": "AB DG ZZ -KB P0 EA EA EA EA EA F GT F EA EA EA EQ F SG EQ CW CW F NZ CW CW CW E ES JK ND AQ JK P3 IAC GH",
-          "end": "AB AB ZZ P2 ZZ P3 FA FA -PR FA FA PW PW PW PW PW -YA YZ YZ"}}
-LINE["v"]["first"] = LINE["v"]["even"]
-KIND = {-9: "start", 0: "first", 1: "odd", 2: "even", 3: "odd", 4: "even", 5: "last", 6: "end"}
-STEP = {"names": 0, "d": 1, "f0": 2, "fit": 3, "f1": 4, "slice": 5, "gather": 6, "test": 7, "side": 8, "first": 8.5, "draw": 9,
-        "g": 9.5, "repeats": 100.5, "sums": 109.8, "sums1": 109.8, "hit": 9.1, "early": 9.2, "kb": 101.5, "list": 8.5, "const": 50, "late": 90}
+    fins, whys = [[0.0] * n for m in mach], [[-1] * n for m in mach]
+    base = [replay(order, 0, m, fins[k], whys[k]) for k, m in enumerate(mach)]
+    parts, best = [1.0] * len(mach), float(len(mach))
+    keep, seed = list(order), 12345
+    place = [0] * n
+    for it in range(MOVES):
+        if it == 0 or moved:
+            for k, i in enumerate(order):
+                place[i] = k
+            late, chains = [], [[] for m in mach]
+            for k, m in enumerate(mach):
+                i = max(ends, key=lambda e: fins[k][e] + m[1][e])
+                while whys[k][i] >= 0:
+                    chains[k].append(place[i])
+                    if whys[k][i] not in deps[i]:
+                        late.append((whys[k][i], i))
+                    i = whys[k][i]
+        moved = False
+        seed = (seed * 6364136223846793005 + 1442695040888963407) % 2 ** 64
+        p, i = late[(seed >> 44) % len(late)]
+        if (seed >> 30) % 16 < ANY:
+            i = (seed >> 44) % n
+            p = whys[0][i]
+            if p < 0 or p in deps[i]:
+                continue
+        a, b, ahead = place[p], place[i], seed >> 43 & 1
+        for _ in range(max(0, (seed >> 36) % 16 - 6)):
+            x, step = (a - 1, -1) if ahead else (b + 1, 1)
+            while 0 <= x < n and qn[order[x]] != qn[i]:
+                x += step
+            if 0 <= x < n:
+                a, b = (x, b) if ahead else (a, x)
+        p, i = order[a], order[b]
+        b += 1
+        seg = order[a:b]
+        if it % EVERY == 0:
+            a = max(0, a - (seed >> 12) % 40)
+            b = min(n, a + 20 + (seed >> 20) % 70)
+            seg = anew(order, a, b, fins[0], seed)
+        elif ahead:
+            take = {i}
+            for x in reversed(seg):
+                if x in take:
+                    take |= deps[x]
+            if p in take:
+                continue
+            seg = [x for x in seg if x in take] + [x for x in seg if x not in take]
+        else:
+            take = {p}
+            for x in seg:
+                if x in take:
+                    take.update(suc[x])
+            if i in take:
+                continue
+            seg = [x for x in seg if x not in take] + [x for x in seg if x in take]
+        new = order[:a] + seg + order[b:]
+        room, loss, idle = TEMP * (1.0 - it / MOVES) * ((seed >> 24) % 1024) / 1024.0, 0.0, [0] * n
+        for k, m in enumerate(mach):
+            c = min([x for x in chains[k] if x >= b] + [n - 1])
+            f = list(fins[k])
+            replay(new, a, m, f, idle, c + 1)
+            loss += (f[new[c]] - fins[k][new[c]]) / base[k]
+            if loss > room + 0.004:
+                break
+        if loss > room:
+            continue
+        f2, w2 = [list(f) for f in fins], [list(w) for w in whys]
+        part = [replay(new, a, m, f2[k], w2[k]) / base[k] for k, m in enumerate(mach)]
+        if sum(part) <= sum(parts) + room:
+            for k, i in enumerate(new):
+                place[i] = k
+            order = sorted(new, key=lambda i: (f2[0][i] - dur[i], place[i]))
+            fins, whys, parts, moved = f2, w2, part, True
+            if sum(part) < best:
+                best, keep = sum(part), list(order)
+    ORDER.append(keep)
+    ORDER.append([replay(keep, 0, m, fins[k], whys[k]) for k, m in enumerate(mach)] + base)
+    return [ops[i] for i in keep]
 
 
 def rank_program(g, core, T, topo):
     rank = T.rank_of(core)
     if rank is None:
-        for c in T.cores:
-            if helper_of(c, T, topo) == core:
-                helper_program(g, core, c, T, topo)
         return
     N = len(T.cores)
-    turn, now, edges, named = [], [0, -9], [], {}
+    edges, named, now = [], {}, [-1]
     ops = []
 
-    def s(n, a=0, b=None, st=1, rows=128):
+    def s(n, a=0, b=None, st=1, rows=128, r0=0):
         b = SCRATCH[n][1][1] if b is None else b
-        return (T[n][0:rows, a:b] if st == 1 else T[n][0:rows, a:b:st], [(n, a, b)], [], len(range(a, b, st)))
+        return (T[n][r0:r0 + rows, a:b] if st == 1 else T[n][r0:r0 + rows, a:b:st], [(n, a, b)], [], len(range(a, b, st)))
+
+    def lanes(n, a, b):
+        return s(n, a * 128, b * 128)
 
     def ind(w, o):
         return (w[0].indirect(o[0]), w[1], o[1], 16 * o[3])
 
-    def rec(q, fn, outs, ins, c, tok=None, lat=0.0, aft=None):
+    def rec(q, fn, outs, ins, c, tok=None, lat=0.0):
         rd, wr = [], []
         for x in ins:
             if isinstance(x, tuple):
@@ -360,22 +361,15 @@ def rank_program(g, core, T, topo):
         for x in outs:
             wr += x[1]
             rd += x[2]
-        ops.append((q, fn, rd, wr, tok, c, lat, aft))
-        turn.append(now[0])
-        if q in "va" and outs[0][1]:
-            x = outs[0][1][0][0]
-            named.setdefault((now[1], q, x if SCRATCH[x][0] == "psum" else x.rstrip("01")), []).append(len(ops) - 1)
+        ops.append((q, fn, sorted(set(rd)), sorted(set(wr)), tok, c, lat))
+        if outs and outs[0][1]:
+            named.setdefault((now[0], q, outs[0][1][0][0]), []).append(len(ops) - 1)
         return len(ops) - 1
-
-    def at(h, step):
-        now[0] = 100 * h + STEP[step]
-        now[1] = -9 if step == "const" else h
 
     def v(x):
         return x[0] if isinstance(x, tuple) else x
 
-    def cost(o, a, f=1.0, fix=None):
-        fix = FIXV if fix is None else fix
+    def cost(o, a, f=1.0, fix=FIXV):
         if o[2]:
             return FIXG + o[3] * SCA * CYC
         if a[2]:
@@ -407,32 +401,31 @@ def rank_program(g, core, T, topo):
     def scan(o, a, b, op0, op1):
         rec("v", lambda: g.vector.tensor_tensor_scan(o[0], a[0], b[0], 0.0, op0, op1), [o], [a, b], cost(o, a, half(o, a, b)))
 
-    def act(o, a, f=AF.Identity, bias=0.0, scale=1.0, acc=None, more=0.0, aft=None):
+    def act(o, a, f=AF.Identity, bias=0.0, scale=1.0, acc=None, more=0.0):
         if acc is None:
             return rec("a", lambda: g.scalar.activation(o[0], a[0], f, v(bias), v(scale)), [o], [a, bias, scale],
-                       cost(o, a, 1.0, FIXA) + more, None, 0.0, aft)
-        else:
-            rec("a", lambda: g.scalar.activation(o[0], a[0], f, v(bias), v(scale), accum_out=acc[0]), [o, acc],
-                [a, bias, scale], cost(o, a, 1.0, FIXA) + 20)
+                       cost(o, a, 1.0, FIXA) + more)
+        return rec("a", lambda: g.scalar.activation(o[0], a[0], f, v(bias), v(scale), accum_out=acc[0]), [o, acc],
+                   [a, bias, scale], cost(o, a, 1.0, FIXA) + 20)
 
-    def mv(q, o, a):
-        (act if q == "a" else cp)(o, a)
+    def mms(L):
+        return rec("p", lambda: [g.tensor.matmul(o[0], l[0], r[0], st, sp) for o, l, r, st, sp in L][-1], [x[0] for x in L],
+                   [x[1] for x in L] + [x[2] for x in L],
+                   sum(FIXP + max(min(64, l[3]), r[3]) * PEC * (4 if SCRATCH[r[1][0][0]][2] == F32 else 1) for o, l, r, st, sp in L))
 
     def mm(o, l, r, st, sp):
-        return rec("p", lambda: g.tensor.matmul(o[0], l[0], r[0], st, sp), [o], [l, r],
-                   max(64, r[3]) * PEC * (4 if SCRATCH[r[1][0][0]][2] == F32 else 1), None, PLAT)
+        return mms([(o, l, r, st, sp)])
 
     def group(o, pairs):
         return [mm(o, l, r, i == 0, i == len(pairs) - 1) for i, (l, r) in enumerate(pairs)]
 
     def iota(o, pat, base, cm, fl=True):
         if fl:
-            rec("g", lambda: g.iota(o[0], pat, base, cm, allow_small_or_imprecise_dtypes=True), [o], [], 130 + 2 * CYC * o[3])
-        else:
-            rec("g", lambda: g.iota(o[0], pat, base, cm), [o], [], 130 + 2 * CYC * o[3])
+            return rec("g", lambda: g.iota(o[0], pat, base, cm, allow_small_or_imprecise_dtypes=True), [o], [], 130 + 2 * CYC * o[3])
+        return rec("g", lambda: g.iota(o[0], pat, base, cm), [o], [], 130 + 2 * CYC * o[3])
 
-    def sel(o, a, pat, op, fill, base, cm, more=()):
-        return rec("g", lambda: g.affine_select(o[0], a[0], pat, op, fill, base, cm), [o], [a] + list(more), 170 + 2 * CYC * o[3])
+    def sel(o, a, pat, op, fill, base, cm):
+        return rec("g", lambda: g.affine_select(o[0], a[0], pat, op, fill, base, cm), [o], [a], 170 + 2 * CYC * o[3])
 
     def gcopy(o, a):
         return sel(o, a, [[0, o[3]]], ALU.is_ge, 0.0, 0, 0)
@@ -440,9 +433,13 @@ def rank_program(g, core, T, topo):
     def diag(o, a, c, off=0):
         sel(o, a, [[-1, 128]], ALU.not_equal, c, -off, 1)
 
-    def dma(q, o, a, sem, lat, c=80.0, **kw):
-        e = {"s": g.sync, "a": g.scalar, "g": g}[q]
-        rec(q, lambda: e.dma_start(o[0], a[0], **kw).then_inc(T.sem[sem], 16), [o], [a], c, (sem, 16), lat)
+    def dmas(q, pairs, sem, lat):
+        e = {"s": g.sync, "a": g.scalar}[q]
+        return rec(q, lambda: [e.dma_start(o[0], a[0]).then_inc(T.sem[sem], 16) for o, a in pairs], [o for o, a in pairs],
+                   [a for o, a in pairs], 80.0 * len(pairs), (sem, 16 * len(pairs)), lat)
+
+    def dma(q, o, a, sem, lat):
+        return dmas(q, [(o, a)], sem, lat)
 
     nloc = [0]
 
@@ -451,44 +448,24 @@ def rank_program(g, core, T, topo):
         eng = topo.engines(core, dst)[:8]
         nloc[0] += len(eng)
         i = rec("g", lambda: g.remote_dma(o[0], a[0], T.sem[sem], T.sem.loc, pid, rid, bits(eng)), [], [a], c, ("loc", 0))
-        rec("x", None, [o], [], 0.0, (sem, len(topo.engines(src, core)[:8])), REM, i)
+        edges.append((i, rec("x", None, [o], [], 0.0, (sem, len(topo.engines(src, core)[:8])), REM)))
         return i
 
     prv, nxt = T.cores[(rank - 1) % N], T.cores[(rank + 1) % N]
-    hlp = helper_of(core, T, topo)
-    hall = topo.engines(core, hlp)
-    nfold = [0, 0]
-
-    def fold(h):
-        heng = hall if h >= NH - 2 else hall[len(hall) // 2:]
-        pr = "PR%d" % (h & 1)
-        src = [s(pr, k * 128, k * 128 + FW) for k in range(0, OPT["lf"] if h == NH - 1 else 16, FW // 128)]
-        if h >= 2:
-            src.append(s("AC", (h - 2) * FW, (h - 1) * FW))
-        rid, pid = topo.addr(hlp, core)
-        nfold[h & 1] += len(heng)
-        t = RemoteDMATransfer(dst_ids=[DstId(rid=rid, pnc=pid)], dma_engine_mask=bits(heng), remote_sem=T.sem["fa%d" % h],
-                              srcs=[x[0] for x in src], dsts=[T.HB[:, h * FW:(h + 1) * FW]], alu_op=1)
-        i = rec("g", lambda: g.remote_dma_fused([t], local_sem=T.sem["fl%d" % (h & 1)]), [], src, 300.0,
-                ("fl%d" % (h & 1), nfold[h & 1]), 1200.0 + 20.0 * FW * len(src) / len(heng))
-        rec("x", None, [s("AC", h * FW, (h + 1) * FW)], [], 0.0, ("fb%d" % h, len(hall) // 2), 2300.0 + 2 * FW, i)
-        return i
 
     def dr(t):
         return (t, [], [], 0)
 
     add, sub, mul, mx, mn = ALU.add, ALU.subtract, ALU.mult, ALU.max, ALU.min
-    MAG, MG1 = 1.5 * 2.0 ** 31, 1.5 * 2.0 ** 23
-    dma("a", s("PEPO", 8, 16), dr(T.po[:]), "dpo", 1700.0)
-    dma("a", s("PEPO", 0, 8), dr(T.pe[:]), "dpe", 1700.0)
-    for c, (a, b) in enumerate(((0, 512), (512, 1024), (1024, 2048))):
-        dma("s", s("LK", a, b), dr(T.lk[:, a:b]), "dl%d" % c, 1650.0 + 0.8 * b)
-    dma("s", s("EM"), dr(T.em[:]), "dem", 4100.0)
+    MAG, EOF = 1.5 * 2.0 ** 31, 1800.0
+    la = [dma("a", s("PEPO", 8, 16), dr(T.po[:]), "dpo", 1700.0), dma("a", s("PEPO", 0, 8), dr(T.pe[:]), "dpe", 1700.0)]
+    ls = [dma("s", s("LK", a, b), dr(T.lk[:, a:b]), "dl%d" % c, 1650.0 + 0.8 * b) for c, (a, b) in enumerate(((0, 512), (512, 1024), (1024, 2048)))]
+    ls.append(dma("s", s("XR", rows=1), dr(T.xb[:, 0]), "dxb", 3300.0))
+    ls.append(dma("s", s("EM", 0, 2048), dr(T.em[:]), "dem", 4100.0))
     for i, t in enumerate((T.nub, T.nua, T.vd)):
         if i == 2:
-            dma("s", s("OB", 0, 256), dr(T.ob[:]), "dob", 4400.0)
-            dma("s", s("XR", rows=1), dr(T.xb[:, 0]), "dxb", 4400.0)
-        dma("s", s("RN", i * 128, (i + 1) * 128, rows=48), dr(t[:]), "dn%d" % i, 4500.0)
+            ls.append(dma("s", s("OB", 0, 256), dr(T.ob[:]), "dob", 4400.0))
+        ls.append(dma("s", s("RN", i * 128, (i + 1) * 128, rows=48), dr(t[:]), "dn%d" % i, 4500.0))
 
     def pc(i):
         return s("PC", i, i + 1)
@@ -499,13 +476,14 @@ def rank_program(g, core, T, topo):
     def st(k):
         return s("ST", k * 128, (k + 1) * 128)
 
-    at(0, "const")
-    ZB, ID, ID32, IDN, IDM, BO = s("ZB", 0, 128), s("ID"), s("ID32"), s("IDN"), s("IDM"), s("BO")
-    ms(s("ZB", 0, 144), 0.0)
+    def pair(j):
+        return s("DN", 384 + j * 128, 512 + j * 128)
+
+    ZB, ID, ID32, IDN, IDM, BO = s("ZB", 0, 128), s("ID", 16, 144), s("ID32"), s("IDN"), s("IDM"), s("BO")
+    ms(s("ZB", 0, 160), 0.0)
     k16 = act(s("K16"), s("ZB", 0, 144), AF.Exp, bias=math.log(16.0), more=1300.0)
-    ms(s("ZB", 144, 512), 0.0)
-    for n in ("Z32", "ZS", "Z1", "AB", "ZP"):
-        ms(s(n), 0.0)
+    for x in (s("ZS"), s("Z1"), s("AB", 160, 208), s("AB", 336, 352)):
+        ms(x, 0.0)
     iota(s("PI", 0, 1), [[0, 1]], 0, 1, False)
     iota(s("COLG"), [[1, 8], [0, 16]], 0, 0)
     iota(s("COLK"), [[1, 16]], 0, 0)
@@ -514,32 +492,41 @@ def rank_program(g, core, T, topo):
     send(nxt, prv, s("LU", 16, 24), s("LU", 24, 32), "pox", 1300.0)
     cp(s("LU", 8, 16), s("PEPO", 0, 8))
     cp(s("L16", 0, 16), s("PEPO"))
-    diag(ID32, s("Z32"), 1.0)
-    for n, c in (("IDM", -512.0), ("ID", 1.0)):
-        diag(s(n), ZB, c)
-    diag(s("IDE"), s("Z32"), 1143 / (4096 * math.log(2.0)))
-    for n, c in (("IC1", 1143.0), ("IS1", -1396.0)):
-        ts(s(n), ID, c, mul)
+    diag(IDM, ZB, -512.0)
+    sel(s("ID"), s("ZB", 0, 160), [[-1, 160]], ALU.not_equal, 1.0, 16, 1)
+    act(ID32, ID)
     for n, c in (("IDN", -1.0), ("ID2K", 2048.0), ("IDB", 65536.0)):
         act(s(n), ID, scale=c)
+    diag(s("DR", 0, 128), IDN, 1.0, -2)
+    for k in range(2):
+        gcopy(s("DR", k, 128, 16), s("ID", 30 + k, 158, 16))
+    for k in range(4):
+        act(s("DR", 128 + 128 * (k // 2) + k % 2, 256 + 128 * (k // 2), 2), s("DR", k // 2, 128, 2))
+    act(s("IDE"), s("DR", 128, 384), scale=1143 / (4096 * math.log(2.0)))
+    for a, c in ((0, 1143.0), (256, -1396.0)):
+        act(s("IC", a, a + 256), s("DR", 128, 384), scale=c)
     p0 = s("PI", 0, 1)
+    ts(s("PI", 8, 9), p0, 15, ALU.bitwise_and, 1, ALU.arith_shift_right)
+    ts(s("PI", 9, 10), p0, 1, ALU.bitwise_and)
+    cp(s("PC", 27, 29), s("PI", 8, 10))
     ts(s("PI", 1, 2), p0, 15, ALU.bitwise_and)
     ts(s("PI", 2, 3), p0, 4, ALU.arith_shift_right)
     ts(s("PI", 3, 4), p0, 7, ALU.bitwise_and)
     ts(s("PI", 4, 5), p0, 3, ALU.arith_shift_right, 1, ALU.bitwise_and)
     tt(s("PI", 5, 6), p0, s("PI", 2, 3), add)
     ts(s("PI", 6, 7), s("PI", 5, 6), 1, ALU.bitwise_and)
+    ts(s("PI", 7, 8), p0, 4, ALU.arith_shift_right, 1, ALU.bitwise_and)
     cp(s("PC", 1, 3), s("PI", 1, 3))
-    cp(s("PC", 3, 7), s("PI", 3, 7))
+    cp(s("PC", 3, 8), s("PI", 3, 8))
     ts(BO, s("COLG"), pc(2), ALU.is_equal)
-    ts(s("RM"), s("COLK"), pc(1), ALU.is_equal)
+    ts(s("RM", 0, 16), s("COLK"), pc(1), ALU.is_equal)
     for k in range(16):
         if k < OPT["stv"]:
             ts(st(k), BO, rm(k), mul)
         else:
             act(st(k), BO, scale=rm(k))
-    ts(pc(7), pc(6), 144.0, mul, pc(4), add)
-    ts(pc(8), pc(3), 16.0, mul, pc(7), add)
+    ts(pc(0), pc(6), 144.0, mul, pc(4), add)
+    ts(pc(8), pc(3), 16.0, mul, pc(0), add)
     ts(s("PERM"), s("C2"), pc(8), add)
     act(pc(9), rm(15), bias=-MAG, scale=2.0 ** 20)
     act(pc(10), pc(1), bias=0.5)
@@ -549,14 +536,15 @@ def rank_program(g, core, T, topo):
     act(pc(20), rm(15), bias=1.0, scale=-1.0)
     act(pc(21), rm(15), bias=-1.0)
     act(pc(14), rm(15), bias=-16.0, scale=16.0)
-    act(pc(16), pc(1), bias=S0 - 1.0, scale=16.0)
-    act(pc(17), pc(1), scale=1.0 / 256)
+    act(pc(15), rm(15), bias=-0.5, scale=2048.0)
+    act(pc(16), rm(15), scale=65536.0)
     act(pc(18), rm(0), scale=512.0)
-    act(pc(19), rm(14), scale=-1.0)
-    act(s("ZP", 136, 144), s("C2"), bias=pc(17), scale=1.0 / 32)
-    iota(s("POSB"), [[2, 128]], -128, 0)
-    ts(s("ZP", 144, 272), s("POSB"), 1.0 / 512, mul)
-    for a in (144, 288):
+    ts(pc(19), pc(1), 13.5, ALU.is_gt, -1.0, mul)
+    for w in range(3):
+        ts(pc(24 + w), pc(1), 1.5, ALU.is_lt, math.log(0.5 ** (2.5 - w)) + EOF / 4096, mul)
+    act(pc(22), pc(7), bias=1.0, scale=-1.0)
+    act(pc(23), pc(7), bias=-EOF, scale=EOF)
+    for a in (0, 144, 288):
         ms(s("CR", a, a + 8), 0.0)
     for c in range(4):
         a, b = c * 512, (c + 1) * 512
@@ -564,115 +552,114 @@ def rank_program(g, core, T, topo):
         ts(s("CW", a, b), s("LK", a, b), -128.0, add, MAG, add)
         act(bk, s("CW", a, b), bias=pc(9))
         tt(s("TB", a, b), s("LK", a, b), bk, add)
-    for r in range(16):
-        mm(s("P6", r, 256, 16), st(r), s("L16", 0, 16), True, True)
+    mms([(s("P6", r, 256, 16), st(r), s("L16", 0, 16), True, True) for r in range(16)])
     cp(s("INI"), s("P6", 0, 256))
     cp(s("L16", 16, 18), s("LU", 22, 24))
-    ms(s("E0"), 0.0)
+    ms(s("CX", 32, 48), 1535.502)
+    ms(s("TB", 2048, 2064), 0.0)
     for i, c in enumerate((-1.0, 1.0, -1.0)):
         ts(s("RB", i * 128, (i + 1) * 128, rows=48), s("RN", i * 128, (i + 1) * 128, rows=48), c / 256, mul)
-    mm(s("P3", 1, 2), s("XR", rows=1), s("ID", 0, 1, rows=1), True, True)
+    mm(s("P3", 1, 2), s("XR", rows=1), s("ID", 16, 17, rows=1), True, True)
     act(s("XB"), s("P3", 1, 2))
+    act(s("EM", 2048, 2064), s("ZB", 0, 16), bias=s("XB"))
     gcopy(s("ZS", 15, 143, 16), s("BO", 0, 128, 16))
     gcopy(s("Z1", 15, 143, 16), s("ST", 0, 128, 16))
-    act(s("ZX"), s("ZS", 0, 128), scale=s("XB"))
     act(s("BO32"), BO)
-    act(s("BO4"), BO, scale=4096.0)
+    act(s("BO4", 0, 128), BO, scale=2.0 ** 17)
+    act(pc(17), pc(1), AF.Exp, bias=15 * math.log(2.0), scale=-math.log(2.0))
+    act(s("BO4", 128, 256), BO, scale=pc(17))
+    iota(s("POSB"), [[0, 8], [-1, 16]], 16, 0)
+    act(s("BO4", 256, 384), s("POSB"), AF.Exp, scale=math.log(2.0))
     act(s("TRI"), BO, scale=pc(21))
     sel(s("TRI"), s("TRI"), [[-1, 128]], ALU.is_gt, 0.0, 0, 1)
-    gcopy(s("TRI", 15, 128, 16), s("ID32", 15, 128, 16))
     diag(s("DIF"), ID, -1.0, -1)
-    gcopy(s("DIF", 0, 128, 16), s("ID", 0, 128, 16))
+    gcopy(s("DIF", 0, 128, 16), s("ID", 16, 144, 16))
     diag(s("DT"), ID, -1.0, 1)
-    gcopy(s("DT", 14, 128, 16), s("ID", 14, 128, 16))
+    gcopy(s("DT", 14, 128, 16), s("ID", 30, 144, 16))
     gcopy(s("DT", 15, 128, 16), s("ZB", 0, 8))
-    act(s("DT32"), s("DT"), scale=1.0 / 512)
-    ts(s("DTN"), s("DT"), -1.0 / 512, mul)
     ts(s("L14"), ID, pc(19), mul)
-    ts(s("D0"), ID, pc(18), mul)
-    act(s("DN"), ID32, scale=pc(11))
+    BA, BC, B1 = s("BB", 0, 128), s("BB", 128, 256), s("BB", 256, 384)
+    act(B1, ID, scale=rm(15))
+    for n, c in ((BA, 2.0 ** 21), (BC, -2.0 ** 17)):
+        ts(n, B1, c, mul)
+    act(s("D0"), ID, scale=pc(18))
+    IDP = s("DN", 256, 384)
+    act(IDP, ID, scale=512.0)
+    act(s("DN", 0, 128), IDP, scale=pc(11))
+    act(s("DN", 128, 256), ID, scale=pc(11))
+    ts(s("RM", 16, 24), s("COLK", 0, 8), pc(27), ALU.is_equal)
+    for j in range(8):
+        (ts(pair(j), BO, rm(16 + j), mul) if j < OPT["prv"] else act(pair(j), BO, scale=rm(16 + j)))
     act(s("S2K"), st(15), scale=-2048.0)
     ts(s("XBN"), BO, s("XB"), mul, -1.0, mul)
     ts(s("ZH"), s("ZS"), 4096.0, mul)
     ts(s("D16"), ID, pc(20), mul, 1.0 / 16, mul)
     ms(s("AQ", 128, 144), 0.0)
-    ts(s("KT"), ZB, pc(16), add)
-    iota(s("DUM"), [[2, 128]], H, 0)
+    iota(s("DUM"), [[2, 128]], H + 16, 0)
     iota(s("CV"), [[512, 96]], 512 * S0 + 128, 0)
-    act(s("ASK", 128, 144), s("RM"), scale=16.0)
-    act(pc(22), s("XB"), bias=-8.0)
-    for f in ("FA", "PW"):
-        act(s(f, 1920, 2048), ZB, bias=pc(22))
-    ts(s("BO8"), BO, 8.0, mul)
-    ts(s("BM", 0, 8), s("COLK", 0, 8), pc(1), ALU.is_equal)
-    gcopy(s("BM", 8, 16), s("BM", 0, 8))
+    act(s("ASK", 128, 144), s("RM", 0, 16), scale=16.0)
+    act(s("BO8"), BO, scale=8.0)
+    iota(s("J8"), [[0, 12], [1, 8]], 0, 0)
+    ts(s("BM", 0, 96), s("J8"), pc(1), ALU.is_equal)
+    ts(s("BM", 96, 112), s("J8", 0, 16), pc(1), ALU.not_equal)
+    tt(s("CV"), s("CV"), s("BM", 0, 96), mul)
     ms(s("CUM", 0, 1), 0.0)
-    ms(s("NN", 128, 144), 0.0)
+    for b in ("P4", "P5"):
+        mm(s(b, 0, 512, 8), ID, s("ZB", 0, 64), True, True)
     for w in (1, 2):
         send(T.cores[(rank - w) % N], T.cores[(rank + w) % N], s("OB", w * 256, (w + 1) * 256), s("OB", 0, 256), "ob%d" % w)
 
     TBW = s("TB", 0, 2048)
-    CH = [(0, 4), (4, 8), (8, 12), (12, 15)]
 
-    def names(lst, a, par, q):
-        a0, t0 = 176 * par, 288 * par
-        mv(q, s("AB", a0 + a, a0 + a + 128), ind(TBW, lst))
-        tr(s("TT", t0, t0 + 128), s("AB", a0 + 32, a0 + 160))
-        tr(s("TT", t0 + 128, t0 + 288), s("AB", a0 + 16, a0 + 176))
-        ts(s("NL", 128 * par, 128 * par + 128), ind(s("TT", t0, t0 + 288), s("PERM")), 1.0 / 512, mul)
-        return s("AB", a0 + 32, a0 + 160)
-
-    def gat(dst, win, a, b, par, bias=0.0, aft=None):
-        return act(s(dst, a * 128, b * 128), ind(win, s("NL", 128 * par + a * 8, 128 * par + b * 8)), bias=bias, aft=aft)
-
-    def weights(o, A, P):
-        if OPT["nm"] == "v":
-            ts(P, A, 2 * MAG, add, 2 * MAG, sub)
+    def tiles(lst, a, par, raw=False):
+        a, n = 176 * par + a, 16 * lst[3]
+        if raw:
+            ts(s("NS", a, a + n), ind(s("LK"), lst), 1.0 / 256, mul, pc(15), add)
         else:
-            act(s("ZZ"), A, bias=2 * MAG)
-            act(P, s("ZZ"), bias=-2 * MAG)
-        tt(o, A, P, sub)
+            ts(s("NS", a, a + n), ind(TBW, lst), 1.0 / 512, mul)
+        act(s("AB", a, a + n), ind(TBW, lst))
+
+    def emis(dst, a, b, par, q, bias=0.0):
+        o, x = s(dst, 16 * a, 16 * b), ind(s("EM"), s("NS", 176 * par + 32 + a, 176 * par + 32 + b))
+        return act(o, x, bias=bias) if q == "a" else ts(o, x, bias, add)
+
+    def weights(o, par, P):
+        a, NF = 176 * par + 32, s("NF", 128 * par, 128 * par + 128)
+        cp(NF, s("NS", a, a + 128))
+        mm(P, IDM, NF, True, True)
+        tt(o, s("AB", a, a + 128), P, add)
+        return NF
 
     CNT = s("P6", 0, 128)
 
-    def repeats(k0, stop):
+    def repeats(o, n, a, k0):
         for c in range(8):
-            act(s("EA", pos[c], pos[c + 1]), s("P7", 384 + 16 * c, 512), AF.Abs, bias=s("KB", k0 + c, k0 + c + 1), scale=-512.0)
-        for a, b in ((0, 3), (3, 8)):
-            act(s("EQ", pos[a], pos[b]), s("EA", pos[a], pos[b]), AF.Relu, bias=128.0, scale=-1.0)
-        if stop is not None:
-            counts(0, True, stop)
+            ts((T.EQ[:, c, 0:128 - 16 * c], [("EQ", c, c + 1)], [], 128 - 16 * c), s(n, a + 16 * c, a + 128), s("KB", k0 + c, k0 + c + 1), ALU.is_equal)
+        mm(s("P7", 0, 128), IDN, s("BO4", 256, 384), True, False)
+        mms([(s("P7", 16 * c + 16, 128), s("BO4", 0, 128), (T.EQ[:, c, 16:128 - 16 * c], [("EQ", c, c + 1)], [], 112 - 16 * c), False, False)
+             for c in range(7)] + [(s("P7", 0, 128), s("BO4", 128, 256), (T.EQ[:, :, 0:16], [("EQ", 0, 8)], [], 128), False, True)])
+        act(o, s("P7", 0, 128), AF.Relu, bias=4096.0, scale=4096.0)
 
-    pos = [sum(128 - 16 * x for x in range(c)) for c in range(9)]
+    def total(o, hs, more):
+        group(s("P7", 0, 128), [(ID32, x) for x in more + [s("PR", 256 * h + x, 256 * h + x + 128) for h in hs for x in (0, 128)]])
+        act(o, s("P7", 0, 128))
 
-    def counts(a, start, stop, shift=0):
-        for c in range(8):
-            mm(s("P6", a + 16 * c + shift, a + 128), s("BO4"), s("EQ", pos[c], pos[c + 1] - shift), start and c == 0, stop and c == 7)
-
-    def targets(h):
-        tt(s("OF"), s("DUM"), CNT, mn)
-        at(h, "list")
-        for r in range(16):
-            mm(s("P6", 128, 136), s("Z1", 15 - r, 143 - r), s("OF", r, 128, 16), r == 0, r == 15)
-        cp(s("OFU", 8 * (h & 1), 8 * (h & 1) + 8), s("P6", 128, 136))
-
-    sent, folds = {}, {}
-    mm(s("P7", 248, 512), ID, s("ZP", 8, 272), True, False)
-    mm(s("P7", 376, 384), ID, s("L16", 8, 16), False, False)
-    mm(s("P7", 384, 512), ID, s("INI", 128, 256), False, True)
-    act(s("KB", 1, 9), s("P7", 376, 384), scale=512.0)
+    sent = {}
+    cp(s("KB", 1, 9), s("PEPO", 8, 16))
     mm(s("P3", 0, 1), st(15), s("L16", 17, 18), True, True)
-    act(s("KB", 0, 1), s("P3", 0, 1), scale=512.0)
+    act(s("KB", 0, 1), s("P3", 0, 1))
+    repeats(s("CR", 8, 136), "INI", 128, 1)
 
     for h in range(NH):
-        w, par = h >> 1, h & 1
+        w, par, last = h >> 1, h & 1, h == NH - 1
         m0 = S0 + 16 * h
+        now[0] = h
         F = "FB" if par else "FA"
         y0 = 144 * h
-        at(h, "names")
-        Y = s("YS", y0, y0 + 128)
+        Y, KH = s("YS", y0, y0 + 128), s("KH", 128 * h, 128 * h + 128)
         mine = [gcopy(Y, s("OB", w * 256 + par, (w + 1) * 256, 2)), gcopy(s("YS", y0 + 128, y0 + 144), s("EM", m0, m0 + 16)),
-                sel(s("SEL", h * 128, (h + 1) * 128), ZB, [[-NH, 8], [0, 16]], ALU.not_equal, 1.0, -h, 1)]
+                sel(s("SEL", h * 128, (h + 1) * 128), ZB, [[-NH, 8], [0, 16]], ALU.not_equal, 1.0, -h, 1),
+                iota(KH, [[0, 128]], m0 // 16, 0)]
         if h > 1:
             edges.extend((sent[h - 2], i) for i in mine)
         r1, r2, k1, k0 = (h - 1) * SL, (h - 2) * SL, (h - 1) * SL, h * SL
@@ -682,248 +669,230 @@ def rank_program(g, core, T, topo):
             sa, sl, su = s("INI", 128 * h, 128 * h + 128), s("L16", 8 * h, 8 * h + 8), s("LU", 16 * h + 8, 16 * h + 16)
             s0 = s("INI", 0, 1)
         if par == 0:
-            act(s("AB", 1, 33), ind(TBW, s("SU", k1 + 134, k1 + 136) if h else s("LU", 22, 24)))
-            A = names(s("RU", r1 + 128, r1 + 136) if h else s("LU", 24, 32), 33, par, OPT["ag"])
+            if h:
+                tiles(s("SU", k1 + 134, k1 + 136), 1, par)
+                tiles(s("RU", r1 + 128, r1 + 136), 33, par)
+            else:
+                tiles(s("LU", 24, 32), 33, par, True)
+                tiles(s("LU", 22, 24), 1, par, True)
             qa, lr = ([(0, 128, s("RX", r1, r1 + 128))], s("RX", r1, r1 + 127)) if h else ([(0, 128, s("INI", 128, 256))], s("INI", 128, 255))
+            for x in range(8):
+                o, a, m = s("YB", 256 * x, 256 * x + 256), s("OB", 256 * w, 256 * w + 256), s("BO32", 16 * x, 16 * x + 1)
+                if OPT["yb"][w][x] == "a":
+                    act(o, a, scale=m)
+                else:
+                    ts(o, a, m, mul)
         else:
-            qa = [(0, 127, s("PK", k1 + 1, k1 + 128)), (127, 128, s("R0", 4 * h - 4, 4 * h - 3))]
-            A = names(s("SU", k1 + 128, k1 + 136), 32, par, OPT["ag"])
+            qa = [(0, 127, s("PK", k1 + 1, k1 + 128)), (127, 128, s("R0", 8 * h - 8, 8 * h - 7))]
+            tiles(s("SU", k1 + 128, k1 + 136), 32, par)
+        a0 = 176 * par
+        A = s("AB", a0 + 32, a0 + 160)
+        tr(s("TT", 0, 128), A)
+        tr(s("TT", 128, 288), s("AB", a0 + 16, a0 + 176))
+        ts(s("NL"), ind(s("TT"), s("PERM")), 1.0 / 512, mul)
         if 0 < h < NH - 1:
-            at(h, "side" if par else "d")
             cp(s("RX", r1, r1 + 136), s("RU", r1, r1 + 136))
-        at(h, "d")
-        for r in range(4):
-            mm(s("P1", r * 128, (r + 1) * 128), ID, Y, True, True)
-        chf, chc, chi = (OPT[x][KIND[h]] for x in ("chf", "chc", "chi"))
-        at(h, "gather")
+        chf, chc, chi = (OPT[x][KINDS[h]] for x in ("chf", "chc", "chi"))
         for a, b, q in chf:
-            mv(q, s(F, a * 128, b * 128), ind(s("EM"), s("NL", 128 * par + a * 8, 128 * par + b * 8)))
+            emis(F, a, b, par, q)
         for a, b, q in chc:
+            o, x = s("CW", a * 128, b * 128), ind(TBW, s("NL", a * 8, b * 8))
             if q == "a":
-                gat("CW", TBW, a, b, par, 34431.5)
-        at(h, "d")
+                act(o, x, bias=34431.5)
+            else:
+                ts(o, x, 34431.5, add)
         SEL = s("SEL", h * 128, (h + 1) * 128, rows=48)
         mm(s("P2", 256, 512), SEL, s("RB", 0, 256, rows=48), True, True)
-        mv(OPT["dg"], s("DG"), ind(TBW, su))
+        act(s("DG"), ind(TBW, su))
 
-        def withq(bank, a, l, stop):
+        def withq(bank, a, l, start, stop):
             for n, (x, y, q) in enumerate(qa):
-                mm(s(bank, a + x, a + y), l, q, False, stop and n == len(qa) - 1)
+                mm(s(bank, a + x, a + y), l, q, start and n == 0, stop and n == len(qa) - 1)
 
-        at(h, "fit")
-        weights(s("WT"), A, s("P0", 256, 384))
-        group(s("P6", 384, 512), [(IDM, sa), (ID32, A)])
+        def fit(a):
+            act(s("GT", a, a + 128), s("P6", 256 + a, 384 + a), AF.Abs, bias=-256.0)
+            ts(s("CL", a, a + 128), s("GT", a, a + 128), 256.0, mn, -256.0, add)
+            tt(s("CB", a, a + 128), s("CL", a, a + 128), s("P2", 256 + a, 384 + a), mul)
+
+        nq = qa[0][1]
         mm(s("P6", 256, 384), ID32, s("DG"), True, False)
-        withq("P6", 256, IDM, True)
-        act(s("GT"), s("P6", 256, 512), AF.Abs, bias=-256.0)
-        ts(s("CL"), s("GT"), 256.0, mn, -256.0, add)
-        tt(s("CB"), s("CL"), s("P2", 256, 512), mul)
+        mm(s("P6", 256, 256 + nq), IDM, qa[0][2], False, True)
+        fit(0)
         mm(s("P2", 0, 128), s("BO32"), s("CB", 0, 128), True, True)
-        ts(s("U2"), s("P2", 0, 128), 255.0, mn, 1535.502, add)
-        mm(s("P0"), ID, s("ZB"), True, False)
-        for r in range(4):
-            withq("P0", r * 128, IDM, False)
-        for r in range(4):
-            mm(s("P0", r * 128, (r + 1) * 128), IDN, s("U2"), False, r == 3)
-        at(h, "slice")
+        ts(s("U2", 0, 128), s("P2", 0, 128), 255.0, mn, 1535.502, add)
+        NF = weights(s("WT"), par, s("P0", 256, 384))
+        group(s("P6", 384, 512), [(IDM, sa), (IDP, NF), (ID, s("WT"))])
+        fit(128)
+        qz = s("PK", k1 + 1, k1 + 129) if par else qa[0][2]
+        mms([(s("P0", r * 128, r * 128 + 128), IDM, qz, r == 0, False) for r in range(2)])
+        mms([(s("P0", r * 128, (r + 1) * 128), IDN, s("U2", 0, 128), False, r == 1) for r in range(2)])
+        if par:
+            group(s("P3", 0, 1), [(ID32, s("DG", 127, 128)), (IDM, qa[1][2])])
+            act(s("GT", 256, 257), s("P3", 0, 1), AF.Abs, bias=-256.0)
+            ts(s("CL", 256, 257), s("GT", 256, 257), 256.0, mn, -256.0, add)
+            tt(s("CB", 256, 257), s("CL", 256, 257), s("P2", 383, 384), mul)
+            mm(s("P3", 1, 2), s("BO32"), s("CB", 256, 257), True, True)
+            ts(s("U2", 128, 144), s("CX", 32, 48), s("P3", 1, 2), add, 1790.502, mn)
+            group(s("P3", 16, 32), [(IDM, s("R0", 8 * h - 8, 8 * h + 8)), (IDN, s("U2", 128, 144))])
+            act(s("CX", 0, 32), ind(s("TB", 0, 2064), s("NS", a0 + 158, a0 + 160)), bias=34431.5)
+            tt(s("JK", 128, 144), s("CX", 16, 32), s("P3", 16, 32), add)
+            ts(s("IW", 2048, 2064), s("JK", 128, 144), 33024.0, ALU.is_equal)
         group(s("P6", 256, 384), [(ID, s("WT")), (s("BO32"), s("CB", 128, 256))])
         act(s("SG"), s("P6", 256, 384), AF.Sign, bias=-1.0 / 512)
-        at(h, "side")
-        mm(s("P6", 384, 512), s("DN"), A, True, False)
-        withq("P6", 384, s("D0"), True)
-        if OPT["nd"] == "v":
-            ts(s("ND"), s("WT"), -255.0, add, pc(14), mx)
-        else:
-            act(s("JK", 0, 128), s("WT"), AF.Relu, bias=-239.0)
-            act(s("ND"), s("JK", 0, 128), bias=pc(14), scale=pc(20))
-        group(s("P2", 128, 256), [(s("L14"), sa), (s("DT32"), A), (s("DTN"), s("WT"))])
-        TZ = s("P2", 256, 384)
-        group(TZ, [(st(h), s("KT")), (IDN, sa)])
-        at(h, "first")
+        mm(s("P6", 384, 512), s("DN", 0, 128), NF, True, False)
+        mm(s("P6", 384, 512), s("DN", 128, 256), s("WT"), False, False)
+        withq("P6", 384, s("D0"), False, True)
+        act(s("JK", 0, 128), s("WT"), AF.Relu, bias=-239.0)
+        act(s("ND"), s("JK", 0, 128), bias=pc(14), scale=pc(20))
         if par == 0:
             kb = 16 * h
-            ts(s("EQ0", 1, 128), lr, 512.0, mul, s("KB", kb, kb + 1), ALU.is_equal)
-            if h:
-                mm(CNT, ID, s("CR", 144 * w + 7, 144 * w + 135), True, False)
-            else:
-                mm(CNT, ID, ZB, True, False)
-                repeats(1, None)
-                counts(0, False, False, 1)
+            ts(s("EQ0", 1, 128), lr, s("KB", kb, kb + 1), ALU.is_equal)
+            R = s("CR", 144 * w + 7, 144 * w + 135)
+            mm(CNT, ID, R, True, False)
             mm(s("P6", 1, 128), ID, lr, False, False)
             if h:
-                mm(s("P6", 0, 1), ID, s("PK", k1, k1 + 1), False, False)
+                mm(s("P6", 0, 1), ID, s("PK", k1 + 127, k1 + 128), False, False)
             else:
                 mm(s("P6", 0, 1), st(15), s("L16", 17, 18), False, False)
-            mm(s("P6", 1, 128), s("BO4"), s("EQ0", 1, 128), False, True)
+            mm(s("P6", 1, 128), s("BO4", 0, 128), s("EQ0", 1, 128), False, True)
         else:
-            repeats(16 * h + 1, False)
-            mm(CNT, ID, s("PK", k1, k1 + 128), False, True)
+            R = s("EA")
+            repeats(R, "PK", k1, 16 * h + 1)
+            group(CNT, [(ID, s("PK", k1, k1 + 128)), (ID, R)])
         mm(s("P6", 256, 384), s("XBN"), Y, True, False)
+        mm(s("P6", 256, 384), ID, R, False, False)
         if par == 0:
-            if h:
-                mm(s("P6", 256, 384), ID, s("CR", 144 * w + 7, 144 * w + 135), False, False)
-            else:
-                counts(256, False, False, 1)
-            mm(s("P6", 257, 384), s("BO4"), s("EQ0", 1, 128), False, False)
-        else:
-            counts(256, False, False)
+            mm(s("P6", 257, 384), s("BO4", 0, 128), s("EQ0", 1, 128), False, False)
         mm(s("P6", 256, 384), s("S2K"), s("SG"), False, True)
         act(s("NZ"), s("P6", 256, 384), AF.Relu, bias=2049.0)
-        targets(h)
-        at(h, "side")
+        tt(s("OF"), s("DUM"), CNT, mn)
+        mms([(s("P6", 128, 136), s("Z1", 15 - r, 143 - r), s("OF", r, 128, 16), r == 0, r == 15) for r in range(16)])
+        cp(s("OFU", 8 * par, 8 * par + 8), s("P6", 128, 136))
         act(s("AQ", 0, 128), s("P6", 384, 512), bias=pc(12))
-        at(h, "test")
-        group(s("P3", 384, 512), [(SEL, s("RB", 256, 384, rows=48)), (s("D16"), s("K16", 0, 128))])
-        mm(s("P3", 0, 128), s("ZX"), Y, True, False)
+        mm(s("P3", 384, 512), SEL, s("RB", 256, 384, rows=48), True, False)
+        mm(s("P3", 384, 512), s("D16"), s("K16", 0, 128), False, False)
         for a, b, q in chf:
-            tt(s("PW", a * 128, b * 128), s(F, a * 128, b * 128), s("P1", 0, (b - a) * 128), mul)
-            for k in range(a, b):
-                mm(s("P3", 0, 128), s("ZS", 15 - k, 143 - k), s("PW", k * 128, (k + 1) * 128), False, False)
+            mms([(s("P1", 8 * (t % 32), 8 * (t % 32) + 8, rows=16, r0=32 * (t // 32)), s(F, 16 * t, 16 * t + 16),
+                  s("YB", 2 * t + par, 2048, 256), True, True) for t in range(a, b)])
+        act(s("XS"), s("P1", 0, 256), bias=pc(23), scale=pc(22))
+        mms([(s("P3", 32 * c, 32 * c + 32, rows=32, r0=32 * (x // 2)), s("ID", 16 + 32 * c - 16 * (x % 2), 48 + 32 * c - 16 * (x % 2)),
+              s("XS", x, 256, 8), False, False) for c in range(4) for x in range(8)])
         mm(s("P3", 0, 128), s("ID2K"), s("SG"), False, True)
-        act(s("E1"), s("P3", 0, 128), AF.Relu, bias=-2048.0)
+        act(s("E1"), s("P3", 0, 128), AF.Relu, bias=EOF - 2048.0)
         tt(s("EV"), s("E1"), s("P3", 384, 512), mul)
+        mm(s("P1", 128, 256), s("L14"), sa, True, False)
+        mm(s("P1", 128, 256), s("DT"), NF, False, False)
+        mm(s("P1", 128, 256), s("ZS", 0, 128), KH, False, False)
         mm(s("P2", 0, 128), s("ZH", 0, 128), s("K16", 0, 128), True, False)
-        for a, b, q in chc:
-            tt(s("XW", a * 128, b * 128), s("CW", a * 128, b * 128), s("P0", 0, (b - a) * 128), add)
+        if sum(y - x for x, y, q in chc) < 15:
+            act(s("QS"), s("P0", 0, 256), bias=34431.5)
+        for a in range(0, 15, 2):
+            b = min(a + 2, 15)
+            if any(x <= a < y for x, y, q in chc):
+                tt(lanes("XW", a, b), s("CW", a * 128, b * 128), s("P0", 0, (b - a) * 128), add)
+            else:
+                tt(lanes("XW", a, b), ind(TBW, s("NL", a * 8, b * 8)), s("QS", 0, (b - a) * 128), add)
         for a, b in chi:
-            ts(s("IW", a * 128, b * 128), s("XW", a * 128, b * 128), 33024.0, ALU.is_equal)
-            for k in range(a, b):
-                mm(s("P2", 0, 128), s("ZH", 15 - k, 143 - k), s("IW", k * 128, (k + 1) * 128), False, k == 14)
-        at(h, "draw")
+            ts(lanes("IW", a, b), lanes("XW", a, b), 33024.0, ALU.is_equal)
+            if par and b == OPT["late"]:
+                mms([(s("P2", 127, 128), s("ZH", 15 - k, 143 - k), s("IW", 2048 + k, 2049 + k), False, False) for k in range(15)])
+            mms([(s("P2", 0, nq), s("ZH", 15 - k, 143 - k), s("IW", k * 128, k * 128 + nq), False, k == 14) for k in range(a, b)])
         mm(s("P0", 0, 128), s("IDB"), s("NZ"), True, False)
         tt(s("SW"), s("EV"), s("P2", 0, 128), mn)
-        ask = mm(s("P0", 0, 128), s("BO32"), s("SW"), False, True)
+        mm(s("P0", 0, 128), s("BO32"), s("SW"), False, True)
         ts(s("ASK", 0, 128), s("P0", 0, 128), 0.0, ALU.is_le)
-        at(h, "hit")
         tt(s("SE"), s("E1"), s("P2", 0, 128), mn)
-        group(s("P1", 0, 128), [(s("BO32"), s("SW")), (s("TRI"), s("SE"))])
-        ts(s("HIT"), s("P1", 0, 128), 0.0, ALU.is_gt)
-        mm(s("P1", 128, 256), s("DIF"), s("HIT"), True, True)
-        tt(s("NN", 0, 128), s("ND"), s("P1", 128, 256), mul)
-        at(h, "g")
+        mm(s("P1", 0, 128), s("BO32"), s("SW"), False, False)
+        mm(s("P1", 0, 128), s("TRI"), s("SE"), False, False)
+        scan(s("CUM", 1, 145), s("ASK"), s("K16"), add, mn)
+        mm(s("P1", 0, 128), BA, s("ASK", 0, 128), False, False)
+        mms([(s("P1", 0, 128), BC, s("CUM", 0, 128), False, False), (s("P1", 128, 256), B1, s("CUM", 0, 128), False, True)])
+        ts(s("HIT"), s("P1", 0, 128), pc(16), ALU.is_gt)
+        tt(s("XX"), s("HIT"), s("P1", 128, 256), mul)
+        mm(s("P0", 128, 256), s("DIF"), s("HIT"), True, True)
+        tt(s("NN", 0, 128), s("ND"), s("P0", 128, 256), mul)
         tt(s("SV"), s("SG"), s("P2", 0, 128), mn)
         act(s("ES"), s("P3", 0, 128))
-        arg = group(s("P3", 256, 384), [(s("IDE"), s("ES")), (s("IS1"), s("SG")), (s("IC1"), s("SV"))])
-        at(h, "hit")
-        tt(s("XX"), s("HIT"), s("P2", 128, 256), mul)
-        at(h, "g")
-        gb = math.log(0.5 ** (2.5 - w))
-        GH, GL = s("GH", 128 * par, 128 * par + 128), s("GL", 128 * par, 128 * par + 128)
-        act(s("P3", 128, 256), s("P3", 256, 384), AF.Exp, bias=gb, scale=math.log(2.0) / 1143)
-        act(GH, s("P3", 128, 256))
-        tt(GL, s("P3", 128, 256), GH, sub)
-        at(h, "draw")
-        PL, PB, PX = s("P7", 376, 384), s("P7", 248, 376), s("P7", 384, 512)
-        last = h == NH - 1
-        mm(s("P7", 248, 512), ID, s("ZP", 8, 272), True, False)
-        mm(PL, ID, sl, False, False)
-        for o in () if last else (PB, PX):
-            mm(o, ID, sa, False, False)
-        for r in range(16):
-            mm(PL, s("ZS", 15 - r, 143 - r), s("XX", r, 128, 16), False, False)
-        for o in () if last else (PB, PX):
-            mm(o, BO, s("XX"), False, False)
+        for x in (0, 128):
+            group(s("P3", 256 + x, 384 + x), [(s("IDE", x, x + 128), s("ES")), (s("IC", 256 + x, 384 + x), s("SG")), (s("IC", x, x + 128), s("SV"))])
+        GL = s("GL", 256 * par, 256 * par + 256)
+        act(s("P3", 0, 256), s("P3", 256, 512), AF.Exp, bias=pc(24 + w), scale=math.log(2.0) / 1143)
+        act(s("GH"), s("P3", 0, 256), scale=pc(28))
+        tt(GL, s("P3", 0, 256), s("GH"), sub)
+        PL, PX = s("P7", 376, 384), s("P7", 248, 376)
+        for x in range(2) if h == NH - 2 else ():
+            total(s("PR", 1536 + 128 * x, 1664 + 128 * x), (x, x + 2), [])
+        if last:
+            total(s("YA", 0, 256, 2), (h - 1,), [s("PR", 1536, 1664)])
+        mm(PL, ID, sl, True, False)
+        if not last:
+            mm(PX, ID, sa, False, False)
         if par == 0:
-            at(h, "early")
-            ts(s("E0", 32, 33), s("P2", 256, 257), 1.0, add, s("ASK", 0, 1), mul)
-            group(s("P6", 256, 257), [(ID, s0), (st(0), s("E0", 32, 33)), (BO, s("XX", 0, 1))])
-            cp(s("E0", 4 * h, 4 * h + 1), s("P6", 256, 257))
-            sent[h] = send(prv, nxt, s("R0", 4 * h, 4 * h + 8), s("E0", 4 * h, 4 * h + 8), "re%d" % h)
-            at(h, "draw")
-        scan(s("CUM", 1, 145), s("ASK"), s("K16"), add, mn)
-        act(s("JK"), s("CUM", 1, 145), AF.Sign, bias=pc(10), scale=-1.0, acc=s("IAC", 0, 1))
-        group(s("P0", 128, 256), [(ID, s("CUM", 1, 129)), (IDN, s("CUM", 0, 128))])
-        tt(s("ZZ"), s("CUM", 1, 129), TZ, add)
-        tt(s("YY"), s("ZZ"), s("P0", 128, 256), mul)
-        for r in range(16):
-            mm(PL, s("Z1", 15 - r, 143 - r), s("YY", r, 128, 16), False, last and r == 15)
-        for o in () if last else (PB, PX):
-            i = mm(o, st(0), s("YY"), False, o is PX)
+            group(s("P6", 256, 257), [(ID, s0), (BO, s("XX", 0, 1))])
+            ts(s("E0", 8 * h, 8 * h + 16), s("ZB", 0, 16), s("P6", 256, 257), add)
+            sent[h] = send(prv, nxt, s("R0", 8 * h, 8 * h + 16), s("E0", 8 * h, 8 * h + 16), "re%d" % h)
+        mms([(PL, s("ZS", 15 - r, 143 - r), s("XX", r, 128, 16), False, last and r == 15) for r in range(16)]
+            + ([] if last else [(PX, BO, s("XX"), False, True)]))
+        act(s("JC"), s("CUM", 1, 145), AF.Sign, bias=pc(10), scale=-1.0, acc=s("IAC", 0, 1))
         if last:
             cp(s("SU", k0 + 128, k0 + 136), PL)
         else:
             cp(s("SU", k0, k0 + 136), s("P7", 248, 384))
             if h != NH - 2:
-                at(h, "draw" if par else "kb")
                 sent[h] = send(prv, nxt, s("RU", k0, k0 + 136), s("SU", k0, k0 + 136), "rx%d" % h)
-            at(h, "repeats" if par else "draw")
-            cp(s("PK", k0, k0 + (1 if par else 128)), s("P7", 375 if par else 248, 376))
-            at(h, "repeats" if par else "kb")
-            act(s("KB", 16 * h + 16, 16 * h + 25), s("P7", 375, 384), scale=512.0)
-        at(h, "draw")
+            cp(s("PK", k0, k0 + 130), s("SU", k0, k0 + 130))
+            act(s("KB", 16 * h + 16, 16 * h + 25), s("P7", 375, 384))
         IDX = s("IDX", 0, 1)
         ts(IDX, s("IAC", 0, 1), 0.5, mul, 72.0, add)
-        tt(s("G1", 0, 16), ind(s("AB", 176 * par + 32, 176 * par + 176), IDX), s("CV", 16 * h, 16 * h + 16), sub)
+        tt(s("G1", 0, 16), ind(s("AB", a0 + 32, a0 + 176), IDX), s("BM", 96, 112), mul)
         act(s("EM", m0, m0 + 16), ind(s("YS", y0, y0 + 144), IDX))
-        tt(ind(s("NN"), IDX), s("G1", 0, 16), s("BM"), mul)
+        tt(ind(s("AB", a0 + 32, a0 + 176), IDX), s("G1", 0, 16), s("CV", 16 * h, 16 * h + 16), add)
         tt(ind(s("TB"), s("OFU", 8 * par, 8 * par + 8)), A, s("NN", 0, 128), sub)
         act(s("IAC", 1, 2), s("IAC", 0, 1), AF.Sign, bias=-111.0)
         ts(s("IDX", 2, 3), s("IAC", 1, 2), 128.0, mul, pc(13), add)
-        mv(OPT["tbm"], s("G1", 16, 32), ind(s("AQ"), IDX))
+        act(s("G1", 16, 32), ind(s("AQ"), IDX))
         cp(ind(s("TB", m0, m0 + 272), s("IDX", 2, 3)), s("G1", 16, 32))
         if par and not last:
-            at(h, "repeats")
-            repeats(16 * h + 17, True)
-            act(s("CS", 128 * w, 128 * w + 128), CNT)
+            repeats(s("CS", 128 * w, 128 * w + 128), "PK", k0, 16 * h + 17)
             sent[h] = send(prv, nxt, s("CR", 144 * w + 152, 144 * w + 280), s("CS", 128 * w, 128 * w + 128), "cx%d" % w)
-        at(h, "g" if last else ("sums", "sums1")[par])
-        for c, (a, b) in enumerate(OPT["chl"] if last else OPT["chg"][par]):
-            bk = "P%d" % (4 + (c & 1))
-            for k in range(a, b + (b == 15)):
-                group(s(bk, (k - a) * 128, (k - a) * 128 + 128), [(st(k), GH), (st(k), GL)])
-            tt(s("PR%d" % par, a * 128, b * 128), s(F, a * 128, b * 128), s(bk, 0, (b - a) * 128), mul)
-            if b == 15:
-                act(s("PR%d" % par, 1920, 2048), s(bk, (15 - a) * 128, (16 - a) * 128), scale=s("XB"))
-            if last and b == OPT["lf"]:
-                fold(h)
-            for k in range(a, b + (b == 15)) if last and a >= OPT["lf"] else ():
-                mm(s("P7", 0, 128), ID32, s("PR1", k * 128, (k + 1) * 128), k == OPT["lf"], False)
+        for c in range(4):
+            bk, e, t0 = "P%d" % (4 + c % 2), c // 2, 64 * (c % 2)
+            g0 = 256 * par + 128 * e + t0
+            mms([(s(bk, j, 512, 8), pair(j), s("GL", g0, g0 + 64), True, True) for j in range(1, 8)])
+            for x, y in OPT["sc"]:
+                scan(s("SC", 512 * c + x, 512 * c + y), s(bk, x, y), s(F, 16 * t0 + 2 * x + e, 16 * t0 + 2 * y, 2), mul, add)
+        mm(s("P4", 1, 512, 2), pair(0), GL, True, True)
+        tt(s("PR", 256 * h, 256 * h + 256), s("SC", 7, 2048, 8), s("P4", 1, 512, 2), mul)
         if last:
-            a = h if OPT["lf"] else h - 2
-            for x in range(0, FW, 128):
-                mm(s("P7", 0, 128), ID32, s("AC", a * FW + x, a * FW + x + 128), False, x == FW - 128)
-            act(s("YA", 1, 256, 2), s("P7", 0, 128))
-        else:
-            edges.append((sent[h], fold(h)))
-    at(NH, "names")
+            total(s("YA", 1, 256, 2), (h,), [s("PR", 1664, 1792)])
+    now[0] = NH
     for par in range(2):
         F = "PW" if par else "FA"
-        A = names(s("SU", (4 + par) * SL + 128, (4 + par) * SL + 136), 32, par, "a")
+        tiles(s("SU", (4 + par) * SL + 128, (4 + par) * SL + 136), 32, par)
         for a, b, q in OPT["zq"][par]:
-            if q == "a":
-                gat(F, s("EM"), a, b, par, -8.0)
-            else:
-                ts(s(F, a * 128, b * 128), ind(s("EM"), s("NL", 128 * par + a * 8, 128 * par + b * 8)), -8.0, add)
+            emis(F, a, b, par, q, -8.0)
         WB = s("WB", 128 * par, 128 * par + 128)
-        weights(WB, A, s("P%d" % (2 + par), 128, 256))
+        weights(WB, par, s("P%d" % (2 + par), 128, 256))
         mm(s("P%d" % (2 + par), 0, 128), s("BO8"), WB, True, False)
-        for c, (a, b) in enumerate(OPT["zp"][par]):
-            bk = ("P0", "P1", "P6")[(len(OPT["zp"][0]) * par + c) % 3]
-            for k in range(a, b):
-                mm(s(bk, (k - a) * 128, (k - a) * 128 + 128), st(k), WB, True, True)
-            z0 = 2048 * par
-            tt(s("PZ", z0 + a * 128, z0 + b * 128), s(F, a * 128, b * 128), s(bk, 0, (b - a) * 128), mul)
-            for k in range(a, b):
-                mm(s("P%d" % (2 + par), 0, 128), ID, s("PZ", z0 + k * 128, z0 + (k + 1) * 128), False,
-                   (a, b) == OPT["zp"][par][-1] and k == b - 1)
+        for c, (t0, e, d) in enumerate(OPT["zp"][par]):
+            bk, z0, n, m = ("P0", "P1", "P6")[(4 * par + c) % 3], 2048 * par + 512 * c, 32 * d, 16 // d
+            mms([(s(bk, j, 512, m), st(d * j + e), s("WB", 128 * par + t0, 128 * par + t0 + n), True, True) for j in range(m)])
+            tt(s("PZ", z0, z0 + 512), s(F, 16 * t0 + e, 16 * (t0 + n), d), s(bk), mul)
+            mms([(s("P%d" % (2 + par), t0, t0 + n), ID, s("PZ", z0 + j, z0 + 512, m), False, c == 3 and j == m - 1) for j in range(m)])
         act(s("YZ", par, 256, 2), s("P%d" % (2 + par), 0, 128))
-    tt(s("YA", 0, 256, 2), s("AC", 4 * FW, 4 * FW + 128), s("AC", 4 * FW + 128, 4 * FW + 256), add)
     dma("s", dr(T.ya[:]), s("YA"), "dya", 2000.0)
     dma("s", dr(T.yz[:]), s("YZ"), "dyz", 2000.0)
 
-    for q in "sa":
-        loads = [i for i in range(k16 + 1) if ops[i][0] == q]
-        edges.extend(zip(loads, loads[1:]))
-    edges.extend((k16, i) for i in range(k16 + 1, len(ops)) if ops[i][0] == "a" and turn[i] < 100)
+    la.append(k16)
+    edges.extend(zip(la, la[1:]))
+    edges.extend((k16, i) for i in range(k16 + 1, k16 + 99) if ops[i][0] == "a")
+    edges.extend(zip(ls, ls[1:]))
+    line = []
     for q in "va":
-        seq = []
-        for h in [-9] + list(range(NH + 1)):
-            for x in LINE[q][KIND[h]].split():
-                k = (h - 1, q, x[1:]) if x[0] == "-" else (h, q, {"F": "FB" if h & 1 else "FA"}.get(x, x))
-                if named.get(k):
-                    seq.append(named[k].pop(0))
-        edges.extend(zip(seq, seq[1:]))
-    ops = schedule(ops, turn, edges)
+        keys = [(h - x.count("-"), q, x.strip("-")) for h in range(NH + 1) for x in LINE[q][(KINDS + ("end",))[h]].split()]
+        seq = [named[k].pop(0) for k in keys if named.get(k)]
+        line.extend(zip(seq, seq[1:]))
+    ops = schedule(ops, edges, line)
     deps = depends(ops, True)
     clock = {q: {} for q in "vapgsx"}
     at, waits, need = [], [], set()

import math
from concourse.mybir import AluOpType as ALU, ActivationFunctionType as AF

F32, BF, F16, I32, U16 = "float32", "bfloat16", "float16", "int32", "uint16"
H, S0, NH = 2048, 1952, 6
SL = 144
SB = {
    "LK": (2048, I32), "TB": (2320, F32), "EM": (2064, BF), "OB": (768, BF), "XB": (1, F32), "XS": (256, F16), "YB": (2048, BF),
    "PEPO": (16, I32), "RN": (384, I32), "RB": (384, BF), "L16": (20, F16), "INI": (256, F16),
    "RX": (5 * SL, F16), "PK": (6 * SL, F16), "LU": (32, U16), "SU": (6 * SL, U16), "RU": (5 * SL, U16), "CR": (432, BF), "CS": (256, BF),
    "EQ0": (128, BF), "KB": (7 * 16, F32), "AB": (352, F32), "DG": (128, F32), "TT": (288, F32), "NL": (128, U16), "PERM": (8, U16),
    "NS": (352, U16), "NF": (256, F16),
    "FA": (2048, BF), "FB": (2048, BF), "CW": (2048, F32), "CX": (48, F32), "QS": (256, F32), "XW": (2048, BF), "IW": (2064, BF), "PW": (2048, BF),
    "SC": (2048, F32), "PR": (7 * 256, F32), "PZ": (4096, F16), "J8": (96, F32), "DR": (384, BF),
    "CL": (264, BF), "GT": (264, BF), "CB": (264, F32), "U2": (144, F16),
    "WT": (128, BF), "WB": (256, BF), "SG": (128, BF), "ND": (128, BF), "AQ": (144, F32), "YS": (6 * 144, BF),
    "EA": (128, BF), "OF": (128, F16), "OFU": (16, U16), "SV": (128, BF), "SE": (128, F32), "SW": (128, F32),
    "ES": (128, F32), "GH": (256, BF), "GL": (512, BF), "HIT": (128, BF), "ASK": (144, BF), "CUM": (145, BF), "E0": (48, F16), "R0": (48, F16),
    "XR": (128, BF), "XX": (128, F16), "NN": (128, F32), "JK": (144, BF), "JC": (144, BF), "IAC": (2, F32),
    "IDX": (4, U16), "G1": (40, F32), "YA": (256, F32), "YZ": (256, F32),
    "PI": (10, I32), "PC": (40, F32), "RM": (24, F32), "BM": (112, F32), "COLG": (128, F32), "COLK": (16, F32),
    "DUM": (128, F32), "CV": (96, F32), "C2": (8, F32), "BO": (128, BF), "BO32": (128, F32), "BO4": (384, BF),
    "ZS": (143, BF), "Z1": (143, BF), "TRI": (128, F32), "DIF": (128, BF), "DT": (128, BF),
    "L14": (128, BF), "S2K": (128, BF), "XBN": (128, BF), "ZH": (143, BF), "D16": (128, BF), "BB": (384, BF),
    "ID2K": (128, BF), "IDB": (128, BF), "NZ": (128, BF), "E1": (128, F32), "EV": (128, F32),
    "ID": (160, BF), "IDN": (128, BF), "IDM": (128, BF), "ID32": (128, F32),
    "BO8": (128, BF), "IC": (512, F16), "IDE": (256, F32), "DN": (1408, BF), "D0": (128, BF), "ST": (2048, BF), "SEL": (768, BF),
    "ZB": (160, BF), "POSB": (128, BF), "K16": (144, BF), "KH": (768, BF),
}
SCRATCH = {n: ("sbuf", [128, w], d) for n, (w, d) in SB.items()}
SCRATCH["EQ"] = ("sbuf", [128, 8, 128], BF)
for _b in range(8):
    SCRATCH["P%d" % _b] = ("psum", [128, 512], F32)
DMAS = ["dpo", "dpe", "dl0", "dl1", "dl2", "dem", "dob", "dn0", "dn1", "dn2", "dxb", "dya", "dyz"]
SEMAPHORES = (["qv", "qa", "qp", "qg", "loc", "pox", "ob1", "ob2", "cx0", "cx1"] + DMAS + ["rx%d" % h for h in (0, 1, 2, 3)]
              + ["re%d" % h for h in (0, 2, 4)])
CYC, PEC, FIXV, FIXA, FIXG, FIXP, GAT, SCA, REM = 0.85, 0.43, 15.0, 15.0, 60.0, 2.0, 1.56, 3.8, 1800.0
KINDS = ("first", "odd", "even", "odd", "even", "last")
OPT = {"stv": 12, "prv": 0, "sc": [(0, 256), (256, 512)], "late": 12, "yb": ["vvvvaaaa", "aaaaaaaa", "aaaaaaaa"],
       "chf": {k: [(32, 64, "a"), (64, 96, "a"), (96, 128, "a"), (0, 32, "a")] for k in KINDS},
       "chc": {k: [(8, 10, "a") if k in ("odd", "last") else (0, 4, "v"), (10, 12, "a"), (12, 14, "a"), (14, 15, "a")] for k in KINDS},
       "chi": {k: [(0, 4), (4, 8), (8, 12), (12, 14), (14, 15)] for k in KINDS},
       "zq": [[(0, 32, "a"), (32, 64, "a"), (64, 128, "a")], [(0, 32, "a"), (32, 64, "a"), (64, 96, "a"), (96, 128, "a")]],
       "zp": [[(0, 0, 2), (0, 1, 2), (64, 0, 2), (64, 1, 2)], [(0, 0, 2), (0, 1, 2), (64, 0, 1), (96, 0, 1)]]}


def bits(engines):
    m = 0
    for e in engines:
        m |= 1 << e
    return m


def hit(x, y):
    return x[1] < y[2] and y[1] < x[2]


def soft(a, b):
    return (a[0] == b[0] and a[0] in "va" and a[4] is None
            and not any(x[0] == y[0] and hit(x, y) for u, w in ((a[3], b[2] + b[3]), (a[2], b[3])) for x in u for y in w))


def depends(ops, banks):
    deps, last, lastmm, others = [], {}, {}, {}
    for i, (q, fn, rd, wr, tok, c, lat) in enumerate(ops):
        d = set()
        for lst, isw in ((rd, False), (wr, True)):
            for r in lst:
                ps = SCRATCH[r[0]][0] == "psum"
                for (j, r2, w2) in last.get(r[0], []):
                    same = ops[j][0] == q
                    if q == "p" and same:
                        continue
                    if (banks and ps and not same) or ((w2 or isw) and hit(r, r2)):
                        d.add(j)
        if q == "p" and not banks:
            if wr[0][0] in lastmm:
                d.add(lastmm[wr[0][0]])
            lastmm[wr[0][0]] = i
            d |= others.pop(wr[0][0], set())
        elif not banks:
            for r in rd + wr:
                if SCRATCH[r[0]][0] == "psum":
                    others.setdefault(r[0], set()).add(i)
                    if r[0] in lastmm:
                        d.add(lastmm[r[0]])
        if q == "x":
            d = set()
        deps.append(d)
        for lst, isw in ((rd, False), (wr, True)):
            for r in lst:
                old = last.get(r[0], [])
                if isw:
                    old = [e for e in old if not (r[1] <= e[1][1] and e[1][2] <= r[2] and
                                                  (e[0] in d or (q == "p" and ops[e[0]][0] == q)))]
                last[r[0]] = old + [(i, r, isw)]
    return deps


MACHINES = [(1.0, 1.0, 1.0, 205.0, -100.0, 0.0), (1.3, 1.3, 1.1, 160.0, 500.0, 200.0)]
MOVES = 100000
TEMP = 0.002
ANY = 4
EVERY = 4
ORDER = []


REST = "SW SE ASK CUM SV OFU HIT IDX XX G1 NN AB %s IDX TB"
LINE = {
    "v": {"first": "-ZB -PI -PI -PI -PI -PI -PI -PI -PC -PC -BO -RM -ST -ST -ST -ST -ST -ST -ST -ST -ST -ST -ST -ST -LU -LU -L16 "
                   "-CW -CW -INI -TB -CW NS -TB -CW -TB -TB NS NF TT TT CL NL CB WT CW U2 CW CL CB XW XW XW XW IW XW IW OF XW XW IW XW EV IW IW "
                   + REST % "TB SU",
          "even": "NS RX NS TT TT NF CL NL CB WT CW U2 CW CL CB XW XW XW XW IW XW IW OF XW XW IW XW EV IW IW " + REST % "TB SU",
          "odd": "NS TT TT NF EQ EQ EQ EQ CL NL CB WT EQ EQ EQ EQ CW U2 CW CL CB CL CB XW XW U2 XW XW JK XW IW IW IW OF XW XW IW XW EV IW IW " + REST % "SU TB",
          "end": "NS NS NF NF WB WB PW PZ PZ PZ PZ PZ PZ PZ PZ"},
    "a": {"first": "-P4 -P5 -P0 FA -P1 FA DG AB AB GT FA FA GT QS XS SG CW CW CW NZ E1 JK ND AQ ES IAC IAC G1 EM "
                   "P3 GH KB",
          "even": "AB DG AB GT FA FA GT FA QS FA CW XS SG CW CW NZ E1 JK ND AQ ES IAC IAC G1 EM P3 GH KB",
          "odd": "DG AB GT FB FB GT GT FB QS FB CX EA XS SG CW CW CW CW NZ E1 JK ND AQ ES IAC IAC G1 EM P3 GH KB",
          "end": "AB AB FA FA FA PW PW PW PW YZ YZ"}}
for _q in "va":
    LINE[_q]["last"] = LINE[_q]["odd"]


def schedule(ops, edges, line):
    if ORDER:
        return [ops[i] for i in ORDER[0]]
    n = len(ops)
    deps = depends(ops, False)
    data = [set(d) for d in deps]
    for j, i in edges:
        deps[i].add(j)
    suc = [[] for _ in range(n)]
    for i in range(n):
        for j in deps[i]:
            suc[j].append(i)
    Q = {"v": 0, "a": 1, "p": 2, "g": 3, "s": 4, "x": 5}
    qn = [Q[o[0]] for o in ops]
    bank = [sorted(set(int(r[0][1]) for r in o[2] + o[3] if SCRATCH[r[0]][0] == "psum")) if o[0] in "va" else [] for o in ops]
    byidx = [o[0] in "va" and any(SCRATCH[r[0]][2] == U16 for r in o[2]) and not any(SCRATCH[r[0]][2] == F16 for r in o[3]) for o in ops]
    near = [{j: ops[j][0] == ops[i][0] and (ops[i][0] == "p" or j not in data[i]) or soft(ops[j], ops[i]) for j in deps[i]} for i in range(n)]
    mach = []
    for f, pf, gf, hop, rem, call in MACHINES:
        dur = [o[5] * (pf if o[0] == "p" else 1.0 if o[4] else f * (gf if byidx[i] else 1.0)) + (call if o[0] == "g" and o[4] else 0.0)
               for i, o in enumerate(ops)]
        lat = [o[6] + (rem if o[0] == "x" else 0.0) for o in ops]
        mach.append((dur, lat, [[(j, 0.0 if near[i][j] else lat[j] + hop) for j in deps[i]] for i in range(n)], hop))

    def replay(order, a, m, fin, why, z=None):
        dur, lat, need, hop = m
        lastq, lastb = [-1] * 6, [-1] * 16
        for i in order[max(0, a - 100):a]:
            lastq[qn[i]] = i
            for b in bank[i]:
                lastb[2 * b + qn[i]] = i
        for i in order[a:z]:
            q = qn[i]
            x, w = 0.0, -1
            for j, e in need[i]:
                if fin[j] + e > x:
                    x, w = fin[j] + e, j
            j = lastq[q]
            if j >= 0 and q != 5 and fin[j] > x:
                x, w = fin[j], j
            for b in bank[i]:
                j = lastb[2 * b + 1 - q]
                if j >= 0 and fin[j] + hop > x:
                    x, w = fin[j] + hop, j
                lastb[2 * b + q] = i
            lastq[q] = i
            fin[i] = x + dur[i]
            why[i] = w
        return z or max(fin[i] + lat[i] for i in ends) + 0.02 * sum(fin) / n

    ends = [i for i in range(n) if not suc[i]]
    dur, lat, need, hop = mach[0]
    need = [list(x) for x in need]
    for j, i in line:
        need[i].append((j, 0.0))
    after = [[] for _ in range(n)]
    for i in range(n):
        for j, e in need[i]:
            after[j].append(i)
    left, topo_order = [len(d) for d in need], [i for i in range(n) if not need[i]]
    for i in topo_order:
        for k in after[i]:
            left[k] -= 1
            if not left[k]:
                topo_order.append(k)
    assert len(topo_order) == n, "the named order contradicts the calls' needs"
    chain = [0.0] * n
    for i in reversed(topo_order):
        chain[i] += dur[i] + (lat[i] if not suc[i] else 0.0)
        for j, e in need[i]:
            chain[j] = max(chain[j], chain[i] + e)
    left, t, held = [len(d) for d in need], [0.0] * n, [[] for _ in range(6)]
    ready = [i for i in range(n) if not left[i]]
    while ready:
        i = max(ready, key=lambda k: (chain[k], -k))
        ready.remove(i)
        x = max([t[j] + dur[j] + e for j, e in need[i]] + [0.0])
        if qn[i] != 5:
            for a, b in held[qn[i]]:
                if a < x + dur[i] and x < b:
                    x = b
            held[qn[i]].append((x, x + dur[i]))
            held[qn[i]].sort()
        t[i] = x
        for k in after[i]:
            left[k] -= 1
            if not left[k]:
                ready.append(k)
    rank_in = {i: k for k, i in enumerate(topo_order)}
    order = sorted(range(n), key=lambda i: (t[i], rank_in[i]))
    need = mach[0][2]
    outs = [[] for _ in range(n)]
    for i in range(n):
        for j, e in need[i]:
            outs[j].append((i, e))

    def anew(order, a, b, fin, seed):
        tail, nxt = [0.0] * n, [0.0] * 6
        for k in range(min(n, b + 150) - 1, a - 1, -1):
            i = order[k]
            tail[i] = dur[i] + max([lat[i] if not outs[i] else 0.0, nxt[qn[i]]] + [e + tail[x] for x, e in outs[i]])
            if k >= b and qn[i] != 5:
                nxt[qn[i]] = tail[i]
        seg, f, free, used = order[a:b], list(fin), [0.0] * 6, [0.0] * 16
        for i in order[max(0, a - 100):a]:
            free[qn[i]] = f[i]
            for x in bank[i]:
                used[2 * x + qn[i]] = f[i] + hop
        wait, noise, reach = {i: 0 for i in seg}, 100.0 * (seed >> 50 & 7), 0.25 * (seed >> 54 & 3) + 0.25
        for i in seg:
            seed = (seed * 6364136223846793005 + 1442695040888963407) % 2 ** 64
            tail[i] += noise * (seed >> 40 & 1023) / 1024.0
            for x in suc[i]:
                if x in wait:
                    wait[x] += 1
        data = {i: max([f[j] + e for j, e in need[i]] + [0.0]) for i in seg if not wait[i]}
        new = []
        while data:
            est = {i: max([x, free[qn[i]] if qn[i] != 5 else 0.0] + [used[2 * y + 1 - qn[i]] for y in bank[i]]) for i, x in data.items()}
            i = min(est, key=lambda x: (est[x], x))
            i = max((x for x in est if qn[x] == qn[i] and est[x] <= est[i] + reach * (dur[i] + hop)), key=lambda x: (tail[x], -x))
            new.append(i)
            del data[i]
            f[i] = free[qn[i]] = est[i] + dur[i]
            for x in bank[i]:
                used[2 * x + qn[i]] = f[i] + hop
            for x in suc[i]:
                if x in wait:
                    wait[x] -= 1
                    if not wait[x]:
                        data[x] = max([f[j] + e for j, e in need[x]])
        return new

    fins, whys = [[0.0] * n for m in mach], [[-1] * n for m in mach]
    base = [replay(order, 0, m, fins[k], whys[k]) for k, m in enumerate(mach)]
    parts, best = [1.0] * len(mach), float(len(mach))
    keep, seed = list(order), 12345
    place = [0] * n
    for it in range(MOVES):
        if it == 0 or moved:
            for k, i in enumerate(order):
                place[i] = k
            late, chains = [], [[] for m in mach]
            for k, m in enumerate(mach):
                i = max(ends, key=lambda e: fins[k][e] + m[1][e])
                while whys[k][i] >= 0:
                    chains[k].append(place[i])
                    if whys[k][i] not in deps[i]:
                        late.append((whys[k][i], i))
                    i = whys[k][i]
        moved = False
        seed = (seed * 6364136223846793005 + 1442695040888963407) % 2 ** 64
        p, i = late[(seed >> 44) % len(late)]
        if (seed >> 30) % 16 < ANY:
            i = (seed >> 44) % n
            p = whys[0][i]
            if p < 0 or p in deps[i]:
                continue
        a, b, ahead = place[p], place[i], seed >> 43 & 1
        for _ in range(max(0, (seed >> 36) % 16 - 6)):
            x, step = (a - 1, -1) if ahead else (b + 1, 1)
            while 0 <= x < n and qn[order[x]] != qn[i]:
                x += step
            if 0 <= x < n:
                a, b = (x, b) if ahead else (a, x)
        p, i = order[a], order[b]
        b += 1
        seg = order[a:b]
        if it % EVERY == 0:
            a = max(0, a - (seed >> 12) % 40)
            b = min(n, a + 20 + (seed >> 20) % 70)
            seg = anew(order, a, b, fins[0], seed)
        elif ahead:
            take = {i}
            for x in reversed(seg):
                if x in take:
                    take |= deps[x]
            if p in take:
                continue
            seg = [x for x in seg if x in take] + [x for x in seg if x not in take]
        else:
            take = {p}
            for x in seg:
                if x in take:
                    take.update(suc[x])
            if i in take:
                continue
            seg = [x for x in seg if x not in take] + [x for x in seg if x in take]
        new = order[:a] + seg + order[b:]
        room, loss, idle = TEMP * (1.0 - it / MOVES) * ((seed >> 24) % 1024) / 1024.0, 0.0, [0] * n
        for k, m in enumerate(mach):
            c = min([x for x in chains[k] if x >= b] + [n - 1])
            f = list(fins[k])
            replay(new, a, m, f, idle, c + 1)
            loss += (f[new[c]] - fins[k][new[c]]) / base[k]
            if loss > room + 0.004:
                break
        if loss > room:
            continue
        f2, w2 = [list(f) for f in fins], [list(w) for w in whys]
        part = [replay(new, a, m, f2[k], w2[k]) / base[k] for k, m in enumerate(mach)]
        if sum(part) <= sum(parts) + room:
            for k, i in enumerate(new):
                place[i] = k
            order = sorted(new, key=lambda i: (f2[0][i] - dur[i], place[i]))
            fins, whys, parts, moved = f2, w2, part, True
            if sum(part) < best:
                best, keep = sum(part), list(order)
    ORDER.append(keep)
    ORDER.append([replay(keep, 0, m, fins[k], whys[k]) for k, m in enumerate(mach)] + base)
    return [ops[i] for i in keep]


def rank_program(g, core, T, topo):
    rank = T.rank_of(core)
    if rank is None:
        return
    N = len(T.cores)
    edges, named, now = [], {}, [-1]
    ops = []

    def s(n, a=0, b=None, st=1, rows=128, r0=0):
        b = SCRATCH[n][1][1] if b is None else b
        return (T[n][r0:r0 + rows, a:b] if st == 1 else T[n][r0:r0 + rows, a:b:st], [(n, a, b)], [], len(range(a, b, st)))

    def lanes(n, a, b):
        return s(n, a * 128, b * 128)

    def ind(w, o):
        return (w[0].indirect(o[0]), w[1], o[1], 16 * o[3])

    def rec(q, fn, outs, ins, c, tok=None, lat=0.0):
        rd, wr = [], []
        for x in ins:
            if isinstance(x, tuple):
                rd += x[1] + x[2]
        for x in outs:
            wr += x[1]
            rd += x[2]
        ops.append((q, fn, sorted(set(rd)), sorted(set(wr)), tok, c, lat))
        if outs and outs[0][1]:
            named.setdefault((now[0], q, outs[0][1][0][0]), []).append(len(ops) - 1)
        return len(ops) - 1

    def v(x):
        return x[0] if isinstance(x, tuple) else x

    def cost(o, a, f=1.0, fix=FIXV):
        if o[2]:
            return FIXG + o[3] * SCA * CYC
        if a[2]:
            return FIXG + o[3] * GAT * CYC
        return fix + max(64, o[3] * f) * CYC

    def half(*x):
        return 0.5 if all(SCRATCH[y[1][0][0]][2] in (BF, F16, U16) for y in x) else 1.0

    def tt(o, a, b, op):
        f = 1.0 if "psum" in (SCRATCH[a[1][0][0]][0], SCRATCH[b[1][0][0]][0]) else 2.0
        return rec("v", lambda: g.vector.tensor_tensor(o[0], a[0], b[0], op), [o], [a, b], cost(o, a, f))

    def ts(o, a, s1, op0, s2=None, op1=None):
        if op1 is None:
            return rec("v", lambda: g.vector.tensor_scalar(o[0], a[0], v(s1), None, op0), [o], [a, s1], cost(o, a, half(o, a)))
        return rec("v", lambda: g.vector.tensor_scalar(o[0], a[0], v(s1), v(s2), op0, op1), [o], [a, s1, s2],
                   cost(o, a, half(o, a)))

    def cp(o, a):
        return rec("v", lambda: g.vector.tensor_copy(o[0], a[0]), [o], [a], cost(o, a, half(o, a)))

    def ms(o, c):
        rec("v", lambda: g.vector.memset(o[0], c), [o], [], cost(o, o, half(o)))

    def tr(o, a):
        rec("v", lambda: g.vector.transpose(o[0], a[0]), [o], [a], cost(o, a))

    def scan(o, a, b, op0, op1):
        rec("v", lambda: g.vector.tensor_tensor_scan(o[0], a[0], b[0], 0.0, op0, op1), [o], [a, b], cost(o, a, half(o, a, b)))

    def act(o, a, f=AF.Identity, bias=0.0, scale=1.0, acc=None, more=0.0):
        if acc is None:
            return rec("a", lambda: g.scalar.activation(o[0], a[0], f, v(bias), v(scale)), [o], [a, bias, scale],
                       cost(o, a, 1.0, FIXA) + more)
        return rec("a", lambda: g.scalar.activation(o[0], a[0], f, v(bias), v(scale), accum_out=acc[0]), [o, acc],
                   [a, bias, scale], cost(o, a, 1.0, FIXA) + 20)

    def mms(L):
        return rec("p", lambda: [g.tensor.matmul(o[0], l[0], r[0], st, sp) for o, l, r, st, sp in L][-1], [x[0] for x in L],
                   [x[1] for x in L] + [x[2] for x in L],
                   sum(FIXP + max(min(64, l[3]), r[3]) * PEC * (4 if SCRATCH[r[1][0][0]][2] == F32 else 1) for o, l, r, st, sp in L))

    def mm(o, l, r, st, sp):
        return mms([(o, l, r, st, sp)])

    def group(o, pairs):
        return [mm(o, l, r, i == 0, i == len(pairs) - 1) for i, (l, r) in enumerate(pairs)]

    def iota(o, pat, base, cm, fl=True):
        if fl:
            return rec("g", lambda: g.iota(o[0], pat, base, cm, allow_small_or_imprecise_dtypes=True), [o], [], 130 + 2 * CYC * o[3])
        return rec("g", lambda: g.iota(o[0], pat, base, cm), [o], [], 130 + 2 * CYC * o[3])

    def sel(o, a, pat, op, fill, base, cm):
        return rec("g", lambda: g.affine_select(o[0], a[0], pat, op, fill, base, cm), [o], [a], 170 + 2 * CYC * o[3])

    def gcopy(o, a):
        return sel(o, a, [[0, o[3]]], ALU.is_ge, 0.0, 0, 0)

    def diag(o, a, c, off=0):
        sel(o, a, [[-1, 128]], ALU.not_equal, c, -off, 1)

    def dmas(q, pairs, sem, lat):
        e = {"s": g.sync, "a": g.scalar}[q]
        return rec(q, lambda: [e.dma_start(o[0], a[0]).then_inc(T.sem[sem], 16) for o, a in pairs], [o for o, a in pairs],
                   [a for o, a in pairs], 80.0 * len(pairs), (sem, 16 * len(pairs)), lat)

    def dma(q, o, a, sem, lat):
        return dmas(q, [(o, a)], sem, lat)

    nloc = [0]

    def send(dst, src, o, a, sem, c=300.0):
        rid, pid = topo.addr(dst, core)
        eng = topo.engines(core, dst)[:8]
        nloc[0] += len(eng)
        i = rec("g", lambda: g.remote_dma(o[0], a[0], T.sem[sem], T.sem.loc, pid, rid, bits(eng)), [], [a], c, ("loc", 0))
        edges.append((i, rec("x", None, [o], [], 0.0, (sem, len(topo.engines(src, core)[:8])), REM)))
        return i

    prv, nxt = T.cores[(rank - 1) % N], T.cores[(rank + 1) % N]

    def dr(t):
        return (t, [], [], 0)

    add, sub, mul, mx, mn = ALU.add, ALU.subtract, ALU.mult, ALU.max, ALU.min
    MAG, EOF = 1.5 * 2.0 ** 31, 1800.0
    la = [dma("a", s("PEPO", 8, 16), dr(T.po[:]), "dpo", 1700.0), dma("a", s("PEPO", 0, 8), dr(T.pe[:]), "dpe", 1700.0)]
    ls = [dma("s", s("LK", a, b), dr(T.lk[:, a:b]), "dl%d" % c, 1650.0 + 0.8 * b) for c, (a, b) in enumerate(((0, 512), (512, 1024), (1024, 2048)))]
    ls.append(dma("s", s("XR", rows=1), dr(T.xb[:, 0]), "dxb", 3300.0))
    ls.append(dma("s", s("EM", 0, 2048), dr(T.em[:]), "dem", 4100.0))
    for i, t in enumerate((T.nub, T.nua, T.vd)):
        if i == 2:
            ls.append(dma("s", s("OB", 0, 256), dr(T.ob[:]), "dob", 4400.0))
        ls.append(dma("s", s("RN", i * 128, (i + 1) * 128, rows=48), dr(t[:]), "dn%d" % i, 4500.0))

    def pc(i):
        return s("PC", i, i + 1)

    def rm(i):
        return s("RM", i, i + 1)

    def st(k):
        return s("ST", k * 128, (k + 1) * 128)

    def pair(j):
        return s("DN", 384 + j * 128, 512 + j * 128)

    ZB, ID, ID32, IDN, IDM, BO = s("ZB", 0, 128), s("ID", 16, 144), s("ID32"), s("IDN"), s("IDM"), s("BO")
    ms(s("ZB", 0, 160), 0.0)
    k16 = act(s("K16"), s("ZB", 0, 144), AF.Exp, bias=math.log(16.0), more=1300.0)
    for x in (s("ZS"), s("Z1"), s("AB", 160, 208), s("AB", 336, 352)):
        ms(x, 0.0)
    iota(s("PI", 0, 1), [[0, 1]], 0, 1, False)
    iota(s("COLG"), [[1, 8], [0, 16]], 0, 0)
    iota(s("COLK"), [[1, 16]], 0, 0)
    iota(s("C2"), [[2, 8]], 0, 0)
    cp(s("LU", 24, 32), s("PEPO", 8, 16))
    send(nxt, prv, s("LU", 16, 24), s("LU", 24, 32), "pox", 1300.0)
    cp(s("LU", 8, 16), s("PEPO", 0, 8))
    cp(s("L16", 0, 16), s("PEPO"))
    diag(IDM, ZB, -512.0)
    sel(s("ID"), s("ZB", 0, 160), [[-1, 160]], ALU.not_equal, 1.0, 16, 1)
    act(ID32, ID)
    for n, c in (("IDN", -1.0), ("ID2K", 2048.0), ("IDB", 65536.0)):
        act(s(n), ID, scale=c)
    diag(s("DR", 0, 128), IDN, 1.0, -2)
    for k in range(2):
        gcopy(s("DR", k, 128, 16), s("ID", 30 + k, 158, 16))
    for k in range(4):
        act(s("DR", 128 + 128 * (k // 2) + k % 2, 256 + 128 * (k // 2), 2), s("DR", k // 2, 128, 2))
    act(s("IDE"), s("DR", 128, 384), scale=1143 / (4096 * math.log(2.0)))
    for a, c in ((0, 1143.0), (256, -1396.0)):
        act(s("IC", a, a + 256), s("DR", 128, 384), scale=c)
    p0 = s("PI", 0, 1)
    ts(s("PI", 8, 9), p0, 15, ALU.bitwise_and, 1, ALU.arith_shift_right)
    ts(s("PI", 9, 10), p0, 1, ALU.bitwise_and)
    cp(s("PC", 27, 29), s("PI", 8, 10))
    ts(s("PI", 1, 2), p0, 15, ALU.bitwise_and)
    ts(s("PI", 2, 3), p0, 4, ALU.arith_shift_right)
    ts(s("PI", 3, 4), p0, 7, ALU.bitwise_and)
    ts(s("PI", 4, 5), p0, 3, ALU.arith_shift_right, 1, ALU.bitwise_and)
    tt(s("PI", 5, 6), p0, s("PI", 2, 3), add)
    ts(s("PI", 6, 7), s("PI", 5, 6), 1, ALU.bitwise_and)
    ts(s("PI", 7, 8), p0, 4, ALU.arith_shift_right, 1, ALU.bitwise_and)
    cp(s("PC", 1, 3), s("PI", 1, 3))
    cp(s("PC", 3, 8), s("PI", 3, 8))
    ts(BO, s("COLG"), pc(2), ALU.is_equal)
    ts(s("RM", 0, 16), s("COLK"), pc(1), ALU.is_equal)
    for k in range(16):
        if k < OPT["stv"]:
            ts(st(k), BO, rm(k), mul)
        else:
            act(st(k), BO, scale=rm(k))
    ts(pc(0), pc(6), 144.0, mul, pc(4), add)
    ts(pc(8), pc(3), 16.0, mul, pc(0), add)
    ts(s("PERM"), s("C2"), pc(8), add)
    act(pc(9), rm(15), bias=-MAG, scale=2.0 ** 20)
    act(pc(10), pc(1), bias=0.5)
    act(pc(11), rm(0), bias=1.0, scale=-1.0)
    act(pc(12), rm(0), scale=128.0)
    act(pc(13), pc(1), bias=128.0)
    act(pc(20), rm(15), bias=1.0, scale=-1.0)
    act(pc(21), rm(15), bias=-1.0)
    act(pc(14), rm(15), bias=-16.0, scale=16.0)
    act(pc(15), rm(15), bias=-0.5, scale=2048.0)
    act(pc(16), rm(15), scale=65536.0)
    act(pc(18), rm(0), scale=512.0)
    ts(pc(19), pc(1), 13.5, ALU.is_gt, -1.0, mul)
    for w in range(3):
        ts(pc(24 + w), pc(1), 1.5, ALU.is_lt, math.log(0.5 ** (2.5 - w)) + EOF / 4096, mul)
    act(pc(22), pc(7), bias=1.0, scale=-1.0)
    act(pc(23), pc(7), bias=-EOF, scale=EOF)
    for a in (0, 144, 288):
        ms(s("CR", a, a + 8), 0.0)
    for c in range(4):
        a, b = c * 512, (c + 1) * 512
        bk = s(("P4", "P5", "P0", "P1")[c])
        ts(s("CW", a, b), s("LK", a, b), -128.0, add, MAG, add)
        act(bk, s("CW", a, b), bias=pc(9))
        tt(s("TB", a, b), s("LK", a, b), bk, add)
    mms([(s("P6", r, 256, 16), st(r), s("L16", 0, 16), True, True) for r in range(16)])
    cp(s("INI"), s("P6", 0, 256))
    cp(s("L16", 16, 18), s("LU", 22, 24))
    ms(s("CX", 32, 48), 1535.502)
    ms(s("TB", 2048, 2064), 0.0)
    for i, c in enumerate((-1.0, 1.0, -1.0)):
        ts(s("RB", i * 128, (i + 1) * 128, rows=48), s("RN", i * 128, (i + 1) * 128, rows=48), c / 256, mul)
    mm(s("P3", 1, 2), s("XR", rows=1), s("ID", 16, 17, rows=1), True, True)
    act(s("XB"), s("P3", 1, 2))
    act(s("EM", 2048, 2064), s("ZB", 0, 16), bias=s("XB"))
    gcopy(s("ZS", 15, 143, 16), s("BO", 0, 128, 16))
    gcopy(s("Z1", 15, 143, 16), s("ST", 0, 128, 16))
    act(s("BO32"), BO)
    act(s("BO4", 0, 128), BO, scale=2.0 ** 17)
    act(pc(17), pc(1), AF.Exp, bias=15 * math.log(2.0), scale=-math.log(2.0))
    act(s("BO4", 128, 256), BO, scale=pc(17))
    iota(s("POSB"), [[0, 8], [-1, 16]], 16, 0)
    act(s("BO4", 256, 384), s("POSB"), AF.Exp, scale=math.log(2.0))
    act(s("TRI"), BO, scale=pc(21))
    sel(s("TRI"), s("TRI"), [[-1, 128]], ALU.is_gt, 0.0, 0, 1)
    diag(s("DIF"), ID, -1.0, -1)
    gcopy(s("DIF", 0, 128, 16), s("ID", 16, 144, 16))
    diag(s("DT"), ID, -1.0, 1)
    gcopy(s("DT", 14, 128, 16), s("ID", 30, 144, 16))
    gcopy(s("DT", 15, 128, 16), s("ZB", 0, 8))
    ts(s("L14"), ID, pc(19), mul)
    BA, BC, B1 = s("BB", 0, 128), s("BB", 128, 256), s("BB", 256, 384)
    act(B1, ID, scale=rm(15))
    for n, c in ((BA, 2.0 ** 21), (BC, -2.0 ** 17)):
        ts(n, B1, c, mul)
    act(s("D0"), ID, scale=pc(18))
    IDP = s("DN", 256, 384)
    act(IDP, ID, scale=512.0)
    act(s("DN", 0, 128), IDP, scale=pc(11))
    act(s("DN", 128, 256), ID, scale=pc(11))
    ts(s("RM", 16, 24), s("COLK", 0, 8), pc(27), ALU.is_equal)
    for j in range(8):
        (ts(pair(j), BO, rm(16 + j), mul) if j < OPT["prv"] else act(pair(j), BO, scale=rm(16 + j)))
    act(s("S2K"), st(15), scale=-2048.0)
    ts(s("XBN"), BO, s("XB"), mul, -1.0, mul)
    ts(s("ZH"), s("ZS"), 4096.0, mul)
    ts(s("D16"), ID, pc(20), mul, 1.0 / 16, mul)
    ms(s("AQ", 128, 144), 0.0)
    iota(s("DUM"), [[2, 128]], H + 16, 0)
    iota(s("CV"), [[512, 96]], 512 * S0 + 128, 0)
    act(s("ASK", 128, 144), s("RM", 0, 16), scale=16.0)
    act(s("BO8"), BO, scale=8.0)
    iota(s("J8"), [[0, 12], [1, 8]], 0, 0)
    ts(s("BM", 0, 96), s("J8"), pc(1), ALU.is_equal)
    ts(s("BM", 96, 112), s("J8", 0, 16), pc(1), ALU.not_equal)
    tt(s("CV"), s("CV"), s("BM", 0, 96), mul)
    ms(s("CUM", 0, 1), 0.0)
    for b in ("P4", "P5"):
        mm(s(b, 0, 512, 8), ID, s("ZB", 0, 64), True, True)
    for w in (1, 2):
        send(T.cores[(rank - w) % N], T.cores[(rank + w) % N], s("OB", w * 256, (w + 1) * 256), s("OB", 0, 256), "ob%d" % w)

    TBW = s("TB", 0, 2048)

    def tiles(lst, a, par, raw=False):
        a, n = 176 * par + a, 16 * lst[3]
        if raw:
            ts(s("NS", a, a + n), ind(s("LK"), lst), 1.0 / 256, mul, pc(15), add)
        else:
            ts(s("NS", a, a + n), ind(TBW, lst), 1.0 / 512, mul)
        act(s("AB", a, a + n), ind(TBW, lst))

    def emis(dst, a, b, par, q, bias=0.0):
        o, x = s(dst, 16 * a, 16 * b), ind(s("EM"), s("NS", 176 * par + 32 + a, 176 * par + 32 + b))
        return act(o, x, bias=bias) if q == "a" else ts(o, x, bias, add)

    def weights(o, par, P):
        a, NF = 176 * par + 32, s("NF", 128 * par, 128 * par + 128)
        cp(NF, s("NS", a, a + 128))
        mm(P, IDM, NF, True, True)
        tt(o, s("AB", a, a + 128), P, add)
        return NF

    CNT = s("P6", 0, 128)

    def repeats(o, n, a, k0):
        for c in range(8):
            ts((T.EQ[:, c, 0:128 - 16 * c], [("EQ", c, c + 1)], [], 128 - 16 * c), s(n, a + 16 * c, a + 128), s("KB", k0 + c, k0 + c + 1), ALU.is_equal)
        mm(s("P7", 0, 128), IDN, s("BO4", 256, 384), True, False)
        mms([(s("P7", 16 * c + 16, 128), s("BO4", 0, 128), (T.EQ[:, c, 16:128 - 16 * c], [("EQ", c, c + 1)], [], 112 - 16 * c), False, False)
             for c in range(7)] + [(s("P7", 0, 128), s("BO4", 128, 256), (T.EQ[:, :, 0:16], [("EQ", 0, 8)], [], 128), False, True)])
        act(o, s("P7", 0, 128), AF.Relu, bias=4096.0, scale=4096.0)

    def total(o, hs, more):
        group(s("P7", 0, 128), [(ID32, x) for x in more + [s("PR", 256 * h + x, 256 * h + x + 128) for h in hs for x in (0, 128)]])
        act(o, s("P7", 0, 128))

    sent = {}
    cp(s("KB", 1, 9), s("PEPO", 8, 16))
    mm(s("P3", 0, 1), st(15), s("L16", 17, 18), True, True)
    act(s("KB", 0, 1), s("P3", 0, 1))
    repeats(s("CR", 8, 136), "INI", 128, 1)

    for h in range(NH):
        w, par, last = h >> 1, h & 1, h == NH - 1
        m0 = S0 + 16 * h
        now[0] = h
        F = "FB" if par else "FA"
        y0 = 144 * h
        Y, KH = s("YS", y0, y0 + 128), s("KH", 128 * h, 128 * h + 128)
        mine = [gcopy(Y, s("OB", w * 256 + par, (w + 1) * 256, 2)), gcopy(s("YS", y0 + 128, y0 + 144), s("EM", m0, m0 + 16)),
                sel(s("SEL", h * 128, (h + 1) * 128), ZB, [[-NH, 8], [0, 16]], ALU.not_equal, 1.0, -h, 1),
                iota(KH, [[0, 128]], m0 // 16, 0)]
        if h > 1:
            edges.extend((sent[h - 2], i) for i in mine)
        r1, r2, k1, k0 = (h - 1) * SL, (h - 2) * SL, (h - 1) * SL, h * SL
        if h > 1:
            sa, sl, su, s0 = s("RX", r2, r2 + 128), s("RX", r2 + 128, r2 + 136), s("RU", r2 + 128, r2 + 136), s("RX", r2, r2 + 1)
        else:
            sa, sl, su = s("INI", 128 * h, 128 * h + 128), s("L16", 8 * h, 8 * h + 8), s("LU", 16 * h + 8, 16 * h + 16)
            s0 = s("INI", 0, 1)
        if par == 0:
            if h:
                tiles(s("SU", k1 + 134, k1 + 136), 1, par)
                tiles(s("RU", r1 + 128, r1 + 136), 33, par)
            else:
                tiles(s("LU", 24, 32), 33, par, True)
                tiles(s("LU", 22, 24), 1, par, True)
            qa, lr = ([(0, 128, s("RX", r1, r1 + 128))], s("RX", r1, r1 + 127)) if h else ([(0, 128, s("INI", 128, 256))], s("INI", 128, 255))
            for x in range(8):
                o, a, m = s("YB", 256 * x, 256 * x + 256), s("OB", 256 * w, 256 * w + 256), s("BO32", 16 * x, 16 * x + 1)
                if OPT["yb"][w][x] == "a":
                    act(o, a, scale=m)
                else:
                    ts(o, a, m, mul)
        else:
            qa = [(0, 127, s("PK", k1 + 1, k1 + 128)), (127, 128, s("R0", 8 * h - 8, 8 * h - 7))]
            tiles(s("SU", k1 + 128, k1 + 136), 32, par)
        a0 = 176 * par
        A = s("AB", a0 + 32, a0 + 160)
        tr(s("TT", 0, 128), A)
        tr(s("TT", 128, 288), s("AB", a0 + 16, a0 + 176))
        ts(s("NL"), ind(s("TT"), s("PERM")), 1.0 / 512, mul)
        if 0 < h < NH - 1:
            cp(s("RX", r1, r1 + 136), s("RU", r1, r1 + 136))
        chf, chc, chi = (OPT[x][KINDS[h]] for x in ("chf", "chc", "chi"))
        for a, b, q in chf:
            emis(F, a, b, par, q)
        for a, b, q in chc:
            o, x = s("CW", a * 128, b * 128), ind(TBW, s("NL", a * 8, b * 8))
            if q == "a":
                act(o, x, bias=34431.5)
            else:
                ts(o, x, 34431.5, add)
        SEL = s("SEL", h * 128, (h + 1) * 128, rows=48)
        mm(s("P2", 256, 512), SEL, s("RB", 0, 256, rows=48), True, True)
        act(s("DG"), ind(TBW, su))

        def withq(bank, a, l, start, stop):
            for n, (x, y, q) in enumerate(qa):
                mm(s(bank, a + x, a + y), l, q, start and n == 0, stop and n == len(qa) - 1)

        def fit(a):
            act(s("GT", a, a + 128), s("P6", 256 + a, 384 + a), AF.Abs, bias=-256.0)
            ts(s("CL", a, a + 128), s("GT", a, a + 128), 256.0, mn, -256.0, add)
            tt(s("CB", a, a + 128), s("CL", a, a + 128), s("P2", 256 + a, 384 + a), mul)

        nq = qa[0][1]
        mm(s("P6", 256, 384), ID32, s("DG"), True, False)
        mm(s("P6", 256, 256 + nq), IDM, qa[0][2], False, True)
        fit(0)
        mm(s("P2", 0, 128), s("BO32"), s("CB", 0, 128), True, True)
        ts(s("U2", 0, 128), s("P2", 0, 128), 255.0, mn, 1535.502, add)
        NF = weights(s("WT"), par, s("P0", 256, 384))
        group(s("P6", 384, 512), [(IDM, sa), (IDP, NF), (ID, s("WT"))])
        fit(128)
        qz = s("PK", k1 + 1, k1 + 129) if par else qa[0][2]
        mms([(s("P0", r * 128, r * 128 + 128), IDM, qz, r == 0, False) for r in range(2)])
        mms([(s("P0", r * 128, (r + 1) * 128), IDN, s("U2", 0, 128), False, r == 1) for r in range(2)])
        if par:
            group(s("P3", 0, 1), [(ID32, s("DG", 127, 128)), (IDM, qa[1][2])])
            act(s("GT", 256, 257), s("P3", 0, 1), AF.Abs, bias=-256.0)
            ts(s("CL", 256, 257), s("GT", 256, 257), 256.0, mn, -256.0, add)
            tt(s("CB", 256, 257), s("CL", 256, 257), s("P2", 383, 384), mul)
            mm(s("P3", 1, 2), s("BO32"), s("CB", 256, 257), True, True)
            ts(s("U2", 128, 144), s("CX", 32, 48), s("P3", 1, 2), add, 1790.502, mn)
            group(s("P3", 16, 32), [(IDM, s("R0", 8 * h - 8, 8 * h + 8)), (IDN, s("U2", 128, 144))])
            act(s("CX", 0, 32), ind(s("TB", 0, 2064), s("NS", a0 + 158, a0 + 160)), bias=34431.5)
            tt(s("JK", 128, 144), s("CX", 16, 32), s("P3", 16, 32), add)
            ts(s("IW", 2048, 2064), s("JK", 128, 144), 33024.0, ALU.is_equal)
        group(s("P6", 256, 384), [(ID, s("WT")), (s("BO32"), s("CB", 128, 256))])
        act(s("SG"), s("P6", 256, 384), AF.Sign, bias=-1.0 / 512)
        mm(s("P6", 384, 512), s("DN", 0, 128), NF, True, False)
        mm(s("P6", 384, 512), s("DN", 128, 256), s("WT"), False, False)
        withq("P6", 384, s("D0"), False, True)
        act(s("JK", 0, 128), s("WT"), AF.Relu, bias=-239.0)
        act(s("ND"), s("JK", 0, 128), bias=pc(14), scale=pc(20))
        if par == 0:
            kb = 16 * h
            ts(s("EQ0", 1, 128), lr, s("KB", kb, kb + 1), ALU.is_equal)
            R = s("CR", 144 * w + 7, 144 * w + 135)
            mm(CNT, ID, R, True, False)
            mm(s("P6", 1, 128), ID, lr, False, False)
            if h:
                mm(s("P6", 0, 1), ID, s("PK", k1 + 127, k1 + 128), False, False)
            else:
                mm(s("P6", 0, 1), st(15), s("L16", 17, 18), False, False)
            mm(s("P6", 1, 128), s("BO4", 0, 128), s("EQ0", 1, 128), False, True)
        else:
            R = s("EA")
            repeats(R, "PK", k1, 16 * h + 1)
            group(CNT, [(ID, s("PK", k1, k1 + 128)), (ID, R)])
        mm(s("P6", 256, 384), s("XBN"), Y, True, False)
        mm(s("P6", 256, 384), ID, R, False, False)
        if par == 0:
            mm(s("P6", 257, 384), s("BO4", 0, 128), s("EQ0", 1, 128), False, False)
        mm(s("P6", 256, 384), s("S2K"), s("SG"), False, True)
        act(s("NZ"), s("P6", 256, 384), AF.Relu, bias=2049.0)
        tt(s("OF"), s("DUM"), CNT, mn)
        mms([(s("P6", 128, 136), s("Z1", 15 - r, 143 - r), s("OF", r, 128, 16), r == 0, r == 15) for r in range(16)])
        cp(s("OFU", 8 * par, 8 * par + 8), s("P6", 128, 136))
        act(s("AQ", 0, 128), s("P6", 384, 512), bias=pc(12))
        mm(s("P3", 384, 512), SEL, s("RB", 256, 384, rows=48), True, False)
        mm(s("P3", 384, 512), s("D16"), s("K16", 0, 128), False, False)
        for a, b, q in chf:
            mms([(s("P1", 8 * (t % 32), 8 * (t % 32) + 8, rows=16, r0=32 * (t // 32)), s(F, 16 * t, 16 * t + 16),
                  s("YB", 2 * t + par, 2048, 256), True, True) for t in range(a, b)])
        act(s("XS"), s("P1", 0, 256), bias=pc(23), scale=pc(22))
        mms([(s("P3", 32 * c, 32 * c + 32, rows=32, r0=32 * (x // 2)), s("ID", 16 + 32 * c - 16 * (x % 2), 48 + 32 * c - 16 * (x % 2)),
              s("XS", x, 256, 8), False, False) for c in range(4) for x in range(8)])
        mm(s("P3", 0, 128), s("ID2K"), s("SG"), False, True)
        act(s("E1"), s("P3", 0, 128), AF.Relu, bias=EOF - 2048.0)
        tt(s("EV"), s("E1"), s("P3", 384, 512), mul)
        mm(s("P1", 128, 256), s("L14"), sa, True, False)
        mm(s("P1", 128, 256), s("DT"), NF, False, False)
        mm(s("P1", 128, 256), s("ZS", 0, 128), KH, False, False)
        mm(s("P2", 0, 128), s("ZH", 0, 128), s("K16", 0, 128), True, False)
        if sum(y - x for x, y, q in chc) < 15:
            act(s("QS"), s("P0", 0, 256), bias=34431.5)
        for a in range(0, 15, 2):
            b = min(a + 2, 15)
            if any(x <= a < y for x, y, q in chc):
                tt(lanes("XW", a, b), s("CW", a * 128, b * 128), s("P0", 0, (b - a) * 128), add)
            else:
                tt(lanes("XW", a, b), ind(TBW, s("NL", a * 8, b * 8)), s("QS", 0, (b - a) * 128), add)
        for a, b in chi:
            ts(lanes("IW", a, b), lanes("XW", a, b), 33024.0, ALU.is_equal)
            if par and b == OPT["late"]:
                mms([(s("P2", 127, 128), s("ZH", 15 - k, 143 - k), s("IW", 2048 + k, 2049 + k), False, False) for k in range(15)])
            mms([(s("P2", 0, nq), s("ZH", 15 - k, 143 - k), s("IW", k * 128, k * 128 + nq), False, k == 14) for k in range(a, b)])
        mm(s("P0", 0, 128), s("IDB"), s("NZ"), True, False)
        tt(s("SW"), s("EV"), s("P2", 0, 128), mn)
        mm(s("P0", 0, 128), s("BO32"), s("SW"), False, True)
        ts(s("ASK", 0, 128), s("P0", 0, 128), 0.0, ALU.is_le)
        tt(s("SE"), s("E1"), s("P2", 0, 128), mn)
        mm(s("P1", 0, 128), s("BO32"), s("SW"), False, False)
        mm(s("P1", 0, 128), s("TRI"), s("SE"), False, False)
        scan(s("CUM", 1, 145), s("ASK"), s("K16"), add, mn)
        mm(s("P1", 0, 128), BA, s("ASK", 0, 128), False, False)
        mms([(s("P1", 0, 128), BC, s("CUM", 0, 128), False, False), (s("P1", 128, 256), B1, s("CUM", 0, 128), False, True)])
        ts(s("HIT"), s("P1", 0, 128), pc(16), ALU.is_gt)
        tt(s("XX"), s("HIT"), s("P1", 128, 256), mul)
        mm(s("P0", 128, 256), s("DIF"), s("HIT"), True, True)
        tt(s("NN", 0, 128), s("ND"), s("P0", 128, 256), mul)
        tt(s("SV"), s("SG"), s("P2", 0, 128), mn)
        act(s("ES"), s("P3", 0, 128))
        for x in (0, 128):
            group(s("P3", 256 + x, 384 + x), [(s("IDE", x, x + 128), s("ES")), (s("IC", 256 + x, 384 + x), s("SG")), (s("IC", x, x + 128), s("SV"))])
        GL = s("GL", 256 * par, 256 * par + 256)
        act(s("P3", 0, 256), s("P3", 256, 512), AF.Exp, bias=pc(24 + w), scale=math.log(2.0) / 1143)
        act(s("GH"), s("P3", 0, 256), scale=pc(28))
        tt(GL, s("P3", 0, 256), s("GH"), sub)
        PL, PX = s("P7", 376, 384), s("P7", 248, 376)
        for x in range(2) if h == NH - 2 else ():
            total(s("PR", 1536 + 128 * x, 1664 + 128 * x), (x, x + 2), [])
        if last:
            total(s("YA", 0, 256, 2), (h - 1,), [s("PR", 1536, 1664)])
        mm(PL, ID, sl, True, False)
        if not last:
            mm(PX, ID, sa, False, False)
        if par == 0:
            group(s("P6", 256, 257), [(ID, s0), (BO, s("XX", 0, 1))])
            ts(s("E0", 8 * h, 8 * h + 16), s("ZB", 0, 16), s("P6", 256, 257), add)
            sent[h] = send(prv, nxt, s("R0", 8 * h, 8 * h + 16), s("E0", 8 * h, 8 * h + 16), "re%d" % h)
        mms([(PL, s("ZS", 15 - r, 143 - r), s("XX", r, 128, 16), False, last and r == 15) for r in range(16)]
            + ([] if last else [(PX, BO, s("XX"), False, True)]))
        act(s("JC"), s("CUM", 1, 145), AF.Sign, bias=pc(10), scale=-1.0, acc=s("IAC", 0, 1))
        if last:
            cp(s("SU", k0 + 128, k0 + 136), PL)
        else:
            cp(s("SU", k0, k0 + 136), s("P7", 248, 384))
            if h != NH - 2:
                sent[h] = send(prv, nxt, s("RU", k0, k0 + 136), s("SU", k0, k0 + 136), "rx%d" % h)
            cp(s("PK", k0, k0 + 130), s("SU", k0, k0 + 130))
            act(s("KB", 16 * h + 16, 16 * h + 25), s("P7", 375, 384))
        IDX = s("IDX", 0, 1)
        ts(IDX, s("IAC", 0, 1), 0.5, mul, 72.0, add)
        tt(s("G1", 0, 16), ind(s("AB", a0 + 32, a0 + 176), IDX), s("BM", 96, 112), mul)
        act(s("EM", m0, m0 + 16), ind(s("YS", y0, y0 + 144), IDX))
        tt(ind(s("AB", a0 + 32, a0 + 176), IDX), s("G1", 0, 16), s("CV", 16 * h, 16 * h + 16), add)
        tt(ind(s("TB"), s("OFU", 8 * par, 8 * par + 8)), A, s("NN", 0, 128), sub)
        act(s("IAC", 1, 2), s("IAC", 0, 1), AF.Sign, bias=-111.0)
        ts(s("IDX", 2, 3), s("IAC", 1, 2), 128.0, mul, pc(13), add)
        act(s("G1", 16, 32), ind(s("AQ"), IDX))
        cp(ind(s("TB", m0, m0 + 272), s("IDX", 2, 3)), s("G1", 16, 32))
        if par and not last:
            repeats(s("CS", 128 * w, 128 * w + 128), "PK", k0, 16 * h + 17)
            sent[h] = send(prv, nxt, s("CR", 144 * w + 152, 144 * w + 280), s("CS", 128 * w, 128 * w + 128), "cx%d" % w)
        for c in range(4):
            bk, e, t0 = "P%d" % (4 + c % 2), c // 2, 64 * (c % 2)
            g0 = 256 * par + 128 * e + t0
            mms([(s(bk, j, 512, 8), pair(j), s("GL", g0, g0 + 64), True, True) for j in range(1, 8)])
            for x, y in OPT["sc"]:
                scan(s("SC", 512 * c + x, 512 * c + y), s(bk, x, y), s(F, 16 * t0 + 2 * x + e, 16 * t0 + 2 * y, 2), mul, add)
        mm(s("P4", 1, 512, 2), pair(0), GL, True, True)
        tt(s("PR", 256 * h, 256 * h + 256), s("SC", 7, 2048, 8), s("P4", 1, 512, 2), mul)
        if last:
            total(s("YA", 1, 256, 2), (h,), [s("PR", 1664, 1792)])
    now[0] = NH
    for par in range(2):
        F = "PW" if par else "FA"
        tiles(s("SU", (4 + par) * SL + 128, (4 + par) * SL + 136), 32, par)
        for a, b, q in OPT["zq"][par]:
            emis(F, a, b, par, q, -8.0)
        WB = s("WB", 128 * par, 128 * par + 128)
        weights(WB, par, s("P%d" % (2 + par), 128, 256))
        mm(s("P%d" % (2 + par), 0, 128), s("BO8"), WB, True, False)
        for c, (t0, e, d) in enumerate(OPT["zp"][par]):
            bk, z0, n, m = ("P0", "P1", "P6")[(4 * par + c) % 3], 2048 * par + 512 * c, 32 * d, 16 // d
            mms([(s(bk, j, 512, m), st(d * j + e), s("WB", 128 * par + t0, 128 * par + t0 + n), True, True) for j in range(m)])
            tt(s("PZ", z0, z0 + 512), s(F, 16 * t0 + e, 16 * (t0 + n), d), s(bk), mul)
            mms([(s("P%d" % (2 + par), t0, t0 + n), ID, s("PZ", z0 + j, z0 + 512, m), False, c == 3 and j == m - 1) for j in range(m)])
        act(s("YZ", par, 256, 2), s("P%d" % (2 + par), 0, 128))
    dma("s", dr(T.ya[:]), s("YA"), "dya", 2000.0)
    dma("s", dr(T.yz[:]), s("YZ"), "dyz", 2000.0)

    la.append(k16)
    edges.extend(zip(la, la[1:]))
    edges.extend((k16, i) for i in range(k16 + 1, k16 + 99) if ops[i][0] == "a")
    edges.extend(zip(ls, ls[1:]))
    line = []
    for q in "va":
        keys = [(h - x.count("-"), q, x.strip("-")) for h in range(NH + 1) for x in LINE[q][(KINDS + ("end",))[h]].split()]
        seq = [named[k].pop(0) for k in keys if named.get(k)]
        line.extend(zip(seq, seq[1:]))
    ops = schedule(ops, edges, line)
    deps = depends(ops, True)
    clock = {q: {} for q in "vapgsx"}
    at, waits, need = [], [], set()
    for i, o in enumerate(ops):
        ck = clock[o[0]]
        ws = []
        for j in sorted(deps[i], reverse=True):
            key = ops[j][0] if ops[j][4] is None else ops[j][4][0]
            if ck.get(key, -1) >= j or soft(ops[j], o):
                continue
            ws.append(j)
            need.add(j)
            ck[key] = j
            for k2, v2 in at[j].items():
                if ck.get(k2, -1) < v2:
                    ck[k2] = v2
        waits.append(ws)
        at.append(dict(ck) if o[0] != "x" else {})
    eng = {"v": g.vector, "a": g.scalar, "p": g.tensor, "g": g, "s": g.sync}
    cnt = {q: 0 for q in "vapg"}
    val, top = {}, {}
    for i, o in enumerate(ops):
        q, tok = o[0], o[4]
        if tok is not None:
            val[i] = tok
            top[tok[0]] = tok[1]
        if q == "x":
            continue
        for j in waits[i]:
            eng[q].wait_ge(T.sem[val[j][0]], val[j][1])
        ins = o[1]()
        if tok is None and i in need:
            cnt[q] += 1
            ins.then_inc(T.sem["q" + q], 1)
            val[i] = ("q" + q, cnt[q])
    top["loc"] = nloc[0]
    for q in "vapg":
        top["q" + q] = cnt[q]
    for n in top:
        if top[n] and n not in ("dya", "dyz"):
            g.wait_ge(T.sem[n], top[n])
    g.wait_ge(T.sem.dya, 16)
    g.wait_ge(T.sem.dyz, 16)
